import numpy as np, ml_dtypes
CORES = [5,29,101,125,133,157,229,253]
N = 8
BF = ml_dtypes.bfloat16
def gentries(a):
    return np.ascontiguousarray(a.reshape(8, 16, -1).transpose(0, 2, 1)).reshape(8, -1)
def gtable(e):
    e = np.asarray(e); return np.ascontiguousarray(e.reshape(8, -1, 16).transpose(0, 2, 1)).reshape(128, -1).astype(np.int32)
W, L, HS = 1600, 256, 1024
HOP = (1, 0, 3, 0)
HB = W // 12
def above(rng, hub, c, fill=None):
    M = c.shape[2]; s = (N, 8, 16, M); c = c[:, :, None, :]
    k = np.stack([np.stack([np.searchsorted(hub[r, g], c[r, g, 0], side="right") for g in range(8)]) for r in range(N)])[:, :, None, :] + rng.integers(0, 24, s)
    e1 = np.where(k < HB, np.take_along_axis(hub[:, :, None, :], np.minimum(k, HB - 1), 3), 0)
    e2 = np.where(c < W - 1, np.minimum(c + 1 + ((W - 1 - c) * rng.random(s) ** 2).astype(np.int64), W - 1), 0)
    e = np.where(rng.random(s) < 0.6, e1, e2)
    e = np.where(rng.random(s) < 0.03, ((c + 1) * rng.random(s)).astype(np.int64), e)
    if fill is None: fill = rng.choice(np.array([0.0, 0.25, 0.5, 0.75, 1.0]), (N, 8, 1, M))
    return np.where(rng.random(s) < fill, e, 0)
def parts(rng):
    hub = np.sort(np.argsort(rng.random((N, 8, W - 1)), axis=-1)[..., :HB] + 1, axis=-1)
    d = rng.integers(0, 256, (N, 8, 16, W)); v = rng.integers(0, 256, (N, 8, 16, L))
    w = rng.integers(1, 256, (N, 8, 16)); a = rng.integers(30, 91, (N, 8, 16))
    p = above(rng, hub, np.broadcast_to(np.arange(W), (N, 8, W)))
    j = np.where(rng.random((N, 8, L)) < 0.5, (W * rng.random((N, 8, L)) ** 1.5).astype(np.int64), np.take_along_axis(hub, rng.integers(0, HB // 2, (N, 8, L)), 2))
    q = above(rng, hub, j)
    pj = np.take_along_axis(p, j[:, :, None, :], 3)
    q = np.where(rng.random(q.shape) < 0.25, np.roll(pj, 1, axis=2), q)
    return d, p, j, q, v, w, a, hub
def pack(d, p, j, q, v, w, a):
    return {"d0": d.reshape(N, 128, W).astype(np.float32).astype(BF), "p0": np.ascontiguousarray(p.reshape(N, 128, W)).astype(np.int32), "j0": np.stack([gtable(x) for x in j]),
            "q0": np.ascontiguousarray(q.reshape(N, 128, L)).astype(np.int32), "v0": v.reshape(N, 128, L).astype(np.float32).astype(BF), "wa": np.ascontiguousarray(np.stack([w, a], axis=-1).reshape(N, 128, 2)).astype(np.int32)}
def setup_inputs(rng):
    d, p, j, q, v, w, a, hub = parts(rng)
    return pack(d, p, j, q, v, w, a)
def setup_inputs_edge(rng):
    d, p, j, q, v, w, a, hub = parts(rng)
    v = rng.integers(96, 160, (N, 8, 16, 1)); a = rng.integers(1, 91, (N, 8, 16))
    near = (np.argsort(rng.random((N, 8, 16, W)), axis=2) < rng.integers(7, 11, (N, 8, 1, W))).astype(np.int64)
    d = v + (2 * rng.integers(0, 2, (N, 8, 16, W)) - 1) * (a[..., None] - near)
    return pack(d, p, j, q, np.repeat(v, L, axis=3), w, a)
def setup_inputs_herd(rng):
    d, p, j, q, v, w, a, hub = parts(rng); o = rng.permutation(8); s = rng.permutation(N)
    for r in range(N):
        x = np.stack([rng.permutation(W)[:L] for g in range(8)])
        if r == s[0]:
            for g in range(8): j[r, g] = x[g, rng.permutation(np.arange(L) % (4 * g + 1))]
        elif r == s[1]:
            j[r] = x
        else:
            j[r, o[0]] = x[0, 0]; j[r, o[1]] = x[1]; j[r, o[2]] = np.tile(x[2, :L // 2], 2); j[r, o[3]] = x[3, rng.integers(0, 4, L)]
            for i in range(4, 8):
                n = 1 + (r + i) % 4; y = x[i].copy(); y[L - n:] = y[:n]; j[r, o[i]] = y
    return pack(d, p, j, q, v, w, a)
def setup_inputs_alike(rng):
    d, p, j, q, v, w, a, hub = parts(rng); o = rng.permutation(8)
    q[:, o[0]] = np.roll(np.take_along_axis(p, j[:, :, None, :], 3), 5, axis=2)[:, o[0]]
    p[:, o[1]] = p[:, o[1]][:, np.arange(16) // 4 * 4]; q[:, o[1]] = q[:, o[1]][:, np.arange(16) // 8 * 8]
    p[:, o[2]] = 0; q[:, o[3]] = 0; p[:, o[4]] = 0; q[:, o[4]] = 0
    q[:, o[5]] = above(rng, hub, j, 1.0)[:, o[5]]
    p[:, o[6]] = above(rng, hub, np.broadcast_to(np.arange(W), (N, 8, W)), 1.0)[:, o[6]]
    a[:, o[7]] = 0
    for r in range(N):
        x = rng.permutation(L); c = L + rng.permutation(W - L)[np.arange(32 * L) % (W - L)].reshape(L, 32).T
        j[r, o[7]] = x; p[r, o[7]][:, x] = c[:16]; q[r, o[7]] = c[16:]
    e = int(rng.integers(0, N)); p[e] = 0; q[e] = 0; j[e] = np.stack([rng.permutation(W)[:L] for g in range(8)])
    return pack(d, p, j, q, v, w, a)
def setup_inputs_ends(rng):
    d, p, j, q, v, w, a, hub = parts(rng); o = rng.permutation(8); c = np.arange(W); e = np.array([0, 1, W - 2, W - 1])
    p[:, o[0]] = np.where(rng.random((N, 16, W)) < 0.5, np.minimum(c + 1, W - 1), c); j[:, o[0], :4] = e; a[:, o[0]] = 5
    p[:, o[1]] = np.where(rng.random((N, 16, W)) < 0.3, W - 1, 0); a[:, o[1]] = 20
    j[:, o[2]] = rng.choice(e, (N, L)); q[:, o[2]] = rng.choice(e, (N, 16, L)); a[:, o[2]] = 30
    w[:, o[3]] = 0; p[:, o[3], :, ::2] = 0; q[:, o[3], :, ::2] = 0
    w[:, o[4]] = 255; v[:, o[4], :, ::2] = 255; p[:, o[4], :, ::3] = 0; q[:, o[4], :, ::2] = 0
    a[:, o[5]] = 0; a[:, o[6]] = 255
    d[:, o[7]] = 0; v[:, o[7]] = 255
    for r in range(N):
        n = r % 4; y = rng.permutation(W)[:L]; y[L - n:] = y[:n].copy()
        j[r, o[7]] = y; a[r, o[7]] = 253 if n == 3 else 255
    return pack(d, p, j, q, v, w, a)
def setup_inputs_spread(rng):
    d, p, j, q, v, w, a, hub = parts(rng)
    d = (np.exp2(8 * rng.random((N, 8, 1, W))) * rng.random((N, 8, 16, W))).astype(np.int64)
    v = (np.exp2(8 * rng.random((N, 8, 1, L))) * rng.random((N, 8, 16, L))).astype(np.int64)
    s = np.argsort(rng.random((N, 8)), axis=1)[..., None] + 1
    a = (np.exp2(s) * rng.random((N, 8, 16))).astype(np.int64)
    w = rng.integers(0, 256, (N, 8, 16)); p = rng.integers(0, W, p.shape); q = rng.integers(0, W, q.shape); j = rng.integers(0, W, j.shape)
    return pack(d, p, j, q, v, w, a)
def check_inputs(d):
    bad = []
    for k, hi in (("d0", 255), ("p0", W - 1), ("j0", W - 1), ("q0", W - 1), ("v0", 255), ("wa", 255)):
        x = np.asarray(d[k]).astype(np.float64)
        if not (np.all(x >= 0) and np.all(x <= hi) and np.all(x == np.floor(x))): bad.append("range of " + k)
    return bad
def stays(d, e, j, v, th):
    x = np.take_along_axis(d, e.reshape(N, 8, 1, 16 * L), 3).reshape(N, 8, 16, 16, L)
    votes = np.add.reduce((np.abs(x - v[:, :, :, None, :]) < th[:, :, :, None, None]).astype(np.int32), axis=2)
    return (e > j[:, :, None, :]) & (votes < 9)
def reference(d0, p0, j0, q0, v0, wa):
    d = d0.astype(np.float32).astype(np.int32).reshape(N, 8, 16, W); p = p0.astype(np.int64).reshape(N, 8, 16, W)
    j = np.stack([gentries(x) for x in j0]).astype(np.int64); q = q0.astype(np.int64).reshape(N, 8, 16, L)
    v = v0.astype(np.float32).astype(np.int32).reshape(N, 8, 16, L)
    w = wa[:, :, 0].astype(np.int32).reshape(N, 8, 16, 1); a = wa[:, :, 1].astype(np.int32).reshape(N, 8, 16)
    waited = np.zeros((N, 8), np.int32)
    for hop in HOP:
        key = (np.arange(8 * N).reshape(N, 8, 1) * W + j).reshape(-1)
        act = np.zeros(8 * N * L, bool); act[np.unique(key, return_index=True)[1]] = True; act = act.reshape(N, 8, L)
        th = a + (waited & 3)[:, :, None]
        pj = np.take_along_axis(p, j[:, :, None, :], 3)
        sp = stays(d, pj, j, v, th); sq = stays(d, q, j, v, th)
        dup = np.any(q[:, :, :, None, :] == pj[:, :, None, :, :], axis=3)
        u = np.where(sp, pj, np.where(sq & ~dup, q, 0))
        f = np.minimum.reduce(np.where(u > 0, u, W), axis=2)
        f = np.where(f < W, f, np.add.reduce(w * v, axis=2) & (HS - 1))
        nd = np.abs(np.take_along_axis(d, j[:, :, None, :], 3) - v)
        nv = np.abs(v - np.take_along_axis(d, f[:, :, None, :], 3))
        d = d.copy(); p = p.copy()
        for r in range(N):
            for g in range(8):
                m = act[r, g]; c = j[r, g][m]
                d[r, g][:, c] = nd[r, g][:, m]; p[r, g][:, c] = u[r, g][:, m]
        waited = np.add.reduce((~act).astype(np.int32), axis=2)
        j = np.where(act, f, j); q = np.where(act[:, :, None, :], u, q); v = np.where(act[:, :, None, :], nv, v)
        j = np.roll(j, hop, axis=0); q = np.roll(q, hop, axis=0); v = np.roll(v, hop, axis=0)
    return {"yd": d.reshape(N, 128, W).astype(np.float32).astype(BF), "yj": j.astype(np.float32), "yq": q.reshape(N, 128, L).astype(np.float32), "yv": v.reshape(N, 128, L).astype(np.float32).astype(BF)}

@@ -1,0 +1,681 @@
+import numpy as np
+from concourse.bass import DstId, RemoteDMATransfer
+from concourse.mybir import AluOpType as ALU, AxisListType, ActivationFunctionType as AF
+
+W, L, H = 1600, 256, 128
+HOP = (1, 0, 3, 0)
+PA = 64
+VS = 64
+SP = (128, 0) * 4
+K = 65536.0
+KK = K * 1024.0
+BETA = 96.0
+WT = 1864
+WD = 1608
+G_ = 1.56
+SC_ = 3.8
+PEF = 0.6
+COMM = 7500.0
+SYNC = 140.0
+SLACK = 40.0
+PH = 3000.0
+TRIES = 3
+ROUNDS = 6
+MORE = 300
+f32, bf, f16, i32, u16 = "float32", "bfloat16", "float16", "int32", "uint16"
+SZ = {f32: 4, bf: 2, f16: 2, i32: 4, u16: 2}
+SB = {
+    "Dm": ([WT], bf), "Ds": ([2, WD], f32), "Pt": ([WT], i32), "IOT": ([W], f32), "IO": ([160], f32),
+    "jin": ([16], i32), "qin": ([L], i32), "win": ([2], i32),
+    "SU": ([10, 144], u16), "SV": ([10, 144], bf), "LU": ([4, 144], u16), "LV": ([4, 144], bf), "JT": ([10, 8], f32),
+    "col": ([32], f32), "coli": ([8], i32), "thc": ([4, 8], f32), "thi": ([4, 4], i32),
+    "ZV": ([144], bf), "Z1": ([144], bf), "BI": ([16, 128], bf), "MT": ([20, 128], bf), "B0f": ([128], f32),
+    "tmp": ([6, 128], f32), "thr": ([128], bf), "OH": ([16], f32), "RL": ([128], u16), "seg": ([8], f32),
+    "dump": ([16], f32), "Pu": ([2, H], u16), "PQ": ([2, 2, H], f16), "Jb": ([2, H], f16),
+    "E": ([2, 8, H], bf), "E2": ([8, H], bf), "act": ([2, H], bf), "sg": ([2, 2 * H], bf), "tau": ([2, H], bf),
+    "rr": ([2, 2, H], bf), "fr": ([2, 2, H], bf), "sig": ([4, 4 * H], bf), "Dj": ([2, 2, H], bf), "nd": ([2, H], bf),
+    "XT": ([2, H], f32), "hi": ([2, 2, 8], i32), "flag": ([2, H], f32), "tM": ([2, 8], f16),
+    "sc1": ([2, 8], f32), "scu": ([2, 8], u16), "jm": ([2, 8], f32), "WQ": ([2, H], f32), "Ww": ([2, H], f32),
+    "Wa": ([2, H], f32), "WTr": ([2, H], f32), "scn": ([2, H], i32), "fi": ([2, 8], i32),
+    "fM": ([2, 16], f16), "fz": ([2, 8], u16), "yqb": ([2, H], f32), "yjb": ([2, H], f32),
+    "v1": ([2, H], f32), "vr": ([2, H * 16], f32), "yy": ([2, 2, H * 16], bf), "ia": ([2, 2, H * 16], bf),
+}
+POOL = ("pD0", "pD1", "pM0", "pM1")
+SCRATCH = {k: ("sbuf", [128] + v[0], v[1]) for k, v in SB.items()}
+SCRATCH.update({k: ("psum", [128, 512], f32) for k in POOL + ("pQ0", "pQ1", "pP0", "pP1")})
+IOS = {"d0": ([128, W], bf), "p0": ([128, W], i32), "j0": ([128, 16], i32), "q0": ([128, L], i32), "v0": ([128, L], bf),
+       "wa": ([128, 2], i32), "yd": ([128, W], bf), "yj": ([8, L], f32), "yq": ([128, L], f32), "yv": ([128, L], bf)}
+ENG = ("V", "S", "T", "G", "Y")
+SEMAPHORES = (["eV", "eS", "eT", "eG"] + ["dm%d" % i for i in range(16)] + ["rel%d" % i for i in range(4)]
+              + ["arr%d" % i for i in range(4)] + ["sent", "fwd"])
+NLOAD = 6
+s_ = np.s_
+
+
+def ap(name, idx=s_[:]):
+    return ("ap", name, idx if isinstance(idx, tuple) else (idx,))
+
+
+def ind(win, off):
+    return ("ind", win, off)
+
+
+def is_ap(a):
+    return isinstance(a, tuple) and len(a) == 3 and a[0] in ("ap", "ind")
+
+
+_span = {}
+
+
+def span(a):
+    key = (a[1], repr(a[2]))
+    if key not in _span:
+        shape, dt = ([128, 512], f32) if a[1][0] == "#" else SCRATCH[a[1]][1:] if a[1] in SCRATCH else IOS[a[1]]
+        x = np.arange(int(np.prod(shape[1:]))).reshape([1] + list(shape[1:]))[(slice(None),) + a[2][1:]]
+        _span[key] = (a[1], int(x.min()) * SZ[dt], (int(x.max()) + 1) * SZ[dt], int(x.size), SZ[dt])
+    return _span[key]
+
+
+def nel(a):
+    return 16 * span(a[2])[3] if a[0] == "ind" else span(a)[3]
+
+
+def is_ps(name):
+    return name[0] == "#" or name in SCRATCH and SCRATCH[name][0] == "psum"
+
+
+def build():
+    ops, ph, cnt = [], [0], [0, 0, 0, 0]
+
+    def op(eng, meth, outs, args, kw=None, cost=64.0, grp=None, first=False, extra=None):
+        kw = kw or {}
+        wr, rd = [], []
+        for o in outs:
+            if o[0] == "ind":
+                wr.append(span(o[1])); rd.append(span(o[2]))
+            else:
+                wr.append(span(o))
+        for k, a in enumerate(list(args) + list(kw.values())):
+            if is_ap(a) and not ((k == 0 or k >= len(args)) and a in outs):
+                rd += [span(a[1]), span(a[2])] if a[0] == "ind" else [span(a)]
+        bank = [x[0] for x in wr + rd if x[0][0] == "#"]
+        ops.append(dict(eng=eng, meth=meth, args=args, kw=kw, wr=wr, rd=rd, cost=cost, grp=grp, first=first, extra=extra,
+                        ph=ph[0], bank=bank[0] if bank else None))
+
+    def vcost(out, ins, base):
+        if out[0] == "ind":
+            return 60 + SC_ * nel(out)
+        if ins[0][0] == "ind":
+            return 60 + G_ * nel(ins[0])
+        if base == 2:
+            r = 1.0 if any(is_ps(a[1]) for a in ins) else 2.0
+        else:
+            r = 0.5 if all(span(a)[4] == 2 for a in ins + [out]) else 1.0
+        return max(64.0, 30 + r * nel(out))
+
+    def cp(out, a): op("V", "tensor_copy", [out], [out, a], cost=vcost(out, [a], 1))
+    def tt(out, a, b, o): op("V", "tensor_tensor", [out], [out, a, b, o], cost=vcost(out, [a, b], 2))
+    def ts(out, a, s1, o1, s2=None, o2=None):
+        op("V", "tensor_scalar", [out], [out, a, s1, s2, o1] + ([o2] if o2 is not None else []), cost=vcost(out, [a], 1))
+    def ms(out, c): op("V", "memset", [out], [out, c], cost=max(64.0, 30 + nel(out) * span(out)[4] / 4))
+    def tr(out, a): op("V", "transpose", [out], [out, a], cost=30 + H)
+    def scan(out, a, b, o0, o1): op("V", "tensor_tensor_scan", [out], [out, a, b, 0.0, o0, o1], cost=30 + H)
+    def act(out, a, f, bias=None, scale=None, acc=None, more=0):
+        kw = {k: x for k, x in (("bias", bias), ("scale", scale), ("accum_out", acc)) if x is not None}
+        op("S", "activation", [out] + ([acc] if acc else []), [out, a, f], kw,
+           cost=80 + more + nel(out) * (G_ if a[0] == "ind" else 1.0))
+    def sc(out, a, c): act(out, a, AF.Identity, scale=c)
+    def new(i):
+        cnt[i] += 1
+        return cnt[i]
+    def newg(): return new(0)
+    def bank_(): return "#%d" % new(1)
+    def mm(out, lt, rhs, grp, first=False, f=1.0):
+        op("T", "matmul", [out], [out, lt, rhs], cost=max(64, nel(rhs)) * f * PEF + 8, grp=grp, first=first)
+    def dma(q, out, a, nbytes):
+        op(q, "dma_start", [out], [out, a], cost=60.0, extra=("dma", new(2) - 1, 2200 + nbytes / 150.0))
+    def iota(out, pat, base, cm, fl=True):
+        op("G", "iota", [out], [out, pat, base, cm], {"allow_small_or_imprecise_dtypes": True} if fl else {}, cost=160 + 2 * nel(out))
+    def col(i): return ap("col", s_[:, i:i + 1])
+    def coli(i): return ap("coli", s_[:, i:i + 1])
+    def MT(i): return ap("MT", s_[:, i, :])
+    def tmp(i): return ap("tmp", s_[:, i, :])
+    def OH(i): return ap("OH", s_[:, i:i + 1])
+    def ZW(z, i): return ap(z, s_[:, 15 - i:143 - i])
+    def thc(s, i): return ap("thc", s_[:, s, i:i + 1])
+    (M_I, M_NI, M_SG, M_TAU, M_R, M_W4, M_WD, M_LP, M_LQ, M_LA, M_LJ, M_LH, M_T00, M_T01, M_T10, M_T11, M_BO, M_C) = range(18)
+    (C_P, C_G, C_R, C_16, C_G15, C_H0, C_H1, C_P16, C_M16, C_PW, C_BIG, C_LP, C_LQ, C_A1, C_A2, C_W, C_A, C_U, C_T0, C_T1,
+     C_T2, C_T4, C_C, C_ACC) = range(24)
+
+    dma("S", ap("Dm", s_[:, 0:W]), ap("d0"), 128 * 3200)
+    dma("Y", ap("win"), ap("wa"), 1024)
+    dma("Y", ap("jin"), ap("j0"), 8192)
+    dma("Y", ap("SV", s_[:, 0:2, 0:H]), ap("v0"), 65536)
+    dma("Y", ap("qin"), ap("q0"), 131072 + 400000)
+    dma("Y", ap("Pt", s_[:, 0:W]), ap("p0"), 128 * 6400 + 600000)
+    iota(coli(0), [[0, 1]], 0, 1, False)
+    iota(ap("IO"), [[1, 160]], 0, 0)
+    iota(tmp(0), [[16, 8], [0, 16]], 0, 0)
+    iota(tmp(1), [[0, 8], [1, 16]], 0, 0)
+    iota(ap("dump"), [[16, 16]], W + 1 - 2048, 0)
+    iota(ap("seg"), [[2048, 8]], 2048, 0)
+    iota(ap("IOT"), [[1, W]], 0, 0)
+    ms(ap("Dm", s_[:, W:WT]), 0.0)
+    ms(ap("Pt", s_[:, W:WT]), 0)
+    ms(ap("SV", s_[:, :, H:136]), 0.0)
+    ms(ap("flag"), 0.0)
+    ms(tmp(2), 0.5)
+    for i, m in ((1, 112), (2, 15), (3, 16)):
+        ts(coli(i), coli(0), m, ALU.bitwise_and)
+    cp(ap("col", s_[:, 0:4]), ap("coli", s_[:, 0:4]))
+    ts(col(C_G15), col(C_G), 15.0, ALU.add)
+    act(col(C_H1), col(C_16), AF.Sigmoid, bias=-800.0, scale=100.0, more=1560)
+    act(col(C_H0), col(C_16), AF.Sigmoid, bias=800.0, scale=-100.0)
+    ts(col(C_P16), col(C_P), 16.0, ALU.add)
+    ts(col(C_M16), col(C_P), -16.0, ALU.add)
+    cp(ap("col", s_[:, C_W:C_W + 2]), ap("win"))
+    IO128 = ap("IO", s_[:, 0:128])
+    ts(ap("OH"), ap("IO", s_[:, 0:16]), col(C_R), ALU.is_equal)
+    ts(MT(M_BO), tmp(0), col(C_G), ALU.is_equal)
+    ts(MT(M_I), IO128, col(C_P), ALU.is_equal)
+    ts(ap("Z1"), ap("IO", s_[:, 0:144]), col(C_G15), ALU.is_equal)
+    ts(ap("ZV"), ap("Z1"), -KK, ALU.mult)
+    for m, c in ((M_NI, -1.0), (M_SG, 4.5 * K), (M_TAU, -4.5 * K), (M_R, -KK)):
+        sc(MT(m), MT(M_I), c)
+    for i in range(16):
+        if i % 2:
+            sc(ap("BI", s_[:, i, :]), MT(M_BO), OH(i))
+        else:
+            ts(ap("BI", s_[:, i, :]), MT(M_BO), OH(i), ALU.mult)
+    sc(ap("B0f"), MT(M_BO), OH(0))
+    ts(tmp(3), tmp(1), 0.0, ALU.is_equal, 2.0, ALU.mult)
+    scan(tmp(4), tmp(2), tmp(3), ALU.mult, ALU.max)
+    tt(ap("tmp", s_[:, 5, 0:16]), ap("tmp", s_[:, 4, 0:16]), ap("OH"), ALU.mult)
+    op("V", "tensor_reduce", [col(C_PW)], [col(C_PW), ap("tmp", s_[:, 5, 0:16]), AxisListType.X, ALU.add])
+    ts(col(C_BIG), col(C_R), 13.0, ALU.is_ge, 65536.0, ALU.mult)
+    ts(ap("thr"), tmp(4), col(C_BIG), ALU.max)
+    sc(MT(M_W4), MT(M_BO), 4.0)
+    ts(MT(M_WD), MT(M_BO), col(C_PW), ALU.mult, 0.5, ALU.mult)
+    ts(col(C_T0), OH(0), 4.5 * K, ALU.mult)
+    ts(col(C_LP), OH(15), -0.5 * K, ALU.mult, col(C_T0), ALU.add)
+    ts(col(C_C), OH(15), 192.0 / 65536, ALU.mult)
+    sc(MT(M_LP), MT(M_BO), col(C_LP))
+    sc(MT(M_C), MT(M_BO), col(C_C))
+    ts(col(C_T1), OH(0), -256 * K, ALU.mult)
+    ts(col(C_T2), OH(15), 256 * K, ALU.mult, col(C_T1), ALU.add)
+    ts(col(C_LQ), OH(14), -0.5 * K, ALU.mult, col(C_T2), ALU.add)
+    sc(MT(M_LQ), MT(M_BO), col(C_LQ))
+    ts(col(C_T4), OH(0), -1024.0, ALU.mult)
+    ts(col(C_A1), OH(15), 1024.0, ALU.mult, col(C_T4), ALU.add)
+    ts(col(C_A2), OH(15), -1024.0, ALU.mult, col(C_T4), ALU.add)
+    sc(MT(18), ZW("Z1", 1), col(C_A1))
+    sc(MT(19), ZW("Z1", 2), col(C_A2))
+    tt(MT(M_LA), MT(18), MT(19), ALU.add)
+    sc(MT(M_LJ), ZW("Z1", 2), OH(0))
+    sc(MT(M_LH), ZW("Z1", 0), col(C_W))
+    sc(MT(M_T00), MT(M_I), col(C_H0))
+    sc(MT(M_T11), MT(M_I), col(C_H1))
+    ts(MT(M_T10), IO128, col(C_P16), ALU.is_equal, col(C_H0), ALU.mult)
+    ts(MT(M_T01), IO128, col(C_M16), ALU.is_equal, col(C_H1), ALU.mult)
+    TM = {(0, 0): M_T00, (0, 1): M_T01, (1, 0): M_T10, (1, 1): M_T11}
+    ts(ap("dump"), ap("dump"), col(C_R), ALU.add)
+    cp(ap("RL"), IO128)
+    ts(col(C_U), col(C_A), 2.0, ALU.mult, -1.0, ALU.add)
+
+    def scales(s, u):
+        op("V", "reciprocal", [thc(s, 1)], [thc(s, 1), u], cost=240)
+        ts(thc(s, 2), u, 1.0, ALU.min, 192.0, ALU.mult)
+        ts(thc(s, 4), thc(s, 2), -BETA, ALU.mult, -6.9305, ALU.add)
+        a = 800 if s == 0 else 0
+        if a:
+            ts(ap("Ds", s_[:, 0, 0:a]), ap("Dm", s_[:, 0:a]), thc(s, 1), ALU.mult)
+        sc(ap("Ds", s_[:, s % 2, a:WD]), ap("Dm", s_[:, a:WD]), thc(s, 1))
+
+    scales(0, col(C_U))
+    for c in range(2):
+        cp(ap("SU", s_[:, c, H:136]), ap("jin", s_[:, 8 * c:8 * c + 8]))
+        cp(ap("JT", s_[:, c, :]), ap("jin", s_[:, 8 * c:8 * c + 8]))
+        cp(ap("SU", s_[:, c, 0:H]), ap("qin", s_[:, H * c:H * c + H]))
+
+    def tolist(bank, rhs_of, nq):
+        for u in range(2):
+            gq = newg()
+            for h in range(2):
+                mm(ap(bank, s_[:, u:8 * nq:2]), MT(TM[(h, u)]), rhs_of(h), gq, first=(h == 0))
+
+    def absdiff(out, lst, Dw, u_, v, buf):
+        act(buf, ind(Dw, lst), AF.Identity, scale=u_)
+        gq, o = newg(), ap(bank_(), s_[:, 0:H])
+        mm(o, MT(M_NI), v, gq, first=True)
+        mm(o, MT(M_I), buf, gq)
+        act(out, o, AF.Abs)
+
+    mv = 0
+    src = [("SU", "SV", 0), ("SU", "SV", 1)]
+    for s in range(4):
+        last = s == 3
+        Dw = ap("Ds", s_[:, s % 2, :])
+        u_ = thc(s, 0) if s else col(C_U)
+        nsrc, late = [], []
+        for c in range(2):
+            un, vn, sl = src[c]
+            jt, so = 2 * s + c, 2 * (s + 1) + c
+            ph[0] = jt
+            Qu, Ju, v = ap(un, s_[:, sl, 0:H]), ap(un, s_[:, sl, H:136]), ap(vn, s_[:, sl, 0:H])
+            if un == "LU":
+                op("X", "arrive", [ap("LU", s_[:, sl, :]), ap("LV", s_[:, sl, :])], [], extra=("arr", sl))
+                cp(ap("JT", s_[:, jt, :]), Ju)
+            pP, pQ = ap("pP%d" % c, s_[:, 0:H]), ap("pQ%d" % c, s_[:, 0:H])
+            aP, aQ = ap("pP%d" % c, s_[:, H:2 * H]), ap("pQ%d" % c, s_[:, H:2 * H])
+            P16, Q16, Jb = ap("PQ", s_[:, c, 0, :]), ap("PQ", s_[:, c, 1, :]), ap("Jb", s_[:, c, :])
+            Pu, actb = ap("Pu", s_[:, c, :]), ap("act", s_[:, c, :])
+            cp(Q16, Qu)
+            cp(Jb, ind(ap("IOT"), Ju))
+            cp(Pu, ind(ap("Pt", s_[:, 0:W]), Ju))
+            cp(P16, Pu)
+            for f in late:
+                f()
+            late = []
+            pM = bank_()
+            for b in range(8):
+                ts(ap("E", s_[:, c, b, 0:H - 16 * b]), ap("Jb", s_[:, c, 16 * b:H]), ap("JT", s_[:, jt, b:b + 1]), ALU.is_equal)
+            gq = newg()
+            mm(ap(pM, s_[:, 0:H]), MT(M_NI), ap("thr"), gq, first=True)
+            for b in range(8):
+                mm(ap(pM, s_[:, 16 * b:16 * b + 16]), MT(M_WD), ap("E", s_[:, c, b, 0:16]), gq)
+            for b in range(7):
+                mm(ap(pM, s_[:, 16 * b + 16:H]), MT(M_W4), ap("E", s_[:, c, b, 16:H - 16 * b]), gq)
+            for b in range(8 * c):
+                ts(ap("E2", s_[:, b, :]), Jb, ap("JT", s_[:, jt - 1, b:b + 1]), ALU.is_equal)
+                mm(ap(pM, s_[:, 0:H]), MT(M_W4), ap("E2", s_[:, b, :]), gq)
+            act(actb, ap(pM, s_[:, 0:H]), AF.Sign, bias=-2.0 ** -16, scale=-1.0, acc=None if last else col(C_ACC + c))
+            pM = bank_()
+            for t, x in ((1, Q16), (0, P16)):
+                gq = newg()
+                mm(ap(pM, s_[:, H * t:H * t + H]), MT(M_NI), Jb, gq, first=True)
+                mm(ap(pM, s_[:, H * t:H * t + H]), MT(M_I), x, gq)
+            act(ap("sg", s_[:, c]), ap(pM, s_[:, 0:2 * H]), AF.Sign, bias=-0.5)
+            absdiff(ap("nd", s_[:, c, :]), Ju, Dw, u_, v, ap("Dj", s_[:, c, 0, :]))
+            gq, o = newg(), ap(bank_(), s_[:, 0:H])
+            mm(o, MT(M_LH), v, gq, first=True)
+            mm(o, MT(M_LJ), Jb, gq)
+            mm(o, MT(M_LA), actb, gq)
+            tr(ap("XT", s_[:, c]), o)
+            cp(ap("tM", s_[:, c]), ap("XT", s_[:, c, 2::16]))
+            cp(ap("hi", s_[:, c, 0]), ap("XT", s_[:, c, 0::16]))
+            ts(ap("hi", s_[:, c, 1]), ap("hi", s_[:, c, 0]), 1023, ALU.bitwise_and)
+            tt(ap("flag", s_[:, c, 0::16]), ap("hi", s_[:, c, 1]), ap("seg"), ALU.add)
+            pM = bank_()
+            tolist(pM, lambda h: ap("tM", s_[:, c, h::2]), 1)
+            tt(ap("sc1", s_[:, c, :]), ap(pM, s_[:, 0:8]), ap("dump", s_[:, 8 * c:8 * c + 8]), ALU.min)
+            act(ap("jm", s_[:, c, :]), ap(pM, s_[:, 0:8]), AF.Identity)
+            scu = ap("scu", s_[:, c, :])
+            ts(scu, ap("sc1", s_[:, c, :]), 2048.0, ALU.add)
+            cp(ind(ap("Dm"), scu), ap("nd", s_[:, c, :]))
+            if c == 1 and last:
+                dma("Y", ap("yd"), ap("Dm", s_[:, 0:W]), 128 * 3200)
+            elif c == 1:
+                gq, o = newg(), ap(bank_(), s_[:, 0:1])
+                mm(o, ap("B0f"), col(C_ACC), gq, first=True, f=4.0)
+                mm(o, ap("B0f"), col(C_ACC + 1), gq, f=4.0)
+                ts(ap("thi", s_[:, s, 0:1]), o, -0.5, ALU.mult, 128.0, ALU.add)
+                ts(ap("thi", s_[:, s, 1:2]), ap("thi", s_[:, s, 0:1]), 3, ALU.bitwise_and)
+                ts(thc(s + 1, 0), ap("thi", s_[:, s, 1:2]), 2.0, ALU.mult, col(C_U), ALU.add)
+                scales(s + 1, thc(s + 1, 0))
+            g1 = newg()
+            mm(aQ, MT(M_C), ap("thr"), g1, first=True)
+            for k in range(4):
+                sb, bank = new(3) % 4, bank_()
+                for i in range(4):
+                    gq, o = newg(), ap(bank, s_[:, H * i:H * i + H])
+                    mm(o, ap("BI", s_[:, 4 * k + i, :]), Q16, gq, first=True)
+                    mm(o, MT(M_NI), P16, gq)
+                act(ap("sig", s_[:, sb]), ap(bank), AF.Sigmoid, bias=-4.125, scale=128.0)
+                for i in range(4):
+                    mm(aQ, ZW("Z1", 4 * k + i), ap("sig", s_[:, sb, H * i:H * i + H]), g1)
+            for l0 in range(0, VS, 32):
+                act(ap("vr", s_[:, c, 16 * l0:16 * l0 + 512]), ind(v, ap("RL", s_[:, l0:l0 + 32])), AF.Identity, bias=-192.0, scale=thc(s, 1))
+            if VS < H:
+                x = ap("v1", s_[:, c, VS:H])
+                act(x, ap(vn, s_[:, sl, VS:H]), AF.Identity, bias=-192.0, scale=thc(s, 1))
+                for i in range(16):
+                    o = ap("vr", s_[:, c, 16 * VS + i::16])
+                    op("G", "affine_select", [o], [o, x, [[0, H - VS]], ALU.is_ge, 0.0, 0, 0], cost=205 + 2 * (H - VS))
+            sp = SP[jt]
+            gP, gP2, gQ = newg(), newg(), newg()
+            if sp:
+                mm(aP, MT(M_C), ap("thr"), gP, first=True)
+            else:
+                mm(pP, MT(M_SG), ap("sg", s_[:, c, 0:H]), gP2, first=True)
+            for t, ln, ls, pa, pb, ga, gb, ns in ((1, un, sl, aQ, pQ, g1, gQ, H), (0, "Pu", c, aP, pP, gP, gP2, sp)):
+                for l0 in range(0, H, PA):
+                    x = slice(16 * l0, 16 * (l0 + PA))
+                    y, o = ap("yy", s_[:, c, t, x]), ap("ia", s_[:, c, t, x])
+                    tt(y, ind(Dw, ap(ln, s_[:, ls, l0:l0 + PA])), ap("vr", s_[:, c, x]), ALU.subtract)
+                    if l0 < ns:
+                        act(o, y, AF.Sigmoid, bias=thc(s, 4), scale=BETA)
+                    else:
+                        ts(o, y, thc(s, 2), ALU.is_equal, 1.0 / 1024, ALU.mult)
+                for i in range(16):
+                    mm(pa if ns else pb, ZW("Z1" if ns else "ZV", i), ap("ia", s_[:, c, t, i::16]), ga if ns else gb)
+                if ns:
+                    act(ap("rr", s_[:, c, t, :]), pa, AF.Identity)
+                    tt(ap("fr", s_[:, c, t, :]), pa, ap("rr", s_[:, c, t, :]), ALU.subtract)
+                    mm(pb, MT(M_SG), ap("sg", s_[:, c, H * t:H * t + H]), gb, first=True)
+                    mm(pb, MT(M_R), ap("fr", s_[:, c, t, :]), gb)
+                mm(pb, MT(M_LQ if t else M_LP), actb, gb)
+            act(ap("tau", s_[:, c, :]), pP, AF.Sign)
+            mm(pQ, MT(M_TAU), ap("tau", s_[:, c, :]), gQ)
+            tt(pP, pP, P16, ALU.min)
+            tt(ap("WQ", s_[:, c, :]), pQ, Q16, ALU.min)
+            Ww = ap("Ww", s_[:, c, :])
+            tt(Ww, pP, ap("WQ", s_[:, c, :]), ALU.max)
+            if last:
+                act(ap("yqb", s_[:, c, :]), Ww, AF.Relu)
+                dma("Y", ap("yq", s_[:, H * c:H * c + H]), ap("yqb", s_[:, c, :]), 65536)
+            else:
+                late.append(lambda Ww=Ww, scu=scu: cp(ind(ap("Pt"), scu), Ww))
+                cp(ap("SU", s_[:, so, 0:H]), Ww)
+            act(ap("Wa", s_[:, c, :]), Ww, AF.Abs)
+            tr(ap("WTr", s_[:, c, :]), ap("Wa", s_[:, c, :]))
+            scan(ap("scn", s_[:, c]), ap("flag", s_[:, c]), ap("WTr", s_[:, c, :]), ALU.max, ALU.min)
+            ts(ap("fi", s_[:, c]), ap("scn", s_[:, c, 15::16]), 2047, ALU.bitwise_and)
+            tt(ap("fM", s_[:, c, 0:8]), ap("fi", s_[:, c]), ap("XT", s_[:, c, 1::16]), ALU.add)
+            tt(ap("fM", s_[:, c, 8:16]), ap("fi", s_[:, c]), ap("XT", s_[:, c, 1::16]), ALU.subtract)
+            pM = bank_()
+            tolist(pM, lambda h: ap("fM", s_[:, c, h::2]), 2)
+            fz = ap("fz", s_[:, c, :])
+            ts(fz, ap(pM, s_[:, 0:8]), float(W), ALU.min)
+            tt(ap("JT", s_[:, so, :]), ap(pM, s_[:, 8:16]), ap("jm", s_[:, c, :]), ALU.max)
+            cp(ap("SU", s_[:, so, H:136]), ap("JT", s_[:, so, :]))
+            absdiff(ap("SV", s_[:, so, 0:H]), fz, Dw, u_, v, ap("Dj", s_[:, c, 1, :]))
+            if last:
+                act(ap("yjb", s_[:, c, :]), ind(ap("IOT"), ap("SU", s_[:, so, H:136])), AF.Identity)
+                dma("Y", ap("yv", s_[:, H * c:H * c + H]), ap("SV", s_[:, so, 0:H]), 32768)
+                dma("Y", ap("yj", s_[:, H * c:H * c + H]), ap("yjb", s_[0:128:16, c, :]), 4096)
+            if HOP[s]:
+                op("G", "send", [], [None, ap("SU", s_[:, so, :]), ap("SV", s_[:, so, :])], cost=300.0, extra=("send", 2 * mv + c, so))
+                nsrc.append(("LU", "LV", 2 * mv + c))
+            else:
+                nsrc.append(("SU", "SV", so))
+        for f in late:
+            f()
+        mv += 1 if HOP[s] else 0
+        src = nsrc
+    return ops
+
+
+def depend(ops):
+    deps = [set() for _ in ops]
+    hist, firsts, sends, sess = {}, {}, {}, {}
+    for k, o in enumerate(ops):
+        acc = [(x, True) for x in o["wr"]] + [(x, False) for x in o["rd"]]
+        for (nm, lo, hi, _, _), w in acc:
+            ps = is_ps(nm)
+            for (j, lo2, hi2, w2) in hist.get(nm, ()):
+                p = ops[j]
+                if ps:
+                    if p["eng"] != o["eng"] or o["grp"] != p["grp"] or o["grp"] is None and (w or w2):
+                        deps[k].add(j)
+                elif (w or w2) and (lo < hi2 and lo2 < hi or (p["extra"] or o["extra"])
+                                    and lo // 16 <= (hi2 - 1) // 16 and lo2 // 16 <= (hi - 1) // 16):
+                    deps[k].add(j)
+        if o["grp"] is not None:
+            if o["first"]:
+                firsts[o["grp"]] = k
+            else:
+                deps[k].add(firsts[o["grp"]])
+        if o["meth"] == "send":
+            sends[o["extra"][1]] = k
+        if o["meth"] == "arrive":
+            deps[k].add(sends[o["extra"][1]])
+        for (nm, lo, hi, _, _), w in acc:
+            hist.setdefault(nm, []).append((k, lo, hi, w))
+        deps[k].discard(k)
+        if o["bank"]:
+            sess.setdefault(o["bank"], []).append(k)
+    for lst in sess.values():
+        inside = set(lst)
+        for k in lst[1:]:
+            deps[lst[0]] |= {j for j in deps[k] - inside if j < lst[0]}
+            deps[k].add(lst[0])
+    return deps, sess
+
+
+def latency(o):
+    return o["extra"][2] if o["meth"] == "dma_start" else COMM if o["meth"] == "arrive" else o["cost"]
+
+
+def gap(ops, j, e):
+    return (0.0 if e == "T" else 40.0) if ops[j]["eng"] == e else SYNC
+
+
+def schedule(ops, deps0, sess, seed, key=None):
+    n = len(ops)
+    deps = [set(d) for d in deps0]
+    rng = np.random.default_rng(seed)
+    succ = [[] for _ in range(n)]
+    for k in range(n):
+        for j in deps[k]:
+            succ[j].append(k)
+    if key is None:
+        pr = [0.0] * n
+        for k in range(n - 1, -1, -1):
+            pr[k] = latency(ops[k]) + max([pr[m] + gap(ops, m, ops[k]["eng"]) for m in succ[k]] + [0.0])
+        phw, amp = PH * float(rng.uniform(0.3, 2.0)), float(rng.uniform(0, 600))
+        key = [pr[k] - phw * ops[k]["ph"] + amp * float(x) for k, x in enumerate(rng.random(n))]
+    left = [len(d) for d in deps]
+    ready_t, done_t, isdone = [0.0] * n, [0.0] * n, [False] * n
+    free = {e: 0.0 for e in ENG + ("X",)}
+    ready = {e: [k for k in range(n) if not left[k] and ops[k]["eng"] == e] for e in free}
+    holder = {b: [] for b in POOL}
+    order, banks, start = [], {}, [0.0] * n
+    opens = [bool(o["bank"]) and sess[o["bank"]][0] == k for k, o in enumerate(ops)]
+    while len(order) < n:
+        best = None
+        fb = [(max([done_t[j] for j in h] + [0.0]), b) for b, h in holder.items() if all(isdone[j] for j in h)]
+        fb = min(fb) if fb else None
+        for e, lst in ready.items():
+            rt = {k: max(ready_t[k], fb[0] + SYNC) if opens[k] else ready_t[k] for k in lst if fb or not opens[k]}
+            if rt:
+                t0 = max(free[e], min(rt.values()))
+                k = max((k for k in rt if rt[k] <= t0 + SLACK), key=lambda k: (key[k], -k))
+                t = max(free[e], rt[k])
+                if best is None or t < best[0]:
+                    best = (t, e, k)
+        t, e, k = best
+        ready[e].remove(k)
+        order.append(k)
+        isdone[k] = True
+        if opens[k]:
+            deps[k] |= set(holder[fb[1]])
+            holder[fb[1]] = sess[ops[k]["bank"]]
+            banks[ops[k]["bank"]] = fb[1]
+        free[e] = t + (ops[k]["cost"] if e != "X" else 0.0)
+        done_t[k] = t + latency(ops[k])
+        start[k] = t
+        for m in succ[k]:
+            ready_t[m] = max(ready_t[m], done_t[k] + gap(ops, m, e))
+            left[m] -= 1
+            if not left[m]:
+                ready[ops[m]["eng"]].append(m)
+    return max(done_t), order, deps, banks, start
+
+
+def backward(ops, deps, start):
+    n = len(ops)
+    left = [0] * n
+    for d in deps:
+        for j in d:
+            left[j] += 1
+    end = [start[k] + latency(ops[k]) for k in range(n)]
+    busy = [o["cost"] if o["eng"] != "X" else 0.0 for o in ops]
+    ready = {e: [k for k in range(n) if not left[k] and ops[k]["eng"] == e] for e in ENG + ("X",)}
+    free = {e: 0.0 for e in ready}
+    rt, out = [0.0] * n, [0.0] * n
+    for _ in range(n):
+        best = None
+        for e, lst in ready.items():
+            if lst:
+                t0 = max(free[e], min(rt[k] for k in lst))
+                k = max((k for k in lst if rt[k] <= t0 + SLACK), key=lambda k: end[k])
+                t = max(free[e], rt[k])
+                if best is None or t < best[0]:
+                    best = (t, e, k)
+        t, e, k = best
+        ready[e].remove(k)
+        free[e] = out[k] = t + busy[k]
+        for j in deps[k]:
+            rt[j] = max(rt[j], out[k] + latency(ops[j]) - busy[j] + gap(ops, j, e))
+            left[j] -= 1
+            if not left[j]:
+                ready[ops[j]["eng"]].append(j)
+    return out
+
+
+def program():
+    ops = build()
+    deps0, sess = depend(ops)
+    best = None
+    for i in range(TRIES):
+        r = schedule(ops, deps0, sess, i)
+        for x in range(ROUNDS):
+            r = schedule(ops, deps0, sess, 0, backward(ops, deps0, r[4]))
+            if best is None or r[0] < best[0]:
+                best = r
+    rng, cur = np.random.default_rng(1), best
+    cl = [o["eng"] + (o["wr"][0][0] if o["wr"] and not o["bank"] else "") + str(o["ph"]) for o in ops]
+    names = sorted(set(cl))
+    for i in range(MORE):
+        off = {names[int(x)]: float(rng.normal() * 2500) for x in rng.integers(0, len(names), 6)}
+        base = [-x for x in cur[4]] if i % 2 else backward(ops, deps0, cur[4])
+        r = schedule(ops, deps0, sess, 0, [x + off.get(c, 0.0) for x, c in zip(base, cl)])
+        if r[0] < cur[0] + 150:
+            cur = r
+        if r[0] < best[0]:
+            best = r
+    total, order, deps, banks, start = best
+    order = list(range(NLOAD)) + [k for k in order if k >= NLOAD and ops[k]["eng"] != "X"]
+    pos = {k: i for i, k in enumerate(order)}
+    pos.update({k: 0 for k, o in enumerate(ops) if o["eng"] == "X"})
+    lastg = {ops[k]["grp"]: k for k in order}
+    seen = {e: {} for e in ENG}
+    marks, waits = set(), {}
+    for k in order:
+        e, m = ops[k]["eng"], {}
+        for j in deps[k]:
+            b = ops[j]
+            if b["meth"] == "send" or e == "T" and b["eng"] == "T":
+                continue
+            key = b["extra"][:2] if b["extra"] else b["eng"]
+            if key not in m or pos[j] > pos[m[key]]:
+                m[key] = j
+        waits[k] = []
+        for key, j in m.items():
+            if seen[e].get(key, -1) < pos[j]:
+                seen[e][key] = pos[j]
+                waits[k].append((key, j)); marks.add(j)
+    cnt, val, out = {e: 0 for e in ENG}, {}, []
+    for k in order:
+        o = ops[k]
+        o["t"] = start[k]
+        if k in marks and not o["extra"]:
+            cnt[o["eng"]] += 1
+            val[k] = cnt[o["eng"]]
+        w = [("e" + key, val[j]) if key in ENG else ("dm%d" % key[1], 16) if key[0] == "dma" else ("arr%d" % key[1], None)
+             for key, j in waits[k]]
+        tail = [o["first"], lastg[o["grp"]] == k] if o["meth"] == "matmul" else []
+        out.append((o, w, tail, k in val))
+    return out, banks, total, ops
+
+
+_prog = []
+
+
+def res(T, banks, a):
+    if not is_ap(a):
+        return a
+    if a[0] == "ind":
+        return res(T, banks, a[1]).indirect(res(T, banks, a[2]))
+    return T[banks.get(a[1], a[1])][a[2] if len(a[2]) > 1 else a[2][0]]
+
+
+def halves(topo, a, b):
+    e = topo.engines(a, b)
+    h = len(e) // 2
+    return sum(1 << x for x in e[:h]), sum(1 << x for x in e[h:]), h
+
+
+def relay_of(T, topo, core):
+    r = T.rank_of(core)
+    dsts = [T.cores[(r + h) % len(T.cores)] for h in HOP if h]
+    c = [x for x in topo.cores_of(core) if T.rank_of(x) is None and all(topo.may_write(x, d) for d in dsts)]
+    c.sort(key=lambda x: topo.die(x) != topo.die(core))
+    return c[0]
+
+
+def pair(g, T, topo, me, to, su, sv, slot, sem, local):
+    rid, pid = topo.addr(to, me)
+    m0, m1, h = halves(topo, me, to)
+    d = [DstId(rid=rid, pnc=pid)]
+    g.remote_dma_fused([
+        RemoteDMATransfer(dst_ids=d, dma_engine_mask=m0, remote_sem=sem, src=su, dst=T.LU[:, slot, 0:136]),
+        RemoteDMATransfer(dst_ids=d, dma_engine_mask=m1, remote_sem=sem, src=sv, dst=T.LV[:, slot, 0:136])], local_sem=local)
+    return 2 * h
+
+
+def call(e, m, args, kw):
+    if m == "matmul": return e.matmul(*args)
+    if m == "activation": return e.activation(*args, **kw)
+    if m == "tensor_copy": return e.tensor_copy(*args)
+    if m == "tensor_tensor": return e.tensor_tensor(*args)
+    if m == "tensor_scalar": return e.tensor_scalar(*args)
+    if m == "tensor_reduce": return e.tensor_reduce(*args)
+    if m == "tensor_tensor_scan": return e.tensor_tensor_scan(*args)
+    if m == "transpose": return e.transpose(*args)
+    if m == "reciprocal": return e.reciprocal(*args)
+    if m == "memset": return e.memset(*args)
+    if m == "affine_select": return e.affine_select(*args)
+    if m == "iota": return e.iota(*args, **kw)
+    return e.dma_start(*args)
+
+
+def rank_program(g, core, T, topo):
+    rank = T.rank_of(core)
+    n = len(T.cores)
+    hops = [h for h in HOP if h]
+    if rank is None:
+        for r, c in enumerate(T.cores):
+            if relay_of(T, topo, c) == core:
+                tot = 0
+                for slot in range(4):
+                    g.wait_ge(T.sem["rel%d" % slot], 2 * halves(topo, c, core)[2])
+                    tot += pair(g, T, topo, core, T.cores[(r + hops[slot // 2]) % n], T.LU[:, slot, 0:136], T.LV[:, slot, 0:136],
+                                slot, T.sem["arr%d" % slot], T.sem.fwd)
+                g.wait_ge(T.sem.fwd, tot)
+        return
+    if not _prog:
+        _prog.append(program())
+    calls, banks = _prog[0][:2]
+    q = {"V": g.vector, "S": g.scalar, "T": g.tensor, "G": g, "Y": g.sync}
+    relay = relay_of(T, topo, core)
+    sent, dmas = 0, []
+    for o, waits, tail, inc in calls:
+        e, m = q[o["eng"]], o["meth"]
+        for nm, val in waits:
+            if val is None:
+                frm = T.cores[(rank - hops[int(nm[3:]) // 2]) % n]
+                val = 2 * halves(topo, relay_of(T, topo, frm), core)[2]
+            e.wait_ge(T.sem[nm], val)
+        if m == "send":
+            _, slot, so = o["extra"]
+            sent += pair(g, T, topo, core, relay, T.SU[:, so, 0:136], T.SV[:, so, 0:136], slot, T.sem["rel%d" % slot], T.sem.sent)
+            continue
+        ins = call(e, m, [res(T, banks, a) for a in o["args"]] + tail, {k: res(T, banks, a) for k, a in o["kw"].items()})
+        if m == "dma_start":
+            ins.then_inc(T.sem["dm%d" % o["extra"][1]], 16); dmas.append(o["extra"][1])
+        elif inc:
+            ins.then_inc(T.sem["e" + o["eng"]], 1)
+    for d in dmas:
+        g.sync.wait_ge(T.sem["dm%d" % d], 16)
+    g.wait_ge(T.sem.sent, sent)

@@ -5,50 +5,60 @@ from concourse.mybir import AluOpType as ALU, AxisListType, ActivationFunctionTy
 W, L, H = 1600, 256, 128
 HOP = (1, 0, 3, 0)
 PA = 64
-VS = 64
-SP = (128, 0) * 4
-K = 65536.0
-KK = K * 1024.0
-BETA = 96.0
-WT = 1864
+SUMN = 128
+DV = (0, 0, 0, 0, 0, 0, 0, 1)
+EARLY = 1
+VDF = 0
+VABS = 1
+FIX1 = 1
+KP, KQ = 6144.0, 3072.0
+MAGIC = 12582912.0
+BIG = 2.0 ** 75
+WT = 1872
 WD = 1608
 G_ = 1.56
 SC_ = 3.8
-PEF = 0.6
-COMM = 7500.0
-SYNC = 140.0
+PEF = 0.5
+TOV = 8.0
+COMM = 6500.0
+SYNC = 150.0
+SAME = 100.0
 SLACK = 40.0
-PH = 3000.0
-TRIES = 3
-ROUNDS = 6
-MORE = 300
+SL2 = 110.0
+PH = 10000.0
+ROUNDS = 4
+MORE = 1500
 f32, bf, f16, i32, u16 = "float32", "bfloat16", "float16", "int32", "uint16"
 SZ = {f32: 4, bf: 2, f16: 2, i32: 4, u16: 2}
+WA = f16 if VABS else f32
 SB = {
-    "Dm": ([WT], bf), "Ds": ([2, WD], f32), "Pt": ([WT], i32), "IOT": ([W], f32), "IO": ([160], f32),
+    "Dm": ([5, WT], bf), "Pt": ([WT], i32), "IOT": ([W], f32), "IO": ([160], f32),
     "jin": ([16], i32), "qin": ([L], i32), "win": ([2], i32),
-    "SU": ([10, 144], u16), "SV": ([10, 144], bf), "LU": ([4, 144], u16), "LV": ([4, 144], bf), "JT": ([10, 8], f32),
-    "col": ([32], f32), "coli": ([8], i32), "thc": ([4, 8], f32), "thi": ([4, 4], i32),
-    "ZV": ([144], bf), "Z1": ([144], bf), "BI": ([16, 128], bf), "MT": ([20, 128], bf), "B0f": ([128], f32),
-    "tmp": ([6, 128], f32), "thr": ([128], bf), "OH": ([16], f32), "RL": ([128], u16), "seg": ([8], f32),
+    "SU": ([10, 144], u16), "SV": ([10, 144], bf), "SX": ([8, H], u16),
+    "LU": ([4, 144], u16), "LV": ([4, 144], bf), "LX": ([4, H], u16), "JT": ([10, 8], f32),
+    "col": ([32], f32), "coli": ([8], i32), "thc": ([4, 8], f32), "thi": ([4, 4], i32), "cd": ([4, 2, 128], f16),
+    "ZP": ([144], bf), "ZQ": ([144], bf), "Z1": ([144], bf), "RS": ([16, 128], bf), "MT": ([18, 128], bf), "B0f": ([128], f32),
+    "tmp": ([6, 128], f32), "tmi": ([2, 128], i32), "ZB": ([128], bf), "thr": ([128], bf), "OH": ([16], f32), "PW": ([8], f32),
     "dump": ([16], f32), "Pu": ([2, H], u16), "PQ": ([2, 2, H], f16), "Jb": ([2, H], f16),
-    "E": ([2, 8, H], bf), "E2": ([8, H], bf), "act": ([2, H], bf), "sg": ([2, 2 * H], bf), "tau": ([2, H], bf),
-    "rr": ([2, 2, H], bf), "fr": ([2, 2, H], bf), "sig": ([4, 4 * H], bf), "Dj": ([2, 2, H], bf), "nd": ([2, H], bf),
-    "XT": ([2, H], f32), "hi": ([2, 2, 8], i32), "flag": ([2, H], f32), "tM": ([2, 8], f16),
-    "sc1": ([2, 8], f32), "scu": ([2, 8], u16), "jm": ([2, 8], f32), "WQ": ([2, H], f32), "Ww": ([2, H], f32),
-    "Wa": ([2, H], f32), "WTr": ([2, H], f32), "scn": ([2, H], i32), "fi": ([2, 8], i32),
-    "fM": ([2, 16], f16), "fz": ([2, 8], u16), "yqb": ([2, H], f32), "yjb": ([2, H], f32),
-    "v1": ([2, H], f32), "vr": ([2, H * 16], f32), "yy": ([2, 2, H * 16], bf), "ia": ([2, 2, H * 16], bf),
+    "E": ([2, 8, H], bf), "E2": ([8, H], bf), "act": ([2, H], bf), "sg": ([2, 2 * H], bf),
+    "rr": ([2, H], bf), "fr": ([2, H], bf), "sig": ([2, 8 * H], bf), "Df": ([2, H], bf), "nd": ([2, H], bf),
+    "XT": ([2, H], f32), "hi": ([2, 2, 8], i32), "hh": ([2, 8], f32), "flag": ([H], WA), "tM": ([2, 8], f16),
+    "sc1": ([2, 8], f32), "scu": ([2, 8], u16), "jm": ([2, 8], f32), "WQ": ([2, H], f16), "X": ([2, H], f16),
+    "Ut": ([2, H], f32), "U": ([2, H], f16), "Wa": ([2, H], WA), "WTr": ([2, H], WA), "scn": ([2, H], WA),
+    "fi": ([2, 2, 8], i32), "fM": ([2, 16], f16), "fz": ([2, 8], u16), "yqb": ([2, 2, H], f32), "yjb": ([2, H], f32),
+    "GJ": ([2, 2, 136 * 16], bf), "mk": ([2, 2, 2, H * 8], bf),
 }
-POOL = ("pD0", "pD1", "pM0", "pM1")
+POOL = ("pD0", "pD1", "pM0", "pM1") + (("pQ0", "pQ1") if FIX1 else ())
 SCRATCH = {k: ("sbuf", [128] + v[0], v[1]) for k, v in SB.items()}
-SCRATCH.update({k: ("psum", [128, 512], f32) for k in POOL + ("pQ0", "pQ1", "pP0", "pP1")})
+SCRATCH.update({k: ("psum", [128, 512], f32) for k in ("pD0", "pD1", "pM0", "pM1", "pQ0", "pQ1", "pP0", "pP1")})
 IOS = {"d0": ([128, W], bf), "p0": ([128, W], i32), "j0": ([128, 16], i32), "q0": ([128, L], i32), "v0": ([128, L], bf),
        "wa": ([128, 2], i32), "yd": ([128, W], bf), "yj": ([8, L], f32), "yq": ([128, L], f32), "yv": ([128, L], bf)}
 ENG = ("V", "S", "T", "G", "Y")
-SEMAPHORES = (["eV", "eS", "eT", "eG"] + ["dm%d" % i for i in range(16)] + ["rel%d" % i for i in range(4)]
-              + ["arr%d" % i for i in range(4)] + ["sent", "fwd"])
-NLOAD = 6
+PARTS = {"x": (("SX", "LX", H, 0),), "u": (("SU", "LU", 136, 0), ("SV", "LV", 136, 1))}
+MSGS = [k + str(i) for i in range(4) for k in (("x", "u") if EARLY else ("u",))]
+SEMAPHORES = (["eV", "eS", "eT", "eG"] + ["dm%d" % i for i in range(20)] + ["rel" + m for m in MSGS]
+              + ["arr" + m for m in MSGS] + ["sent", "fwd"])
+NLOAD = 7
 s_ = np.s_
 
 
@@ -85,11 +95,11 @@ def is_ps(name):
 
 
 def build():
-    ops, ph, cnt = [], [0], [0, 0, 0, 0]
+    ops, ph, cnt = [], [0, 0], [0, 0, 0, 0]
 
-    def op(eng, meth, outs, args, kw=None, cost=64.0, grp=None, first=False, extra=None):
+    def op(eng, meth, outs, args, kw=None, cost=64.0, grp=None, first=False, extra=None, after=()):
         kw = kw or {}
-        wr, rd = [], []
+        wr, rd = [], [span(a) for a in after]
         for o in outs:
             if o[0] == "ind":
                 wr.append(span(o[1])); rd.append(span(o[2]))
@@ -100,7 +110,7 @@ def build():
                 rd += [span(a[1]), span(a[2])] if a[0] == "ind" else [span(a)]
         bank = [x[0] for x in wr + rd if x[0][0] == "#"]
         ops.append(dict(eng=eng, meth=meth, args=args, kw=kw, wr=wr, rd=rd, cost=cost, grp=grp, first=first, extra=extra,
-                        ph=ph[0], bank=bank[0] if bank else None))
+                        ph=ph[0], cls=ph[1], bank=bank[0] if bank else None))
 
     def vcost(out, ins, base):
         if out[0] == "ind":
@@ -118,8 +128,8 @@ def build():
     def ts(out, a, s1, o1, s2=None, o2=None):
         op("V", "tensor_scalar", [out], [out, a, s1, s2, o1] + ([o2] if o2 is not None else []), cost=vcost(out, [a], 1))
     def ms(out, c): op("V", "memset", [out], [out, c], cost=max(64.0, 30 + nel(out) * span(out)[4] / 4))
-    def tr(out, a): op("V", "transpose", [out], [out, a], cost=30 + H)
-    def scan(out, a, b, o0, o1): op("V", "tensor_tensor_scan", [out], [out, a, b, 0.0, o0, o1], cost=30 + H)
+    def tr(out, a): op("V", "transpose", [out], [out, a], cost=vcost(out, [a], 1))
+    def scan(out, a, b, o0, o1): op("V", "tensor_tensor_scan", [out], [out, a, b, 0.0, o0, o1], cost=vcost(out, [a, b], 1))
     def act(out, a, f, bias=None, scale=None, acc=None, more=0):
         kw = {k: x for k, x in (("bias", bias), ("scale", scale), ("accum_out", acc)) if x is not None}
         op("S", "activation", [out] + ([acc] if acc else []), [out, a, f], kw,
@@ -131,39 +141,45 @@ def build():
     def newg(): return new(0)
     def bank_(): return "#%d" % new(1)
     def mm(out, lt, rhs, grp, first=False, f=1.0):
-        op("T", "matmul", [out], [out, lt, rhs], cost=max(64, nel(rhs)) * f * PEF + 8, grp=grp, first=first)
-    def dma(q, out, a, nbytes):
-        op(q, "dma_start", [out], [out, a], cost=60.0, extra=("dma", new(2) - 1, 2200 + nbytes / 150.0))
+        op("T", "matmul", [out], [out, lt, rhs], cost=max(64, nel(rhs)) * f * PEF + TOV, grp=grp, first=first)
+    def dma(q, out, a, nbytes, after=()):
+        op(q, "dma_start", [out], [out, a], cost=60.0, extra=("dma", new(2) - 1, 2200 + nbytes / 150.0), after=after)
     def iota(out, pat, base, cm, fl=True):
         op("G", "iota", [out], [out, pat, base, cm], {"allow_small_or_imprecise_dtypes": True} if fl else {}, cost=160 + 2 * nel(out))
+    def send(kind, slot, so):
+        op("G", "send", [], [None] + [ap(p[0], s_[:, so]) for p in PARTS[kind]], cost=300.0, extra=("send", kind + str(slot), so))
+    def arrive(kind, slot):
+        op("X", "arrive", [ap(p[1], s_[:, slot]) for p in PARTS[kind]], [], extra=("arr", kind + str(slot)))
     def col(i): return ap("col", s_[:, i:i + 1])
     def coli(i): return ap("coli", s_[:, i:i + 1])
     def MT(i): return ap("MT", s_[:, i, :])
+    def RS(i): return ap("RS", s_[:, i, :])
     def tmp(i): return ap("tmp", s_[:, i, :])
     def OH(i): return ap("OH", s_[:, i:i + 1])
     def ZW(z, i): return ap(z, s_[:, 15 - i:143 - i])
     def thc(s, i): return ap("thc", s_[:, s, i:i + 1])
-    (M_I, M_NI, M_SG, M_TAU, M_R, M_W4, M_WD, M_LP, M_LQ, M_LA, M_LJ, M_LH, M_T00, M_T01, M_T10, M_T11, M_BO, M_C) = range(18)
+    def Dm(s, a=0, b=W): return ap("Dm", s_[:, s, a:b])
+    (M_I, M_NI, M_SP, M_SQ, M_N2, M_R, M_LP, M_LQ, M_LA, M_LJ, M_LH, M_T00, M_T01, M_T10, M_T11, M_BO, M_C, M_C3) = range(18)
     (C_P, C_G, C_R, C_16, C_G15, C_H0, C_H1, C_P16, C_M16, C_PW, C_BIG, C_LP, C_LQ, C_A1, C_A2, C_W, C_A, C_U, C_T0, C_T1,
-     C_T2, C_T4, C_C, C_ACC) = range(24)
+     C_T4, C_C, C_C3, C_ACC) = range(24)
 
-    dma("S", ap("Dm", s_[:, 0:W]), ap("d0"), 128 * 3200)
-    dma("Y", ap("win"), ap("wa"), 1024)
-    dma("Y", ap("jin"), ap("j0"), 8192)
-    dma("Y", ap("SV", s_[:, 0:2, 0:H]), ap("v0"), 65536)
-    dma("Y", ap("qin"), ap("q0"), 131072 + 400000)
+    dma("S", Dm(0), ap("d0"), 128 * 3200 + 100000)
+    dma("Y", ap("qin"), ap("q0"), 131072 + 100000)
+    dma("Y", ap("jin"), ap("j0"), 8192 + 100000)
+    dma("Y", ap("win"), ap("wa"), 1024 + 100000)
+    dma("Y", ap("SV", s_[:, 0:2, 0:H]), ap("v0"), 65536 + 400000)
     dma("Y", ap("Pt", s_[:, 0:W]), ap("p0"), 128 * 6400 + 600000)
+    dma("Y", Dm(1), ap("d0"), 128 * 3200 + 1420000)
     iota(coli(0), [[0, 1]], 0, 1, False)
     iota(ap("IO"), [[1, 160]], 0, 0)
     iota(tmp(0), [[16, 8], [0, 16]], 0, 0)
     iota(tmp(1), [[0, 8], [1, 16]], 0, 0)
     iota(ap("dump"), [[16, 16]], W + 1 - 2048, 0)
-    iota(ap("seg"), [[2048, 8]], 2048, 0)
     iota(ap("IOT"), [[1, W]], 0, 0)
-    ms(ap("Dm", s_[:, W:WT]), 0.0)
-    ms(ap("Pt", s_[:, W:WT]), 0)
-    ms(ap("SV", s_[:, :, H:136]), 0.0)
-    ms(ap("flag"), 0.0)
+    iota(ap("tmi", s_[:, 0]), [[-1, 128]], 128, 1, False)
+    for i in range(4):
+        ms(Dm(i, W, WD), 0.0)
+    ms(ap("SV", s_[:, 2:8, H:136]), 0.0)
     ms(tmp(2), 0.5)
     for i, m in ((1, 112), (2, 15), (3, 16)):
         ts(coli(i), coli(0), m, ALU.bitwise_and)
@@ -179,38 +195,34 @@ def build():
     ts(MT(M_BO), tmp(0), col(C_G), ALU.is_equal)
     ts(MT(M_I), IO128, col(C_P), ALU.is_equal)
     ts(ap("Z1"), ap("IO", s_[:, 0:144]), col(C_G15), ALU.is_equal)
-    ts(ap("ZV"), ap("Z1"), -KK, ALU.mult)
-    for m, c in ((M_NI, -1.0), (M_SG, 4.5 * K), (M_TAU, -4.5 * K), (M_R, -KK)):
+    sc(ap("ZP"), ap("Z1"), KP)
+    sc(ap("ZQ"), ap("Z1"), KQ)
+    for m, c in ((M_NI, -1.0), (M_SP, -4.5 * KP), (M_SQ, -4.5 * KQ), (M_N2, -2.0), (M_R, -2.0 ** 20)):
         sc(MT(m), MT(M_I), c)
-    for i in range(16):
-        if i % 2:
-            sc(ap("BI", s_[:, i, :]), MT(M_BO), OH(i))
-        else:
-            ts(ap("BI", s_[:, i, :]), MT(M_BO), OH(i), ALU.mult)
     sc(ap("B0f"), MT(M_BO), OH(0))
-    ts(tmp(3), tmp(1), 0.0, ALU.is_equal, 2.0, ALU.mult)
+    ts(tmp(3), IO128, 0.0, ALU.is_equal, 2.0 ** 63, ALU.mult)
+    ts(ap("flag"), tmp(1), 0.0, ALU.is_equal, 8192.0, ALU.mult)
     scan(tmp(4), tmp(2), tmp(3), ALU.mult, ALU.max)
     tt(ap("tmp", s_[:, 5, 0:16]), ap("tmp", s_[:, 4, 0:16]), ap("OH"), ALU.mult)
     op("V", "tensor_reduce", [col(C_PW)], [col(C_PW), ap("tmp", s_[:, 5, 0:16]), AxisListType.X, ALU.add])
-    ts(col(C_BIG), col(C_R), 13.0, ALU.is_ge, 65536.0, ALU.mult)
-    ts(ap("thr"), tmp(4), col(C_BIG), ALU.max)
-    sc(MT(M_W4), MT(M_BO), 4.0)
-    ts(MT(M_WD), MT(M_BO), col(C_PW), ALU.mult, 0.5, ALU.mult)
-    ts(col(C_T0), OH(0), 4.5 * K, ALU.mult)
-    ts(col(C_LP), OH(15), -0.5 * K, ALU.mult, col(C_T0), ALU.add)
-    ts(col(C_C), OH(15), 192.0 / 65536, ALU.mult)
-    sc(MT(M_LP), MT(M_BO), col(C_LP))
-    sc(MT(M_C), MT(M_BO), col(C_C))
-    ts(col(C_T1), OH(0), -256 * K, ALU.mult)
-    ts(col(C_T2), OH(15), 256 * K, ALU.mult, col(C_T1), ALU.add)
-    ts(col(C_LQ), OH(14), -0.5 * K, ALU.mult, col(C_T2), ALU.add)
-    sc(MT(M_LQ), MT(M_BO), col(C_LQ))
+    ts(col(C_BIG), col(C_R), 13.0, ALU.is_ge, BIG, ALU.mult)
+    ts(ap("thr"), tmp(4), 2.5, ALU.mult, col(C_BIG), ALU.max)
+    ts(ap("PW"), ap("tmp", s_[:, 4, 0::16]), col(C_PW), ALU.mult, 2.0 ** -63, ALU.mult)
+    ts(col(C_T0), OH(0), -4.5 * KP, ALU.mult)
+    ts(col(C_LP), OH(15), 0.5 * KP, ALU.mult, col(C_T0), ALU.add)
+    ts(col(C_T1), OH(0), 8.5 * KQ, ALU.mult)
+    ts(col(C_LQ), OH(15), -12.0 * KQ, ALU.mult, col(C_T1), ALU.add)
+    ts(col(C_C3), OH(14), -5120.0 / 2.0 ** 20 / BIG, ALU.mult)
+    ts(col(C_C), OH(15), 192.0 / BIG, ALU.mult, col(C_C3), ALU.add)
+    for m, c in ((M_LP, C_LP), (M_LQ, C_LQ), (M_C, C_C)):
+        sc(MT(m), MT(M_BO), col(c))
+    ts(MT(M_C3), MT(M_BO), col(C_C3), ALU.mult, -2.0 ** 20, ALU.mult)
     ts(col(C_T4), OH(0), -1024.0, ALU.mult)
     ts(col(C_A1), OH(15), 1024.0, ALU.mult, col(C_T4), ALU.add)
     ts(col(C_A2), OH(15), -1024.0, ALU.mult, col(C_T4), ALU.add)
-    sc(MT(18), ZW("Z1", 1), col(C_A1))
-    sc(MT(19), ZW("Z1", 2), col(C_A2))
-    tt(MT(M_LA), MT(18), MT(19), ALU.add)
+    sc(tmp(2), ZW("Z1", 1), col(C_A1))
+    sc(tmp(5), ZW("Z1", 2), col(C_A2))
+    tt(MT(M_LA), tmp(2), tmp(5), ALU.add)
     sc(MT(M_LJ), ZW("Z1", 2), OH(0))
     sc(MT(M_LH), ZW("Z1", 0), col(C_W))
     sc(MT(M_T00), MT(M_I), col(C_H0))
@@ -219,23 +231,24 @@ def build():
     ts(MT(M_T01), IO128, col(C_M16), ALU.is_equal, col(C_H1), ALU.mult)
     TM = {(0, 0): M_T00, (0, 1): M_T01, (1, 0): M_T10, (1, 1): M_T11}
     ts(ap("dump"), ap("dump"), col(C_R), ALU.add)
-    cp(ap("RL"), IO128)
     ts(col(C_U), col(C_A), 2.0, ALU.mult, -1.0, ALU.add)
+    ts(ap("tmi", s_[:, 1]), ap("tmi", s_[:, 0]), 15, ALU.bitwise_and)
+    tt(ap("ZB"), ap("tmi", s_[:, 1]), MT(M_BO), ALU.mult)
+    for i in range(1, 16):
+        ts(RS(i), ap("ZB"), float(i), ALU.is_equal)
+        op("G", "affine_select", [RS(i)], [RS(i), RS(i), [[-1, 128]], ALU.not_equal, 1.0, 0, 1], cost=205 + 2 * 128, after=[RS(i)])
 
     def scales(s, u):
         op("V", "reciprocal", [thc(s, 1)], [thc(s, 1), u], cost=240)
-        ts(thc(s, 2), u, 1.0, ALU.min, 192.0, ALU.mult)
-        ts(thc(s, 4), thc(s, 2), -BETA, ALU.mult, -6.9305, ALU.add)
-        a = 800 if s == 0 else 0
-        if a:
-            ts(ap("Ds", s_[:, 0, 0:a]), ap("Dm", s_[:, 0:a]), thc(s, 1), ALU.mult)
-        sc(ap("Ds", s_[:, s % 2, a:WD]), ap("Dm", s_[:, a:WD]), thc(s, 1))
+        ts(thc(s, 2), u, 1.0, ALU.min, MAGIC, ALU.mult)
+        ts(ap("cd", s_[:, s, 0]), MT(M_I), thc(s, 1), ALU.mult)
+        ts(ap("cd", s_[:, s, 1]), MT(M_I), thc(s, 1), ALU.mult, -1.0, ALU.mult)
 
     scales(0, col(C_U))
     for c in range(2):
-        cp(ap("SU", s_[:, c, H:136]), ap("jin", s_[:, 8 * c:8 * c + 8]))
+        cp(ap("SU", s_[:, c, 0:8]), ap("jin", s_[:, 8 * c:8 * c + 8]))
         cp(ap("JT", s_[:, c, :]), ap("jin", s_[:, 8 * c:8 * c + 8]))
-        cp(ap("SU", s_[:, c, 0:H]), ap("qin", s_[:, H * c:H * c + H]))
+        cp(ap("SU", s_[:, c, 8:136]), ap("qin", s_[:, H * c:H * c + H]))
 
     def tolist(bank, rhs_of, nq):
         for u in range(2):
@@ -243,59 +256,71 @@ def build():
             for h in range(2):
                 mm(ap(bank, s_[:, u:8 * nq:2]), MT(TM[(h, u)]), rhs_of(h), gq, first=(h == 0))
 
-    def absdiff(out, lst, Dw, u_, v, buf):
-        act(buf, ind(Dw, lst), AF.Identity, scale=u_)
+    def absdiff(out, d, v):
         gq, o = newg(), ap(bank_(), s_[:, 0:H])
         mm(o, MT(M_NI), v, gq, first=True)
-        mm(o, MT(M_I), buf, gq)
+        mm(o, MT(M_I), d, gq)
         act(out, o, AF.Abs)
 
     mv = 0
-    src = [("SU", "SV", 0), ("SU", "SV", 1)]
+    src = [("SU", "SV", "SX", 0), ("SU", "SV", "SX", 1)]
     for s in range(4):
         last = s == 3
-        Dw = ap("Ds", s_[:, s % 2, :])
-        u_ = thc(s, 0) if s else col(C_U)
+        Dw = Dm(s, 0, WD)
         nsrc, late = [], []
         for c in range(2):
-            un, vn, sl = src[c]
+            un, vn, xn, sl = src[c]
             jt, so = 2 * s + c, 2 * (s + 1) + c
-            ph[0] = jt
-            Qu, Ju, v = ap(un, s_[:, sl, 0:H]), ap(un, s_[:, sl, H:136]), ap(vn, s_[:, sl, 0:H])
+            ph[0], ph[1] = jt, 0
+            Qu, Ju, v = ap(un, s_[:, sl, 8:136]), ap(un, s_[:, sl, 0:8]), ap(vn, s_[:, sl, 0:H])
+            early = EARLY and s
             if un == "LU":
-                op("X", "arrive", [ap("LU", s_[:, sl, :]), ap("LV", s_[:, sl, :])], [], extra=("arr", sl))
+                for kind in ("x", "u") if EARLY else ("u",):
+                    arrive(kind, sl)
                 cp(ap("JT", s_[:, jt, :]), Ju)
-            pP, pQ = ap("pP%d" % c, s_[:, 0:H]), ap("pQ%d" % c, s_[:, 0:H])
-            aP, aQ = ap("pP%d" % c, s_[:, H:2 * H]), ap("pQ%d" % c, s_[:, H:2 * H])
-            P16, Q16, Jb = ap("PQ", s_[:, c, 0, :]), ap("PQ", s_[:, c, 1, :]), ap("Jb", s_[:, c, :])
+            if s and not c:
+                dma("Y", Dm(s + 1), Dm(s), 128 * 3200, after=[Ju] if un == "LU" else [])
+            pP, pX, p3 = (ap("pP%d" % c, s_[:, H * i:H * i + H]) for i in range(3))
+            pQ, aQ = ap("pQ%d" % c, s_[:, 0:H]), ap("pQ%d" % c, s_[:, H:2 * H])
+            if FIX1:
+                pQ = aQ = ap("pP%d" % c, s_[:, 3 * H:4 * H])
+            NP, Q16, Jb = ap("PQ", s_[:, c, 0, :]), ap("PQ", s_[:, c, 1, :]), ap("Jb", s_[:, c, :])
             Pu, actb = ap("Pu", s_[:, c, :]), ap("act", s_[:, c, :])
             cp(Q16, Qu)
             cp(Jb, ind(ap("IOT"), Ju))
             cp(Pu, ind(ap("Pt", s_[:, 0:W]), Ju))
-            cp(P16, Pu)
+            ts(NP, Pu, -1.0, ALU.mult)
             for f in late:
                 f()
             late = []
+            if early:
+                act(ap("GJ", s_[:, c, 1, 0:H]), ind(Dw, Ju), AF.Identity)
+            ph[1] = 1
+            for l0 in range(0, H, PA):
+                a = l0 + 8 if l0 or early else 0
+                lst = ap(xn, s_[:, sl, l0:l0 + PA]) if early else ap(un, s_[:, sl, a:l0 + PA + 8])
+                act(ap("GJ", s_[:, c, 1, 16 * a:16 * (l0 + PA + 8)]), ind(Dw, lst), AF.Identity)
+            for l0 in range(0, H, PA):
+                act(ap("GJ", s_[:, c, 0, 16 * (8 + l0):16 * (8 + l0 + PA)]), ind(Dw, ap("Pu", s_[:, c, l0:l0 + PA])), AF.Identity)
+            ph[1] = 0
             pM = bank_()
-            for b in range(8):
-                ts(ap("E", s_[:, c, b, 0:H - 16 * b]), ap("Jb", s_[:, c, 16 * b:H]), ap("JT", s_[:, jt, b:b + 1]), ALU.is_equal)
             gq = newg()
             mm(ap(pM, s_[:, 0:H]), MT(M_NI), ap("thr"), gq, first=True)
             for b in range(8):
-                mm(ap(pM, s_[:, 16 * b:16 * b + 16]), MT(M_WD), ap("E", s_[:, c, b, 0:16]), gq)
-            for b in range(7):
-                mm(ap(pM, s_[:, 16 * b + 16:H]), MT(M_W4), ap("E", s_[:, c, b, 16:H - 16 * b]), gq)
+                e = ap("E", s_[:, c, b, 0:H - 16 * b])
+                ts(e, ap("Jb", s_[:, c, 16 * b:H]), ap("JT", s_[:, jt, b:b + 1]), ALU.is_equal, ap("PW", s_[:, b:b + 1]), ALU.mult)
+                mm(ap(pM, s_[:, 16 * b:H]), MT(M_BO), e, gq)
             for b in range(8 * c):
-                ts(ap("E2", s_[:, b, :]), Jb, ap("JT", s_[:, jt - 1, b:b + 1]), ALU.is_equal)
-                mm(ap(pM, s_[:, 0:H]), MT(M_W4), ap("E2", s_[:, b, :]), gq)
-            act(actb, ap(pM, s_[:, 0:H]), AF.Sign, bias=-2.0 ** -16, scale=-1.0, acc=None if last else col(C_ACC + c))
+                ts(ap("E2", s_[:, b, :]), Jb, ap("JT", s_[:, jt - 1, b:b + 1]), ALU.is_equal, 2.0 ** 64, ALU.mult)
+                mm(ap(pM, s_[:, 0:H]), MT(M_BO), ap("E2", s_[:, b, :]), gq)
+            act(actb, ap(pM, s_[:, 0:H]), AF.Sign, scale=-1.0, acc=None if last else col(C_ACC + c))
             pM = bank_()
-            for t, x in ((1, Q16), (0, P16)):
+            for t, m, x in ((1, M_I, Q16), (0, M_NI, NP)):
                 gq = newg()
                 mm(ap(pM, s_[:, H * t:H * t + H]), MT(M_NI), Jb, gq, first=True)
-                mm(ap(pM, s_[:, H * t:H * t + H]), MT(M_I), x, gq)
+                mm(ap(pM, s_[:, H * t:H * t + H]), MT(m), x, gq)
             act(ap("sg", s_[:, c]), ap(pM, s_[:, 0:2 * H]), AF.Sign, bias=-0.5)
-            absdiff(ap("nd", s_[:, c, :]), Ju, Dw, u_, v, ap("Dj", s_[:, c, 0, :]))
+            absdiff(ap("nd", s_[:, c, :]), ap("GJ", s_[:, c, 1, 0:H]), v)
             gq, o = newg(), ap(bank_(), s_[:, 0:H])
             mm(o, MT(M_LH), v, gq, first=True)
             mm(o, MT(M_LJ), Jb, gq)
@@ -304,16 +329,16 @@ def build():
             cp(ap("tM", s_[:, c]), ap("XT", s_[:, c, 2::16]))
             cp(ap("hi", s_[:, c, 0]), ap("XT", s_[:, c, 0::16]))
             ts(ap("hi", s_[:, c, 1]), ap("hi", s_[:, c, 0]), 1023, ALU.bitwise_and)
-            tt(ap("flag", s_[:, c, 0::16]), ap("hi", s_[:, c, 1]), ap("seg"), ALU.add)
+            ts(ap("hh", s_[:, c]), ap("hi", s_[:, c, 1]), 2048.0, ALU.add)
             pM = bank_()
             tolist(pM, lambda h: ap("tM", s_[:, c, h::2]), 1)
             tt(ap("sc1", s_[:, c, :]), ap(pM, s_[:, 0:8]), ap("dump", s_[:, 8 * c:8 * c + 8]), ALU.min)
             act(ap("jm", s_[:, c, :]), ap(pM, s_[:, 0:8]), AF.Identity)
             scu = ap("scu", s_[:, c, :])
             ts(scu, ap("sc1", s_[:, c, :]), 2048.0, ALU.add)
-            cp(ind(ap("Dm"), scu), ap("nd", s_[:, c, :]))
+            cp(ind(Dm(s + 1, 0, WT), scu), ap("nd", s_[:, c, :]))
             if c == 1 and last:
-                dma("Y", ap("yd"), ap("Dm", s_[:, 0:W]), 128 * 3200)
+                dma("Y", ap("yd"), Dm(4), 128 * 3200)
             elif c == 1:
                 gq, o = newg(), ap(bank_(), s_[:, 0:1])
                 mm(o, ap("B0f"), col(C_ACC), gq, first=True, f=4.0)
@@ -322,82 +347,97 @@ def build():
                 ts(ap("thi", s_[:, s, 1:2]), ap("thi", s_[:, s, 0:1]), 3, ALU.bitwise_and)
                 ts(thc(s + 1, 0), ap("thi", s_[:, s, 1:2]), 2.0, ALU.mult, col(C_U), ALU.add)
                 scales(s + 1, thc(s + 1, 0))
-            g1 = newg()
-            mm(aQ, MT(M_C), ap("thr"), g1, first=True)
-            for k in range(4):
-                sb, bank = new(3) % 4, bank_()
-                for i in range(4):
-                    gq, o = newg(), ap(bank, s_[:, H * i:H * i + H])
-                    mm(o, ap("BI", s_[:, 4 * k + i, :]), Q16, gq, first=True)
-                    mm(o, MT(M_NI), P16, gq)
-                act(ap("sig", s_[:, sb]), ap(bank), AF.Sigmoid, bias=-4.125, scale=128.0)
-                for i in range(4):
-                    mm(aQ, ZW("Z1", 4 * k + i), ap("sig", s_[:, sb, H * i:H * i + H]), g1)
-            for l0 in range(0, VS, 32):
-                act(ap("vr", s_[:, c, 16 * l0:16 * l0 + 512]), ind(v, ap("RL", s_[:, l0:l0 + 32])), AF.Identity, bias=-192.0, scale=thc(s, 1))
-            if VS < H:
-                x = ap("v1", s_[:, c, VS:H])
-                act(x, ap(vn, s_[:, sl, VS:H]), AF.Identity, bias=-192.0, scale=thc(s, 1))
-                for i in range(16):
-                    o = ap("vr", s_[:, c, 16 * VS + i::16])
-                    op("G", "affine_select", [o], [o, x, [[0, H - VS]], ALU.is_ge, 0.0, 0, 0], cost=205 + 2 * (H - VS))
-            sp = SP[jt]
-            gP, gP2, gQ = newg(), newg(), newg()
-            if sp:
-                mm(aP, MT(M_C), ap("thr"), gP, first=True)
+            ph[1] = 1
+            for t, pb, z, msg, ml in ((1, pQ, "ZQ", M_SQ, M_LQ), (0, pP, "ZP", M_SP, M_LP)):
+                for l0 in range(0, H, 64):
+                    for h in range(2):
+                        bank, gq = bank_(), newg()
+                        mm(ap(bank), ap("cd", s_[:, s, 0]), ap("GJ", s_[:, c, t, 16 * (8 + l0) + h:16 * (72 + l0):2]), gq, first=True)
+                        for i in range(8):
+                            mm(ap(bank, s_[:, i::8]), ap("cd", s_[:, s, 1]), ap(vn, s_[:, sl, l0:l0 + 64]), gq)
+                        ts(ap("mk", s_[:, c, t, h, 8 * l0:8 * l0 + 512]), ap(bank), MAGIC, ALU.add, thc(s, 2), ALU.is_equal)
+                gb = newg()
+                mm(pb, MT(ml), actb, gb, first=True)
+                mm(pb, MT(msg), ap("sg", s_[:, c, H * t:H * t + H]), gb)
+                for l0 in range(0, H, SUMN):
+                    for i in range(16):
+                        x = pb[2][1].start + l0
+                        mm(ap(pb[1], s_[:, x:x + SUMN]), ZW(z, i), ap("mk", s_[:, c, t, i % 2, 8 * l0 + i // 2:8 * (l0 + SUMN):8]), gb)
+                if t:
+                    tt(ap("WQ", s_[:, c, :]), pQ, Q16, ALU.max)
+            X, Wa, ph[1] = ap("X", s_[:, c, :]), ap("Wa", s_[:, c, :]), 2
+            tt(pP, pP, NP, ALU.max)
+            tt(X, pP, ap("WQ", s_[:, c, :]), ALU.min)
+            mm(pX, MT(M_NI), X, newg(), first=True)
+            if VABS:
+                tt(Wa, pX, X, ALU.max)
             else:
-                mm(pP, MT(M_SG), ap("sg", s_[:, c, 0:H]), gP2, first=True)
-            for t, ln, ls, pa, pb, ga, gb, ns in ((1, un, sl, aQ, pQ, g1, gQ, H), (0, "Pu", c, aP, pP, gP, gP2, sp)):
-                for l0 in range(0, H, PA):
-                    x = slice(16 * l0, 16 * (l0 + PA))
-                    y, o = ap("yy", s_[:, c, t, x]), ap("ia", s_[:, c, t, x])
-                    tt(y, ind(Dw, ap(ln, s_[:, ls, l0:l0 + PA])), ap("vr", s_[:, c, x]), ALU.subtract)
-                    if l0 < ns:
-                        act(o, y, AF.Sigmoid, bias=thc(s, 4), scale=BETA)
-                    else:
-                        ts(o, y, thc(s, 2), ALU.is_equal, 1.0 / 1024, ALU.mult)
-                for i in range(16):
-                    mm(pa if ns else pb, ZW("Z1" if ns else "ZV", i), ap("ia", s_[:, c, t, i::16]), ga if ns else gb)
-                if ns:
-                    act(ap("rr", s_[:, c, t, :]), pa, AF.Identity)
-                    tt(ap("fr", s_[:, c, t, :]), pa, ap("rr", s_[:, c, t, :]), ALU.subtract)
-                    mm(pb, MT(M_SG), ap("sg", s_[:, c, H * t:H * t + H]), gb, first=True)
-                    mm(pb, MT(M_R), ap("fr", s_[:, c, t, :]), gb)
-                mm(pb, MT(M_LQ if t else M_LP), actb, gb)
-            act(ap("tau", s_[:, c, :]), pP, AF.Sign)
-            mm(pQ, MT(M_TAU), ap("tau", s_[:, c, :]), gQ)
-            tt(pP, pP, P16, ALU.min)
-            tt(ap("WQ", s_[:, c, :]), pQ, Q16, ALU.min)
-            Ww = ap("Ww", s_[:, c, :])
-            tt(Ww, pP, ap("WQ", s_[:, c, :]), ALU.max)
+                act(Wa, pX, AF.Abs)
             if last:
-                act(ap("yqb", s_[:, c, :]), Ww, AF.Relu)
-                dma("Y", ap("yq", s_[:, H * c:H * c + H]), ap("yqb", s_[:, c, :]), 65536)
-            else:
-                late.append(lambda Ww=Ww, scu=scu: cp(ind(ap("Pt"), scu), Ww))
-                cp(ap("SU", s_[:, so, 0:H]), Ww)
-            act(ap("Wa", s_[:, c, :]), Ww, AF.Abs)
-            tr(ap("WTr", s_[:, c, :]), ap("Wa", s_[:, c, :]))
-            scan(ap("scn", s_[:, c]), ap("flag", s_[:, c]), ap("WTr", s_[:, c, :]), ALU.max, ALU.min)
-            ts(ap("fi", s_[:, c]), ap("scn", s_[:, c, 15::16]), 2047, ALU.bitwise_and)
-            tt(ap("fM", s_[:, c, 0:8]), ap("fi", s_[:, c]), ap("XT", s_[:, c, 1::16]), ALU.add)
-            tt(ap("fM", s_[:, c, 8:16]), ap("fi", s_[:, c]), ap("XT", s_[:, c, 1::16]), ALU.subtract)
+                act(ap("yqb", s_[:, c, 0]), pX, AF.Relu)
+            elif EARLY:
+                ts(ap("SX", s_[:, so]), Wa, float(W), ALU.min)
+                if HOP[s]:
+                    send("x", 2 * mv + c, so)
+            tr(ap("WTr", s_[:, c, :]), Wa)
+            scan(ap("scn", s_[:, c]), ap("flag"), ap("WTr", s_[:, c, :]), ALU.add, ALU.min)
+            tt(ap("fi", s_[:, c, 0]), ap("scn", s_[:, c, 15::16]), ap("hh", s_[:, c]), ALU.min)
+            ts(ap("fi", s_[:, c, 1]), ap("fi", s_[:, c, 0]), 2047, ALU.bitwise_and)
+            tt(ap("fM", s_[:, c, 0:8]), ap("fi", s_[:, c, 1]), ap("XT", s_[:, c, 1::16]), ALU.add)
+            tt(ap("fM", s_[:, c, 8:16]), ap("fi", s_[:, c, 1]), ap("XT", s_[:, c, 1::16]), ALU.subtract)
             pM = bank_()
             tolist(pM, lambda h: ap("fM", s_[:, c, h::2]), 2)
             fz = ap("fz", s_[:, c, :])
             ts(fz, ap(pM, s_[:, 0:8]), float(W), ALU.min)
             tt(ap("JT", s_[:, so, :]), ap(pM, s_[:, 8:16]), ap("jm", s_[:, c, :]), ALU.max)
-            cp(ap("SU", s_[:, so, H:136]), ap("JT", s_[:, so, :]))
-            absdiff(ap("SV", s_[:, so, 0:H]), fz, Dw, u_, v, ap("Dj", s_[:, c, 1, :]))
+            cp(ap("SU", s_[:, so, 0:8]), ap("JT", s_[:, so, :]))
+            if VDF:
+                tt(ap("Df", s_[:, c]), ind(Dw, fz), v, ALU.subtract)
+                act(ap("SV", s_[:, so, 0:H]), ap("Df", s_[:, c]), AF.Abs)
+            else:
+                act(ap("Df", s_[:, c]), ind(Dw, fz), AF.Identity)
+                absdiff(ap("SV", s_[:, so, 0:H]), ap("Df", s_[:, c]), v)
+            g1, g3 = newg(), newg()
+            if DV[jt]:
+                mm(p3, MT(M_C3), ap("thr"), g3, first=True)
+                mm(p3, MT(M_N2), X, g3)
+            else:
+                mm(aQ, MT(M_C), ap("thr"), g1, first=True)
+            for k in range(2):
+                bank = bank_()
+                for i in range(4):
+                    mm(ap(bank, s_[:, H * i:H * i + H]), RS(4 * k + i + 1), X, newg(), first=True)
+                o = ap("sig", s_[:, c, 512 * k:512 * k + 512])
+                if DV[jt]:
+                    ts(o, ap(bank), 0.0, ALU.is_equal, -8192.0, ALU.mult)
+                else:
+                    act(o, ap(bank), AF.Sigmoid, bias=-4.125, scale=128.0)
+                for i in range(4):
+                    x = 512 * k + H * i
+                    mm(p3 if DV[jt] else aQ, RS(15 - 4 * k - i), ap("sig", s_[:, c, x:x + H]), g3 if DV[jt] else g1)
+            if not DV[jt]:
+                act(ap("rr", s_[:, c, :]), aQ, AF.Identity)
+                tt(ap("fr", s_[:, c, :]), aQ, ap("rr", s_[:, c, :]), ALU.subtract)
+                mm(p3, MT(M_N2), X, g3, first=True)
+                mm(p3, MT(M_R), ap("fr", s_[:, c, :]), g3)
             if last:
-                act(ap("yjb", s_[:, c, :]), ind(ap("IOT"), ap("SU", s_[:, so, H:136])), AF.Identity)
+                tt(p3, p3, X, ALU.min)
+                tt(ap("yqb", s_[:, c, 1]), p3, ap("yqb", s_[:, c, 0]), ALU.max)
+                dma("Y", ap("yq", s_[:, H * c:H * c + H]), ap("yqb", s_[:, c, 1]), 65536)
+                act(ap("yjb", s_[:, c, :]), ind(ap("IOT"), ap("SU", s_[:, so, 0:8])), AF.Identity)
                 dma("Y", ap("yv", s_[:, H * c:H * c + H]), ap("SV", s_[:, so, 0:H]), 32768)
                 dma("Y", ap("yj", s_[:, H * c:H * c + H]), ap("yjb", s_[0:128:16, c, :]), 4096)
-            if HOP[s]:
-                op("G", "send", [], [None, ap("SU", s_[:, so, :]), ap("SV", s_[:, so, :])], cost=300.0, extra=("send", 2 * mv + c, so))
-                nsrc.append(("LU", "LV", 2 * mv + c))
             else:
-                nsrc.append(("SU", "SV", so))
+                U = ap("U", s_[:, c, :])
+                tt(ap("Ut", s_[:, c, :]), p3, X, ALU.min)
+                tt(U, pX, ap("Ut", s_[:, c, :]), ALU.max)
+                cp(ap("SU", s_[:, so, 8:136]), U)
+                late.append(lambda U=U, scu=scu: cp(ind(ap("Pt"), scu), U))
+            if HOP[s]:
+                send("u", 2 * mv + c, so)
+                nsrc.append(("LU", "LV", "LX", 2 * mv + c))
+            else:
+                nsrc.append(("SU", "SV", "SX", so))
         for f in late:
             f()
         mv += 1 if HOP[s] else 0
@@ -439,6 +479,15 @@ def depend(ops):
         for k in lst[1:]:
             deps[lst[0]] |= {j for j in deps[k] - inside if j < lst[0]}
             deps[k].add(lst[0])
+    anc = []
+    for k, d in enumerate(deps):
+        m = 0
+        for j in d:
+            m |= anc[j]
+        deps[k] = {j for j in d if not m >> j & 1 or ops[j]["extra"]}
+        for j in d:
+            m |= 1 << j
+        anc.append(0 if ops[k]["meth"] in ("arrive", "send") else m)
     return deps, sess
 
 
@@ -446,115 +495,133 @@ def latency(o):
     return o["extra"][2] if o["meth"] == "dma_start" else COMM if o["meth"] == "arrive" else o["cost"]
 
 
-def gap(ops, j, e):
-    return (0.0 if e == "T" else 40.0) if ops[j]["eng"] == e else SYNC
-
-
-def schedule(ops, deps0, sess, seed, key=None):
+def graph(ops, deps, sess):
     n = len(ops)
-    deps = [set(d) for d in deps0]
-    rng = np.random.default_rng(seed)
+    eng = [o["eng"] for o in ops]
     succ = [[] for _ in range(n)]
     for k in range(n):
         for j in deps[k]:
-            succ[j].append(k)
-    if key is None:
-        pr = [0.0] * n
-        for k in range(n - 1, -1, -1):
-            pr[k] = latency(ops[k]) + max([pr[m] + gap(ops, m, ops[k]["eng"]) for m in succ[k]] + [0.0])
-        phw, amp = PH * float(rng.uniform(0.3, 2.0)), float(rng.uniform(0, 600))
-        key = [pr[k] - phw * ops[k]["ph"] + amp * float(x) for k, x in enumerate(rng.random(n))]
-    left = [len(d) for d in deps]
-    ready_t, done_t, isdone = [0.0] * n, [0.0] * n, [False] * n
+            succ[j].append((k, (0.0 if eng[k] == "T" else SAME) if eng[j] == eng[k] else SYNC))
+    return dict(n=n, eng=eng, succ=succ, lat=[latency(o) for o in ops], busy=[o["cost"] if o["eng"] != "X" else 0.0 for o in ops],
+                nd=[len(d) for d in deps], bank=[o["bank"] for o in ops], sess=sess,
+                opens=[bool(o["bank"]) and sess[o["bank"]][0] == k for k, o in enumerate(ops)],
+                slack=[SL2 if o["cls"] == 2 else SLACK for o in ops],
+                pred=[[(j, (0.0 if eng[k] == "T" else SAME) if eng[j] == eng[k] else SYNC) for j in deps[k]] for k in range(n)])
+
+
+def schedule(gr, key):
+    n, eng, succ, lat, busy, bank, sess, opens, slack = (gr[x] for x in "n eng succ lat busy bank sess opens slack".split())
+    left = list(gr["nd"])
+    ready_t, done_t = [0.0] * n, [0.0] * n
     free = {e: 0.0 for e in ENG + ("X",)}
-    ready = {e: [k for k in range(n) if not left[k] and ops[k]["eng"] == e] for e in free}
-    holder = {b: [] for b in POOL}
-    order, banks, start = [], {}, [0.0] * n
-    opens = [bool(o["bank"]) and sess[o["bank"]][0] == k for k, o in enumerate(ops)]
+    ready = {e: [k for k in range(n) if not left[k] and eng[k] == e] for e in free}
+    fbank = [(0.0, b) for b in POOL]
+    held, heldt, banks, prev, lastof = {}, {}, {}, {}, {}
+    order, start, cand = [], [0.0] * n, {}
+    dirty = set(free)
     while len(order) < n:
-        best = None
-        fb = [(max([done_t[j] for j in h] + [0.0]), b) for b, h in holder.items() if all(isdone[j] for j in h)]
-        fb = min(fb) if fb else None
-        for e, lst in ready.items():
-            rt = {k: max(ready_t[k], fb[0] + SYNC) if opens[k] else ready_t[k] for k in lst if fb or not opens[k]}
-            if rt:
-                t0 = max(free[e], min(rt.values()))
-                k = max((k for k in rt if rt[k] <= t0 + SLACK), key=lambda k: (key[k], -k))
-                t = max(free[e], rt[k])
-                if best is None or t < best[0]:
-                    best = (t, e, k)
-        t, e, k = best
+        fb = min(fbank) if fbank else None
+        for e in dirty:
+            lst = [(max(ready_t[k], fb[0] + SYNC) if opens[k] else ready_t[k], k) for k in ready[e] if fb or not opens[k]]
+            if lst:
+                t0 = max(free[e], min(lst)[0])
+                _, k, r = max((key[k], k, r) for r, k in lst if r <= t0 + slack[k])
+                cand[e] = (max(free[e], r), e, k)
+            else:
+                cand.pop(e, None)
+        t, e, k = min(cand.values())
+        dirty = {e}
         ready[e].remove(k)
         order.append(k)
-        isdone[k] = True
-        if opens[k]:
-            deps[k] |= set(holder[fb[1]])
-            holder[fb[1]] = sess[ops[k]["bank"]]
-            banks[ops[k]["bank"]] = fb[1]
-        free[e] = t + (ops[k]["cost"] if e != "X" else 0.0)
-        done_t[k] = t + latency(ops[k])
+        free[e] = t + busy[k]
+        d = done_t[k] = t + lat[k]
         start[k] = t
-        for m in succ[k]:
-            ready_t[m] = max(ready_t[m], done_t[k] + gap(ops, m, e))
+        b = bank[k]
+        if b:
+            if opens[k]:
+                fbank.remove(fb)
+                banks[b], held[b], heldt[b] = fb[1], len(sess[b]), 0.0
+                prev[k] = lastof.get(fb[1], ())
+                lastof[fb[1]] = sess[b]
+            held[b] -= 1
+            heldt[b] = max(heldt[b], d)
+            if not held[b]:
+                fbank.append((heldt[b], banks[b]))
+                dirty.add("T")
+        for m, gp in succ[k]:
+            if d + gp > ready_t[m]:
+                ready_t[m] = d + gp
             left[m] -= 1
             if not left[m]:
-                ready[ops[m]["eng"]].append(m)
-    return max(done_t), order, deps, banks, start
+                ready[eng[m]].append(m)
+                dirty.add(eng[m])
+    return max(done_t), order, prev, banks, start
 
 
-def backward(ops, deps, start):
-    n = len(ops)
-    left = [0] * n
-    for d in deps:
-        for j in d:
-            left[j] += 1
-    end = [start[k] + latency(ops[k]) for k in range(n)]
-    busy = [o["cost"] if o["eng"] != "X" else 0.0 for o in ops]
-    ready = {e: [k for k in range(n) if not left[k] and ops[k]["eng"] == e] for e in ENG + ("X",)}
-    free = {e: 0.0 for e in ready}
-    rt, out = [0.0] * n, [0.0] * n
+def backward(gr, start):
+    n, eng, pred, lat, busy = (gr[x] for x in "n eng pred lat busy".split())
+    left = [len(x) for x in gr["succ"]]
+    end = [start[k] + lat[k] for k in range(n)]
+    free = {e: 0.0 for e in ENG + ("X",)}
+    ready = {e: [k for k in range(n) if not left[k] and eng[k] == e] for e in free}
+    rt, out, cand = [0.0] * n, [0.0] * n, {}
+    dirty = set(free)
     for _ in range(n):
-        best = None
-        for e, lst in ready.items():
+        for e in dirty:
+            lst = ready[e]
             if lst:
                 t0 = max(free[e], min(rt[k] for k in lst))
-                k = max((k for k in lst if rt[k] <= t0 + SLACK), key=lambda k: end[k])
-                t = max(free[e], rt[k])
-                if best is None or t < best[0]:
-                    best = (t, e, k)
-        t, e, k = best
+                _, k = max((end[k], k) for k in lst if rt[k] <= t0 + SLACK)
+                cand[e] = (max(free[e], rt[k]), e, k)
+            else:
+                cand.pop(e, None)
+        t, e, k = min(cand.values())
+        dirty = {e}
         ready[e].remove(k)
         free[e] = out[k] = t + busy[k]
-        for j in deps[k]:
-            rt[j] = max(rt[j], out[k] + latency(ops[j]) - busy[j] + gap(ops, j, e))
+        for j, gp in pred[k]:
+            rt[j] = max(rt[j], out[k] + lat[j] - busy[j] + gp)
             left[j] -= 1
             if not left[j]:
-                ready[ops[j]["eng"]].append(j)
+                ready[eng[j]].append(j)
+                dirty.add(eng[j])
     return out
+
+
+def search(ops, gr):
+    n = gr["n"]
+    pr = [0.0] * n
+    for k in range(n - 1, -1, -1):
+        pr[k] = gr["lat"][k] + max([pr[m] + g for m, g in gr["succ"][k] if ops[m]["ph"] == ops[k]["ph"]] + [0.0])
+    best = None
+    for w0, w2 in ((1.5, 2.5), (0.5, 2.5), (0.9, 0.9), (0.0, 0.0)):
+        r = schedule(gr, [0.3 * pr[k] + PH * ((w0, 0.0, w2)[o["cls"]] - o["ph"]) - k * 1e-3 for k, o in enumerate(ops)])
+        for x in range(ROUNDS + 1):
+            if best is None or r[0] < best[0]:
+                best = r
+            r = schedule(gr, backward(gr, r[4]))
+    rng, cur = np.random.default_rng(1), best
+    cl = [o["eng"] + (o["wr"][0][0] if o["wr"] and not o["bank"] else "") + str(o["ph"]) for o in ops]
+    c2 = ["%d.%d" % (o["ph"], o["cls"]) for o in ops]
+    names, name2 = sorted(set(cl)), sorted(set(c2))
+    for i in range(MORE):
+        off = {names[int(x)]: float(rng.normal() * 2000) for x in rng.integers(0, len(names), 4)}
+        off[name2[int(rng.integers(0, len(name2)))]] = float(rng.normal() * 2000)
+        base = [-x for x in cur[4]] if i % 2 else backward(gr, cur[4])
+        r = schedule(gr, [x + off.get(c, 0.0) + off.get(d, 0.0) for x, c, d in zip(base, cl, c2)])
+        if r[0] < cur[0] + 200:
+            cur = r
+        if r[0] < best[0]:
+            best = r
+    return best
 
 
 def program():
     ops = build()
-    deps0, sess = depend(ops)
-    best = None
-    for i in range(TRIES):
-        r = schedule(ops, deps0, sess, i)
-        for x in range(ROUNDS):
-            r = schedule(ops, deps0, sess, 0, backward(ops, deps0, r[4]))
-            if best is None or r[0] < best[0]:
-                best = r
-    rng, cur = np.random.default_rng(1), best
-    cl = [o["eng"] + (o["wr"][0][0] if o["wr"] and not o["bank"] else "") + str(o["ph"]) for o in ops]
-    names = sorted(set(cl))
-    for i in range(MORE):
-        off = {names[int(x)]: float(rng.normal() * 2500) for x in rng.integers(0, len(names), 6)}
-        base = [-x for x in cur[4]] if i % 2 else backward(ops, deps0, cur[4])
-        r = schedule(ops, deps0, sess, 0, [x + off.get(c, 0.0) for x, c in zip(base, cl)])
-        if r[0] < cur[0] + 150:
-            cur = r
-        if r[0] < best[0]:
-            best = r
-    total, order, deps, banks, start = best
+    deps, sess = depend(ops)
+    total, order, prev, banks, start = search(ops, graph(ops, deps, sess))
+    for k, x in prev.items():
+        deps[k] |= set(x)
     order = list(range(NLOAD)) + [k for k in order if k >= NLOAD and ops[k]["eng"] != "X"]
     pos = {k: i for i, k in enumerate(order)}
     pos.update({k: 0 for k, o in enumerate(ops) if o["eng"] == "X"})
@@ -582,7 +649,7 @@ def program():
         if k in marks and not o["extra"]:
             cnt[o["eng"]] += 1
             val[k] = cnt[o["eng"]]
-        w = [("e" + key, val[j]) if key in ENG else ("dm%d" % key[1], 16) if key[0] == "dma" else ("arr%d" % key[1], None)
+        w = [("e" + key, val[j]) if key in ENG else ("dm%d" % key[1], 16) if key[0] == "dma" else ("arr" + key[1], None)
              for key, j in waits[k]]
         tail = [o["first"], lastg[o["grp"]] == k] if o["meth"] == "matmul" else []
         out.append((o, w, tail, k in val))
@@ -600,28 +667,18 @@ def res(T, banks, a):
     return T[banks.get(a[1], a[1])][a[2] if len(a[2]) > 1 else a[2][0]]
 
 
-def halves(topo, a, b):
+def share(topo, a, b, k, n):
     e = topo.engines(a, b)
-    h = len(e) // 2
-    return sum(1 << x for x in e[:h]), sum(1 << x for x in e[h:]), h
+    h = len(e) // n
+    return sum(1 << x for x in e[h * k:h * k + h]), h
 
 
-def relay_of(T, topo, core):
+def relays_of(T, topo, core):
     r = T.rank_of(core)
     dsts = [T.cores[(r + h) % len(T.cores)] for h in HOP if h]
     c = [x for x in topo.cores_of(core) if T.rank_of(x) is None and all(topo.may_write(x, d) for d in dsts)]
     c.sort(key=lambda x: topo.die(x) != topo.die(core))
-    return c[0]
-
-
-def pair(g, T, topo, me, to, su, sv, slot, sem, local):
-    rid, pid = topo.addr(to, me)
-    m0, m1, h = halves(topo, me, to)
-    d = [DstId(rid=rid, pnc=pid)]
-    g.remote_dma_fused([
-        RemoteDMATransfer(dst_ids=d, dma_engine_mask=m0, remote_sem=sem, src=su, dst=T.LU[:, slot, 0:136]),
-        RemoteDMATransfer(dst_ids=d, dma_engine_mask=m1, remote_sem=sem, src=sv, dst=T.LV[:, slot, 0:136])], local_sem=local)
-    return 2 * h
+    return c[:2]
 
 
 def call(e, m, args, kw):
@@ -646,30 +703,44 @@ def rank_program(g, core, T, topo):
     hops = [h for h in HOP if h]
     if rank is None:
         for r, c in enumerate(T.cores):
-            if relay_of(T, topo, c) == core:
+            rl = relays_of(T, topo, c)
+            if core in rl:
                 tot = 0
-                for slot in range(4):
-                    g.wait_ge(T.sem["rel%d" % slot], 2 * halves(topo, c, core)[2])
-                    tot += pair(g, T, topo, core, T.cores[(r + hops[slot // 2]) % n], T.LU[:, slot, 0:136], T.LV[:, slot, 0:136],
-                                slot, T.sem["arr%d" % slot], T.sem.fwd)
+                for m in MSGS:
+                    parts, slot = PARTS[m[0]], int(m[1])
+                    to = T.cores[(r + hops[slot // 2]) % n]
+                    rid, pid = topo.addr(to, core)
+                    for k, (_, land, w, by) in enumerate(parts):
+                        if rl[by] == core:
+                            g.wait_ge(T.sem["rel" + m], share(topo, c, core, k, len(parts))[1])
+                            g.remote_dma(T[land][:, slot, 0:w], T[land][:, slot, 0:w], T.sem["arr" + m], T.sem.fwd, pid, rid,
+                                         topo.mask(core, to))
+                            tot += len(topo.engines(core, to))
                 g.wait_ge(T.sem.fwd, tot)
         return
     if not _prog:
         _prog.append(program())
     calls, banks = _prog[0][:2]
     q = {"V": g.vector, "S": g.scalar, "T": g.tensor, "G": g, "Y": g.sync}
-    relay = relay_of(T, topo, core)
+    rl = relays_of(T, topo, core)
     sent, dmas = 0, []
     for o, waits, tail, inc in calls:
         e, m = q[o["eng"]], o["meth"]
         for nm, val in waits:
             if val is None:
-                frm = T.cores[(rank - hops[int(nm[3:]) // 2]) % n]
-                val = 2 * halves(topo, relay_of(T, topo, frm), core)[2]
+                frm = relays_of(T, topo, T.cores[(rank - hops[int(nm[4]) // 2]) % n])
+                val = sum(len(topo.engines(frm[p[3]], core)) for p in PARTS[nm[3]])
             e.wait_ge(T.sem[nm], val)
         if m == "send":
-            _, slot, so = o["extra"]
-            sent += pair(g, T, topo, core, relay, T.SU[:, so, 0:136], T.SV[:, so, 0:136], slot, T.sem["rel%d" % slot], T.sem.sent)
+            _, msg, so = o["extra"]
+            parts, tr = PARTS[msg[0]], []
+            for k, (a, b, w, by) in enumerate(parts):
+                rid, pid = topo.addr(rl[by], core)
+                mask, h = share(topo, core, rl[by], k, len(parts))
+                tr.append(RemoteDMATransfer(dst_ids=[DstId(rid=rid, pnc=pid)], dma_engine_mask=mask, remote_sem=T.sem["rel" + msg],
+                                            src=T[a][:, so, 0:w], dst=T[b][:, int(msg[1]), 0:w]))
+                sent += h
+            g.remote_dma_fused(tr, local_sem=T.sem.sent)
             continue
         ins = call(e, m, [res(T, banks, a) for a in o["args"]] + tail, {k: res(T, banks, a) for k, a in o["kw"].items()})
         if m == "dma_start":

@@ -4,49 +4,59 @@ from concourse.mybir import AluOpType as ALU, AxisListType, ActivationFunctionTy
 
 W, L, H = 1600, 256, 128
 HOP = (1, 0, 3, 0)
-PA = 64
-SUMN = 128
-DV = (0, 0, 0, 0, 0, 0, 0, 1)
-EARLY = 1
-VDF = 0
+PA = (64, 64)
+BL = (64, 64)
+SUMN = (128, 128)
+MS = (512, 512)
+RATE = 190.0
+DV = (0, 1, 0, 0, 0, 1, 0, 1)
+s_ = np.s_
+VDF = 1
 VABS = 1
 FIX1 = 1
-KP, KQ = 6144.0, 3072.0
+KP, KQ = 6656.0, 3328.0
 MAGIC = 12582912.0
 BIG = 2.0 ** 75
 WT = 1872
 WD = 1608
-G_ = 1.56
-SC_ = 3.8
+G_ = 1.7
+SC_ = 4.4
 PEF = 0.5
-TOV = 8.0
-COMM = 6500.0
-SYNC = 150.0
-SAME = 100.0
+TOV = 4.0
+SEND = 500.0
+COMM = 7500.0
+SYNC = 230.0
+SAME = 230.0
 SLACK = 40.0
-SL2 = 110.0
+FILL = 40.0
+SL2 = 240.0
+VARS = ((0.5, 1.4, 1.6, 5.7, 170.0, 10000.0, 135.0), (0.5, 1.3, 2.0, 3.8, 230.0, 7000.0, 200.0))
+SRUN = 8
 PH = 10000.0
 ROUNDS = 4
-MORE = 1500
+MORE = 6500
+FINE = 0
+TEMP = 400.0
+SEED = 1
 f32, bf, f16, i32, u16 = "float32", "bfloat16", "float16", "int32", "uint16"
 SZ = {f32: 4, bf: 2, f16: 2, i32: 4, u16: 2}
 WA = f16 if VABS else f32
 SB = {
     "Dm": ([5, WT], bf), "Pt": ([WT], i32), "IOT": ([W], f32), "IO": ([160], f32),
     "jin": ([16], i32), "qin": ([L], i32), "win": ([2], i32),
-    "SU": ([10, 144], u16), "SV": ([10, 144], bf), "SX": ([8, H], u16),
-    "LU": ([4, 144], u16), "LV": ([4, 144], bf), "LX": ([4, H], u16), "JT": ([10, 8], f32),
-    "col": ([32], f32), "coli": ([8], i32), "thc": ([4, 8], f32), "thi": ([4, 4], i32), "cd": ([4, 2, 128], f16),
-    "ZP": ([144], bf), "ZQ": ([144], bf), "Z1": ([144], bf), "RS": ([16, 128], bf), "MT": ([18, 128], bf), "B0f": ([128], f32),
-    "tmp": ([6, 128], f32), "tmi": ([2, 128], i32), "ZB": ([128], bf), "thr": ([128], bf), "OH": ([16], f32), "PW": ([8], f32),
-    "dump": ([16], f32), "Pu": ([2, H], u16), "PQ": ([2, 2, H], f16), "Jb": ([2, H], f16),
+    "SJ": ([10, 8], u16), "SQ": ([8, H], f16), "SV": ([10, H], bf), "SX": ([8, H], u16),
+    "LJ": ([4, 8], u16), "LQ": ([4, H], f16), "LV": ([4, H], bf), "LX": ([4, H], u16), "JT": ([10, 8], f32),
+    "col": ([32], f32), "coli": ([8], i32), "ct": ([4, 16], f32), "u4": ([4], f32), "thi": ([4, 4], i32), "tho": ([4, 2], u16), "cd": ([4, 2, 128], f16),
+    "ZP": ([144], bf), "ZQ": ([144], bf), "Z1": ([144], bf), "RS": ([16, 8, 16], bf), "MT": ([17, 128], bf), "B0f": ([128], f32),
+    "tmp": ([6, 128], f32), "CI": ([8, 32], f32), "CW": ([8, 32], bf), "thr": ([128], bf), "OH": ([16], f32), "PW": ([8], f32),
+    "dump": ([16], f32), "Pu": ([2, H], u16), "NP": ([2, H], f16), "Jb": ([2, H], f16),
     "E": ([2, 8, H], bf), "E2": ([8, H], bf), "act": ([2, H], bf), "sg": ([2, 2 * H], bf),
     "rr": ([2, H], bf), "fr": ([2, H], bf), "sig": ([2, 8 * H], bf), "Df": ([2, H], bf), "nd": ([2, H], bf),
     "XT": ([2, H], f32), "hi": ([2, 2, 8], i32), "hh": ([2, 8], f32), "flag": ([H], WA), "tM": ([2, 8], f16),
     "sc1": ([2, 8], f32), "scu": ([2, 8], u16), "jm": ([2, 8], f32), "WQ": ([2, H], f16), "X": ([2, H], f16),
     "Ut": ([2, H], f32), "U": ([2, H], f16), "Wa": ([2, H], WA), "WTr": ([2, H], WA), "scn": ([2, H], WA),
     "fi": ([2, 2, 8], i32), "fM": ([2, 16], f16), "fz": ([2, 8], u16), "yqb": ([2, 2, H], f32), "yjb": ([2, H], f32),
-    "GJ": ([2, 2, 136 * 16], bf), "mk": ([2, 2, 2, H * 8], bf),
+    "GJ": ([2, 2, 136 * 16], bf), "mk": ([2, 2, H * 16], bf),
 }
 POOL = ("pD0", "pD1", "pM0", "pM1") + (("pQ0", "pQ1") if FIX1 else ())
 SCRATCH = {k: ("sbuf", [128] + v[0], v[1]) for k, v in SB.items()}
@@ -54,12 +64,12 @@ SCRATCH.update({k: ("psum", [128, 512], f32) for k in ("pD0", "pD1", "pM0", "pM1
 IOS = {"d0": ([128, W], bf), "p0": ([128, W], i32), "j0": ([128, 16], i32), "q0": ([128, L], i32), "v0": ([128, L], bf),
        "wa": ([128, 2], i32), "yd": ([128, W], bf), "yj": ([8, L], f32), "yq": ([128, L], f32), "yv": ([128, L], bf)}
 ENG = ("V", "S", "T", "G", "Y")
-PARTS = {"x": (("SX", "LX", H, 0),), "u": (("SU", "LU", 136, 0), ("SV", "LV", 136, 1))}
-MSGS = [k + str(i) for i in range(4) for k in (("x", "u") if EARLY else ("u",))]
+PARTS = {"x": (("SX", "LX", 0),), "j": (("SJ", "LJ", 1),), "u": (("SQ", "LQ", 0), ("SV", "LV", 1))}
+KINDS = "xju"
+MSGS = [k + str(i) for i in range(4) for k in KINDS]
 SEMAPHORES = (["eV", "eS", "eT", "eG"] + ["dm%d" % i for i in range(20)] + ["rel" + m for m in MSGS]
               + ["arr" + m for m in MSGS] + ["sent", "fwd"])
 NLOAD = 7
-s_ = np.s_
 
 
 def ap(name, idx=s_[:]):
@@ -142,32 +152,38 @@ def build():
     def bank_(): return "#%d" % new(1)
     def mm(out, lt, rhs, grp, first=False, f=1.0):
         op("T", "matmul", [out], [out, lt, rhs], cost=max(64, nel(rhs)) * f * PEF + TOV, grp=grp, first=first)
+    def run(k):
+        sub = ops[k:]
+        del ops[k:]
+        whole = sub[0]["first"] and len({o["grp"] for o in sub}) > 1
+        ops.append(dict(sub[0], wr=sorted({x for o in sub for x in o["wr"]}), rd=sorted({x for o in sub for x in o["rd"]}),
+                        cost=sum(o["cost"] for o in sub), grp=newg() if whole else sub[0]["grp"], sub=sub))
     def dma(q, out, a, nbytes, after=()):
-        op(q, "dma_start", [out], [out, a], cost=60.0, extra=("dma", new(2) - 1, 2200 + nbytes / 150.0), after=after)
+        op(q, "dma_start", [out], [out, a], cost=60.0, extra=("dma", new(2) - 1, 2200 + nbytes / RATE), after=after)
     def iota(out, pat, base, cm, fl=True):
         op("G", "iota", [out], [out, pat, base, cm], {"allow_small_or_imprecise_dtypes": True} if fl else {}, cost=160 + 2 * nel(out))
     def send(kind, slot, so):
-        op("G", "send", [], [None] + [ap(p[0], s_[:, so]) for p in PARTS[kind]], cost=300.0, extra=("send", kind + str(slot), so))
+        op("G", "send", [], [None] + [ap(p[0], s_[:, so]) for p in PARTS[kind]], cost=SEND, extra=("send", kind + str(slot), so))
     def arrive(kind, slot):
         op("X", "arrive", [ap(p[1], s_[:, slot]) for p in PARTS[kind]], [], extra=("arr", kind + str(slot)))
     def col(i): return ap("col", s_[:, i:i + 1])
     def coli(i): return ap("coli", s_[:, i:i + 1])
     def MT(i): return ap("MT", s_[:, i, :])
-    def RS(i): return ap("RS", s_[:, i, :])
+    def RS(i): return ap("RS", s_[:, i])
     def tmp(i): return ap("tmp", s_[:, i, :])
     def OH(i): return ap("OH", s_[:, i:i + 1])
     def ZW(z, i): return ap(z, s_[:, 15 - i:143 - i])
-    def thc(s, i): return ap("thc", s_[:, s, i:i + 1])
+    def thc(s, i): return ap("ct", s_[:, s, (i if s else 4 * i):(i if s else 4 * i) + 1])
     def Dm(s, a=0, b=W): return ap("Dm", s_[:, s, a:b])
-    (M_I, M_NI, M_SP, M_SQ, M_N2, M_R, M_LP, M_LQ, M_LA, M_LJ, M_LH, M_T00, M_T01, M_T10, M_T11, M_BO, M_C, M_C3) = range(18)
+    (M_I, M_NI, M_SP, M_SQ, M_R, M_LP, M_LQ, M_LA, M_LJ, M_LH, M_T00, M_T01, M_T10, M_T11, M_BO, M_C, M_C3) = range(17)
     (C_P, C_G, C_R, C_16, C_G15, C_H0, C_H1, C_P16, C_M16, C_PW, C_BIG, C_LP, C_LQ, C_A1, C_A2, C_W, C_A, C_U, C_T0, C_T1,
-     C_T4, C_C, C_C3, C_ACC) = range(24)
+     C_T4, C_C, C_C3, C_4, C_ACC) = range(25)
 
     dma("S", Dm(0), ap("d0"), 128 * 3200 + 100000)
     dma("Y", ap("qin"), ap("q0"), 131072 + 100000)
     dma("Y", ap("jin"), ap("j0"), 8192 + 100000)
     dma("Y", ap("win"), ap("wa"), 1024 + 100000)
-    dma("Y", ap("SV", s_[:, 0:2, 0:H]), ap("v0"), 65536 + 400000)
+    dma("Y", ap("SV", s_[:, 0:2]), ap("v0"), 65536 + 400000)
     dma("Y", ap("Pt", s_[:, 0:W]), ap("p0"), 128 * 6400 + 600000)
     dma("Y", Dm(1), ap("d0"), 128 * 3200 + 1420000)
     iota(coli(0), [[0, 1]], 0, 1, False)
@@ -176,10 +192,9 @@ def build():
     iota(tmp(1), [[0, 8], [1, 16]], 0, 0)
     iota(ap("dump"), [[16, 16]], W + 1 - 2048, 0)
     iota(ap("IOT"), [[1, W]], 0, 0)
-    iota(ap("tmi", s_[:, 0]), [[-1, 128]], 128, 1, False)
+    iota(ap("CI"), [[16, 8], [0, 2], [1, 16]], 0, 0)
     for i in range(4):
         ms(Dm(i, W, WD), 0.0)
-    ms(ap("SV", s_[:, 2:8, H:136]), 0.0)
     ms(tmp(2), 0.5)
     for i, m in ((1, 112), (2, 15), (3, 16)):
         ts(coli(i), coli(0), m, ALU.bitwise_and)
@@ -197,9 +212,9 @@ def build():
     ts(ap("Z1"), ap("IO", s_[:, 0:144]), col(C_G15), ALU.is_equal)
     sc(ap("ZP"), ap("Z1"), KP)
     sc(ap("ZQ"), ap("Z1"), KQ)
-    for m, c in ((M_NI, -1.0), (M_SP, -4.5 * KP), (M_SQ, -4.5 * KQ), (M_N2, -2.0), (M_R, -2.0 ** 20)):
+    for m, c in ((M_NI, -1.0), (M_SP, -4.5 * KP), (M_SQ, -4.5 * KQ), (M_R, 3200.0)):
         sc(MT(m), MT(M_I), c)
-    sc(ap("B0f"), MT(M_BO), OH(0))
+    ts(ap("B0f"), MT(M_BO), OH(0), ALU.mult, -0.5, ALU.mult)
     ts(tmp(3), IO128, 0.0, ALU.is_equal, 2.0 ** 63, ALU.mult)
     ts(ap("flag"), tmp(1), 0.0, ALU.is_equal, 8192.0, ALU.mult)
     scan(tmp(4), tmp(2), tmp(3), ALU.mult, ALU.max)
@@ -212,11 +227,11 @@ def build():
     ts(col(C_LP), OH(15), 0.5 * KP, ALU.mult, col(C_T0), ALU.add)
     ts(col(C_T1), OH(0), 8.5 * KQ, ALU.mult)
     ts(col(C_LQ), OH(15), -12.0 * KQ, ALU.mult, col(C_T1), ALU.add)
-    ts(col(C_C3), OH(14), -5120.0 / 2.0 ** 20 / BIG, ALU.mult)
+    ts(col(C_C3), OH(14), -1.0 / 256 / BIG, ALU.mult)
     ts(col(C_C), OH(15), 192.0 / BIG, ALU.mult, col(C_C3), ALU.add)
     for m, c in ((M_LP, C_LP), (M_LQ, C_LQ), (M_C, C_C)):
         sc(MT(m), MT(M_BO), col(c))
-    ts(MT(M_C3), MT(M_BO), col(C_C3), ALU.mult, -2.0 ** 20, ALU.mult)
+    ts(MT(M_C3), MT(M_BO), col(C_C3), ALU.mult, -3200.0 * 256, ALU.mult)
     ts(col(C_T4), OH(0), -1024.0, ALU.mult)
     ts(col(C_A1), OH(15), 1024.0, ALU.mult, col(C_T4), ALU.add)
     ts(col(C_A2), OH(15), -1024.0, ALU.mult, col(C_T4), ALU.add)
@@ -232,99 +247,109 @@ def build():
     TM = {(0, 0): M_T00, (0, 1): M_T01, (1, 0): M_T10, (1, 1): M_T11}
     ts(ap("dump"), ap("dump"), col(C_R), ALU.add)
     ts(col(C_U), col(C_A), 2.0, ALU.mult, -1.0, ALU.add)
-    ts(ap("tmi", s_[:, 1]), ap("tmi", s_[:, 0]), 15, ALU.bitwise_and)
-    tt(ap("ZB"), ap("tmi", s_[:, 1]), MT(M_BO), ALU.mult)
+    ts(ap("CW"), ap("CI"), col(C_P), ALU.is_equal)
     for i in range(1, 16):
-        ts(RS(i), ap("ZB"), float(i), ALU.is_equal)
-        op("G", "affine_select", [RS(i)], [RS(i), RS(i), [[-1, 128]], ALU.not_equal, 1.0, 0, 1], cost=205 + 2 * 128, after=[RS(i)])
+        op("G", "affine_select", [RS(i)], [RS(i), ap("CW", s_[:, :, i:i + 16]), [[-16, 8], [-1, 16]], ALU.not_equal, 1.0, 0, 1],
+           cost=205 + 2 * 128)
+    ts(ap("u4"), ap("IO", s_[:, 0:8:2]), col(C_U), ALU.add)
+    op("V", "reciprocal", [ap("ct", s_[:, 0, 0:4])], [ap("ct", s_[:, 0, 0:4]), ap("u4")], cost=260)
+    ts(ap("ct", s_[:, 0, 4:8]), ap("u4"), 1.0, ALU.min, MAGIC, ALU.mult)
+    ts(col(C_4), OH(1), 4.0, ALU.mult)
 
-    def scales(s, u):
-        op("V", "reciprocal", [thc(s, 1)], [thc(s, 1), u], cost=240)
-        ts(thc(s, 2), u, 1.0, ALU.min, MAGIC, ALU.mult)
-        ts(ap("cd", s_[:, s, 0]), MT(M_I), thc(s, 1), ALU.mult)
-        ts(ap("cd", s_[:, s, 1]), MT(M_I), thc(s, 1), ALU.mult, -1.0, ALU.mult)
+    def scales(s):
+        ts(ap("cd", s_[:, s, 0]), MT(M_I), thc(s, 0), ALU.mult)
+        ts(ap("cd", s_[:, s, 1]), MT(M_I), thc(s, 0), ALU.mult, -1.0, ALU.mult)
 
-    scales(0, col(C_U))
+    scales(0)
     for c in range(2):
-        cp(ap("SU", s_[:, c, 0:8]), ap("jin", s_[:, 8 * c:8 * c + 8]))
-        cp(ap("JT", s_[:, c, :]), ap("jin", s_[:, 8 * c:8 * c + 8]))
-        cp(ap("SU", s_[:, c, 8:136]), ap("qin", s_[:, H * c:H * c + H]))
+        cp(ap("SJ", s_[:, c]), ap("jin", s_[:, 8 * c:8 * c + 8]))
+        cp(ap("JT", s_[:, c]), ap("jin", s_[:, 8 * c:8 * c + 8]))
+        cp(ap("SX", s_[:, c]), ap("qin", s_[:, H * c:H * c + H]))
+        cp(ap("SQ", s_[:, c]), ap("qin", s_[:, H * c:H * c + H]))
 
     def tolist(bank, rhs_of, nq):
+        k = len(ops)
         for u in range(2):
             gq = newg()
             for h in range(2):
                 mm(ap(bank, s_[:, u:8 * nq:2]), MT(TM[(h, u)]), rhs_of(h), gq, first=(h == 0))
+        run(k)
+
+    def msum(o, *terms):
+        gq, k = newg(), len(ops)
+        for i, (m, x) in enumerate(terms):
+            mm(o, m, x, gq, first=not i)
+        run(k)
 
     def absdiff(out, d, v):
-        gq, o = newg(), ap(bank_(), s_[:, 0:H])
-        mm(o, MT(M_NI), v, gq, first=True)
-        mm(o, MT(M_I), d, gq)
+        o = ap(bank_(), s_[:, 0:H])
+        msum(o, (MT(M_NI), v), (MT(M_I), d))
         act(out, o, AF.Abs)
 
     mv = 0
-    src = [("SU", "SV", "SX", 0), ("SU", "SV", "SX", 1)]
+    src = [("S", 0), ("S", 1)]
     for s in range(4):
         last = s == 3
         Dw = Dm(s, 0, WD)
         nsrc, late = [], []
         for c in range(2):
-            un, vn, xn, sl = src[c]
+            at, sl = src[c]
+            vn = at + "V"
             jt, so = 2 * s + c, 2 * (s + 1) + c
             ph[0], ph[1] = jt, 0
-            Qu, Ju, v = ap(un, s_[:, sl, 8:136]), ap(un, s_[:, sl, 0:8]), ap(vn, s_[:, sl, 0:H])
-            early = EARLY and s
-            if un == "LU":
-                for kind in ("x", "u") if EARLY else ("u",):
+            Q16, Ju, v = (ap(at + x, s_[:, sl]) for x in "QJV")
+            if at == "L":
+                for kind in KINDS:
                     arrive(kind, sl)
                 cp(ap("JT", s_[:, jt, :]), Ju)
             if s and not c:
-                dma("Y", Dm(s + 1), Dm(s), 128 * 3200, after=[Ju] if un == "LU" else [])
+                dma("Y", Dm(s + 1), Dm(s), 128 * 3200, after=[Ju] if at == "L" else [])
             pP, pX, p3 = (ap("pP%d" % c, s_[:, H * i:H * i + H]) for i in range(3))
             pQ, aQ = ap("pQ%d" % c, s_[:, 0:H]), ap("pQ%d" % c, s_[:, H:2 * H])
             if FIX1:
                 pQ = aQ = ap("pP%d" % c, s_[:, 3 * H:4 * H])
-            NP, Q16, Jb = ap("PQ", s_[:, c, 0, :]), ap("PQ", s_[:, c, 1, :]), ap("Jb", s_[:, c, :])
+            NP, Jb = ap("NP", s_[:, c, :]), ap("Jb", s_[:, c, :])
             Pu, actb = ap("Pu", s_[:, c, :]), ap("act", s_[:, c, :])
-            cp(Q16, Qu)
             cp(Jb, ind(ap("IOT"), Ju))
             cp(Pu, ind(ap("Pt", s_[:, 0:W]), Ju))
             ts(NP, Pu, -1.0, ALU.mult)
             for f in late:
                 f()
             late = []
-            if early:
-                act(ap("GJ", s_[:, c, 1, 0:H]), ind(Dw, Ju), AF.Identity)
+            act(ap("GJ", s_[:, c, 1, 0:H]), ind(Dw, Ju), AF.Identity)
             ph[1] = 1
-            for l0 in range(0, H, PA):
-                a = l0 + 8 if l0 or early else 0
-                lst = ap(xn, s_[:, sl, l0:l0 + PA]) if early else ap(un, s_[:, sl, a:l0 + PA + 8])
-                act(ap("GJ", s_[:, c, 1, 16 * a:16 * (l0 + PA + 8)]), ind(Dw, lst), AF.Identity)
-            for l0 in range(0, H, PA):
-                act(ap("GJ", s_[:, c, 0, 16 * (8 + l0):16 * (8 + l0 + PA)]), ind(Dw, ap("Pu", s_[:, c, l0:l0 + PA])), AF.Identity)
+            for l0 in range(0, H, PA[1]):
+                act(ap("GJ", s_[:, c, 1, 16 * (8 + l0):16 * (8 + l0 + PA[1])]), ind(Dw, ap(at + "X", s_[:, sl, l0:l0 + PA[1]])), AF.Identity)
+            for l0 in range(0, H, PA[0]):
+                act(ap("GJ", s_[:, c, 0, 16 * (8 + l0):16 * (8 + l0 + PA[0])]), ind(Dw, ap("Pu", s_[:, c, l0:l0 + PA[0]])), AF.Identity)
             ph[1] = 0
             pM = bank_()
             gq = newg()
-            mm(ap(pM, s_[:, 0:H]), MT(M_NI), ap("thr"), gq, first=True)
             for b in range(8):
-                e = ap("E", s_[:, c, b, 0:H - 16 * b])
-                ts(e, ap("Jb", s_[:, c, 16 * b:H]), ap("JT", s_[:, jt, b:b + 1]), ALU.is_equal, ap("PW", s_[:, b:b + 1]), ALU.mult)
-                mm(ap(pM, s_[:, 16 * b:H]), MT(M_BO), e, gq)
+                ts(ap("E", s_[:, c, b, 0:H - 16 * b]), ap("Jb", s_[:, c, 16 * b:H]), ap("JT", s_[:, jt, b:b + 1]), ALU.is_equal,
+                   ap("PW", s_[:, b:b + 1]), ALU.mult)
             for b in range(8 * c):
                 ts(ap("E2", s_[:, b, :]), Jb, ap("JT", s_[:, jt - 1, b:b + 1]), ALU.is_equal, 2.0 ** 64, ALU.mult)
-                mm(ap(pM, s_[:, 0:H]), MT(M_BO), ap("E2", s_[:, b, :]), gq)
+            k = len(ops)
+            mm(ap(pM, s_[:, 0:H]), MT(M_NI), ap("thr"), gq, first=True)
+            for b in range(8):
+                mm(ap(pM, s_[:, 16 * b:H]), MT(M_BO), ap("E", s_[:, c, b, 0:H - 16 * b]), gq)
+            run(k)
+            if c:
+                for b in range(8):
+                    mm(ap(pM, s_[:, 0:H]), MT(M_BO), ap("E2", s_[:, b, :]), gq)
+                run(k + 1)
             act(actb, ap(pM, s_[:, 0:H]), AF.Sign, scale=-1.0, acc=None if last else col(C_ACC + c))
-            pM = bank_()
+            pM, k = bank_(), len(ops)
             for t, m, x in ((1, M_I, Q16), (0, M_NI, NP)):
                 gq = newg()
                 mm(ap(pM, s_[:, H * t:H * t + H]), MT(M_NI), Jb, gq, first=True)
                 mm(ap(pM, s_[:, H * t:H * t + H]), MT(m), x, gq)
+            run(k)
             act(ap("sg", s_[:, c]), ap(pM, s_[:, 0:2 * H]), AF.Sign, bias=-0.5)
             absdiff(ap("nd", s_[:, c, :]), ap("GJ", s_[:, c, 1, 0:H]), v)
-            gq, o = newg(), ap(bank_(), s_[:, 0:H])
-            mm(o, MT(M_LH), v, gq, first=True)
-            mm(o, MT(M_LJ), Jb, gq)
-            mm(o, MT(M_LA), actb, gq)
+            o = ap(bank_(), s_[:, 0:H])
+            msum(o, (MT(M_LH), v), (MT(M_LJ), Jb), (MT(M_LA), actb))
             tr(ap("XT", s_[:, c]), o)
             cp(ap("tM", s_[:, c]), ap("XT", s_[:, c, 2::16]))
             cp(ap("hi", s_[:, c, 0]), ap("XT", s_[:, c, 0::16]))
@@ -340,29 +365,39 @@ def build():
             if c == 1 and last:
                 dma("Y", ap("yd"), Dm(4), 128 * 3200)
             elif c == 1:
-                gq, o = newg(), ap(bank_(), s_[:, 0:1])
-                mm(o, ap("B0f"), col(C_ACC), gq, first=True, f=4.0)
-                mm(o, ap("B0f"), col(C_ACC + 1), gq, f=4.0)
-                ts(ap("thi", s_[:, s, 0:1]), o, -0.5, ALU.mult, 128.0, ALU.add)
+                pM = bank_()
+                mm(ap(pM, s_[:, 0:2]), ap("B0f"), ap("col", s_[:, C_ACC:C_ACC + 2]), newg(), first=True, f=4.0)
+                ts(ap("thi", s_[:, s, 0:1]), ap(pM, s_[:, 0:1]), ap(pM, s_[:, 1:2]), ALU.add, 128.0, ALU.add)
                 ts(ap("thi", s_[:, s, 1:2]), ap("thi", s_[:, s, 0:1]), 3, ALU.bitwise_and)
-                ts(thc(s + 1, 0), ap("thi", s_[:, s, 1:2]), 2.0, ALU.mult, col(C_U), ALU.add)
-                scales(s + 1, thc(s + 1, 0))
+                ts(ap("tho", s_[:, s, 0:1]), ap("thi", s_[:, s, 1:2]), col(C_4), ALU.add)
+                cp(ap("ct", s_[:, s + 1]), ind(ap("ct", s_[:, 0, 0:8]), ap("tho", s_[:, s, 0:1])))
+                scales(s + 1)
             ph[1] = 1
             for t, pb, z, msg, ml in ((1, pQ, "ZQ", M_SQ, M_LQ), (0, pP, "ZP", M_SP, M_LP)):
-                for l0 in range(0, H, 64):
-                    for h in range(2):
+                nl = BL[t]
+                nh, ns = nl // 32, 512 // nl
+                for l0 in range(0, H, nl):
+                    for h in range(nh):
                         bank, gq = bank_(), newg()
-                        mm(ap(bank), ap("cd", s_[:, s, 0]), ap("GJ", s_[:, c, t, 16 * (8 + l0) + h:16 * (72 + l0):2]), gq, first=True)
-                        for i in range(8):
-                            mm(ap(bank, s_[:, i::8]), ap("cd", s_[:, s, 1]), ap(vn, s_[:, sl, l0:l0 + 64]), gq)
-                        ts(ap("mk", s_[:, c, t, h, 8 * l0:8 * l0 + 512]), ap(bank), MAGIC, ALU.add, thc(s, 2), ALU.is_equal)
+                        mm(ap(bank), ap("cd", s_[:, s, 0]), ap("GJ", s_[:, c, t, 16 * (8 + l0) + h:16 * (8 + nl + l0):nh]), gq, first=True)
+                        for i in range(ns):
+                            mm(ap(bank, s_[:, i::ns]), ap("cd", s_[:, s, 1]), ap(vn, s_[:, sl, l0:l0 + nl]), gq)
+                        run(len(ops) - ns - 1)
+                        x = ns * (H * h + l0)
+                        for y in range(0, 512, MS[t]):
+                            ts(ap("mk", s_[:, c, t, x + y:x + y + MS[t]]), ap(bank, s_[:, y:y + MS[t]]), MAGIC, ALU.add, thc(s, 1), ALU.is_equal)
                 gb = newg()
                 mm(pb, MT(ml), actb, gb, first=True)
                 mm(pb, MT(msg), ap("sg", s_[:, c, H * t:H * t + H]), gb)
-                for l0 in range(0, H, SUMN):
-                    for i in range(16):
-                        x = pb[2][1].start + l0
-                        mm(ap(pb[1], s_[:, x:x + SUMN]), ZW(z, i), ap("mk", s_[:, c, t, i % 2, 8 * l0 + i // 2:8 * (l0 + SUMN):8]), gb)
+                run(len(ops) - 2)
+                sn = SUMN[t]
+                for l0 in range(0, H, sn):
+                    for h in range(nh):
+                        for i in range(ns):
+                            x, y = pb[2][1].start + l0, ns * (H * h + l0)
+                            mm(ap(pb[1], s_[:, x:x + sn]), ZW(z, nh * i + h), ap("mk", s_[:, c, t, y + i:y + ns * sn:ns]), gb)
+                            if i % SRUN == SRUN - 1:
+                                run(len(ops) - SRUN)
                 if t:
                     tt(ap("WQ", s_[:, c, :]), pQ, Q16, ALU.max)
             X, Wa, ph[1] = ap("X", s_[:, c, :]), ap("Wa", s_[:, c, :]), 2
@@ -373,9 +408,9 @@ def build():
                 tt(Wa, pX, X, ALU.max)
             else:
                 act(Wa, pX, AF.Abs)
-            if last:
+            if last and DV[jt]:
                 act(ap("yqb", s_[:, c, 0]), pX, AF.Relu)
-            elif EARLY:
+            elif not last:
                 ts(ap("SX", s_[:, so]), Wa, float(W), ALU.min)
                 if HOP[s]:
                     send("x", 2 * mv + c, so)
@@ -390,7 +425,9 @@ def build():
             fz = ap("fz", s_[:, c, :])
             ts(fz, ap(pM, s_[:, 0:8]), float(W), ALU.min)
             tt(ap("JT", s_[:, so, :]), ap(pM, s_[:, 8:16]), ap("jm", s_[:, c, :]), ALU.max)
-            cp(ap("SU", s_[:, so, 0:8]), ap("JT", s_[:, so, :]))
+            cp(ap("SJ", s_[:, so]), ap("JT", s_[:, so, :]))
+            if HOP[s]:
+                send("j", 2 * mv + c, so)
             if VDF:
                 tt(ap("Df", s_[:, c]), ind(Dw, fz), v, ALU.subtract)
                 act(ap("SV", s_[:, so, 0:H]), ap("Df", s_[:, c]), AF.Abs)
@@ -400,13 +437,15 @@ def build():
             g1, g3 = newg(), newg()
             if DV[jt]:
                 mm(p3, MT(M_C3), ap("thr"), g3, first=True)
-                mm(p3, MT(M_N2), X, g3)
+                mm(p3, MT(M_NI), X, g3)
+                run(len(ops) - 2)
             else:
                 mm(aQ, MT(M_C), ap("thr"), g1, first=True)
             for k in range(2):
                 bank = bank_()
                 for i in range(4):
                     mm(ap(bank, s_[:, H * i:H * i + H]), RS(4 * k + i + 1), X, newg(), first=True)
+                run(len(ops) - 4)
                 o = ap("sig", s_[:, c, 512 * k:512 * k + 512])
                 if DV[jt]:
                     ts(o, ap(bank), 0.0, ALU.is_equal, -8192.0, ALU.mult)
@@ -415,29 +454,36 @@ def build():
                 for i in range(4):
                     x = 512 * k + H * i
                     mm(p3 if DV[jt] else aQ, RS(15 - 4 * k - i), ap("sig", s_[:, c, x:x + H]), g3 if DV[jt] else g1)
+                run(len(ops) - 4)
             if not DV[jt]:
                 act(ap("rr", s_[:, c, :]), aQ, AF.Identity)
-                tt(ap("fr", s_[:, c, :]), aQ, ap("rr", s_[:, c, :]), ALU.subtract)
-                mm(p3, MT(M_N2), X, g3, first=True)
-                mm(p3, MT(M_R), ap("fr", s_[:, c, :]), g3)
+                tt(ap("fr", s_[:, c, :]), aQ, ap("rr", s_[:, c, :]), ALU.is_le)
+                msum(p3, (MT(M_NI), X), (MT(M_R), ap("fr", s_[:, c, :])))
             if last:
-                tt(p3, p3, X, ALU.min)
-                tt(ap("yqb", s_[:, c, 1]), p3, ap("yqb", s_[:, c, 0]), ALU.max)
+                if DV[jt]:
+                    tt(p3, p3, X, ALU.min)
+                    tt(ap("yqb", s_[:, c, 1]), p3, ap("yqb", s_[:, c, 0]), ALU.max)
+                else:
+                    tt(ap("yqb", s_[:, c, 0]), p3, Wa, ALU.min)
+                    ts(ap("yqb", s_[:, c, 1]), ap("yqb", s_[:, c, 0]), 0.0, ALU.max)
                 dma("Y", ap("yq", s_[:, H * c:H * c + H]), ap("yqb", s_[:, c, 1]), 65536)
-                act(ap("yjb", s_[:, c, :]), ind(ap("IOT"), ap("SU", s_[:, so, 0:8])), AF.Identity)
+                act(ap("yjb", s_[:, c, :]), ind(ap("IOT"), ap("SJ", s_[:, so])), AF.Identity)
                 dma("Y", ap("yv", s_[:, H * c:H * c + H]), ap("SV", s_[:, so, 0:H]), 32768)
                 dma("Y", ap("yj", s_[:, H * c:H * c + H]), ap("yjb", s_[0:128:16, c, :]), 4096)
             else:
                 U = ap("U", s_[:, c, :])
-                tt(ap("Ut", s_[:, c, :]), p3, X, ALU.min)
-                tt(U, pX, ap("Ut", s_[:, c, :]), ALU.max)
-                cp(ap("SU", s_[:, so, 8:136]), U)
+                if DV[jt]:
+                    tt(ap("Ut", s_[:, c, :]), p3, X, ALU.min)
+                    tt(U, pX, ap("Ut", s_[:, c, :]), ALU.max)
+                else:
+                    tt(U, p3, Wa, ALU.min)
+                ts(ap("SQ", s_[:, so]), U, 0.0, ALU.max)
                 late.append(lambda U=U, scu=scu: cp(ind(ap("Pt"), scu), U))
             if HOP[s]:
                 send("u", 2 * mv + c, so)
-                nsrc.append(("LU", "LV", "LX", 2 * mv + c))
+                nsrc.append(("L", 2 * mv + c))
             else:
-                nsrc.append(("SU", "SV", "SX", so))
+                nsrc.append(("S", so))
         for f in late:
             f()
         mv += 1 if HOP[s] else 0
@@ -509,9 +555,10 @@ def graph(ops, deps, sess):
                 pred=[[(j, (0.0 if eng[k] == "T" else SAME) if eng[j] == eng[k] else SYNC) for j in deps[k]] for k in range(n)])
 
 
-def schedule(gr, key):
-    n, eng, succ, lat, busy, bank, sess, opens, slack = (gr[x] for x in "n eng succ lat busy bank sess opens slack".split())
-    left = list(gr["nd"])
+def schedule(gr, key, slack=None):
+    n, eng, succ, lat, busy, bank, sess, opens = (gr[x] for x in "n eng succ lat busy bank sess opens".split())
+    slack = slack or gr["slack"]
+    left, rdy, before, lastk = list(gr["nd"]), [0.0] * n, [None] * n, {}
     ready_t, done_t = [0.0] * n, [0.0] * n
     free = {e: 0.0 for e in ENG + ("X",)}
     ready = {e: [k for k in range(n) if not left[k] and eng[k] == e] for e in free}
@@ -526,10 +573,15 @@ def schedule(gr, key):
             if lst:
                 t0 = max(free[e], min(lst)[0])
                 _, k, r = max((key[k], k, r) for r, k in lst if r <= t0 + slack[k])
-                cand[e] = (max(free[e], r), e, k)
+                if r > t0 + 30.0:
+                    fill = [(key[m], m, x) for x, m in lst if max(x, t0) + busy[m] <= r + FILL]
+                    if fill:
+                        _, k, r = max(fill)
+                cand[e] = (max(free[e], r), e, k, r)
             else:
                 cand.pop(e, None)
-        t, e, k = min(cand.values())
+        t, e, k, rdy[k] = min(cand.values())
+        before[k], lastk[e] = lastk.get(e), k
         dirty = {e}
         ready[e].remove(k)
         order.append(k)
@@ -555,7 +607,7 @@ def schedule(gr, key):
             if not left[m]:
                 ready[eng[m]].append(m)
                 dirty.add(eng[m])
-    return max(done_t), order, prev, banks, start
+    return max(done_t), order, prev, banks, start, key, slack, rdy, before
 
 
 def backward(gr, start):
@@ -588,8 +640,41 @@ def backward(gr, start):
     return out
 
 
+def variant(ops, gr, f, g, sc, sync, comm, rate):
+    busy, lat = [], []
+    for o, b in zip(ops, gr["busy"]):
+        i = [k for k, a in enumerate(o["args"]) if is_ap(a) and a[0] == "ind"]
+        if i:
+            b = 70 + (b - 70) * (g / G_ if i[0] else sc / SC_)
+        busy.append(b * (f if o["eng"] in "VSTG" else 1.0))
+        lat.append(2200 + (o["extra"][2] - 2200) * RATE / rate if o["meth"] == "dma_start" else comm if o["meth"] == "arrive" else busy[-1])
+    return busy, lat, [[(j, sync if x else 0.0) for j, x in p] for p in gr["pred"]], sync
+
+
+def replay(gr, r, var):
+    busy, lat, pred, sync = var
+    done, free, eng, prev = [0.0] * gr["n"], dict.fromkeys(ENG + ("X",), 0.0), gr["eng"], r[2]
+    for k in r[1]:
+        t = free[eng[k]]
+        for j, g in pred[k]:
+            if done[j] + g > t:
+                t = done[j] + g
+        if k in prev:
+            for j in prev[k]:
+                if done[j] + sync > t:
+                    t = done[j] + sync
+        free[eng[k]] = t + busy[k]
+        done[k] = t + lat[k]
+    return max(done)
+
+
 def search(ops, gr):
     n = gr["n"]
+    var = [(variant(ops, gr, *v[1:]), v[0] / v[1]) for v in VARS]
+    tot = 1.0 + sum(v[0] for v in VARS)
+
+    def score(r, lim):
+        return (r[0] + sum(w * replay(gr, r, v) for v, w in var)) / tot if r[0] < lim else 1e9
     pr = [0.0] * n
     for k in range(n - 1, -1, -1):
         pr[k] = gr["lat"][k] + max([pr[m] + g for m, g in gr["succ"][k] if ops[m]["ph"] == ops[k]["ph"]] + [0.0])
@@ -600,7 +685,8 @@ def search(ops, gr):
             if best is None or r[0] < best[0]:
                 best = r
             r = schedule(gr, backward(gr, r[4]))
-    rng, cur = np.random.default_rng(1), best
+    rng, cur = np.random.default_rng(SEED), best
+    xc = xb = score(best, 1e9)
     cl = [o["eng"] + (o["wr"][0][0] if o["wr"] and not o["bank"] else "") + str(o["ph"]) for o in ops]
     c2 = ["%d.%d" % (o["ph"], o["cls"]) for o in ops]
     names, name2 = sorted(set(cl)), sorted(set(c2))
@@ -609,23 +695,63 @@ def search(ops, gr):
         off[name2[int(rng.integers(0, len(name2)))]] = float(rng.normal() * 2000)
         base = [-x for x in cur[4]] if i % 2 else backward(gr, cur[4])
         r = schedule(gr, [x + off.get(c, 0.0) + off.get(d, 0.0) for x, c, d in zip(base, cl, c2)])
-        if r[0] < cur[0] + 200:
+        x = score(r, cur[0] + 1500)
+        if x < xc + 200:
+            cur, xc = r, x
+        if x < xb:
+            best, xb = r, x
+    cur, slack = best, best[6]
+    for i in range(FINE):
+        key, sl = list(cur[5]), list(cur[6])
+        late = chain(gr, cur)
+        for _ in range(int(rng.integers(1, 3)) if late else 0):
+            k, p, rdy = late[int(rng.integers(0, len(late)))]
+            up, x = [k], rng.random()
+            if x < 0.4:
+                sl[k] = max(sl[k], rdy - cur[4][p] + 1.0)
+            elif x < 0.7:
+                for j in up:
+                    up += [m for m, _ in gr["pred"][j] if m not in up and cur[4][m] > cur[4][k] - 2500.0]
+            d = max(key[p] - key[k], 0.0) + 1.0 + (600.0 * rng.random() if x > 0.4 else 0.0)
+            if x < 0.85:
+                for j in up:
+                    key[j] += d
+            else:
+                key[p] -= d
+                sl[p] = SLACK
+        r = schedule(gr, key, sl)
+        if r[0] < cur[0] + TEMP * (1.0 - i / FINE) * rng.random():
             cur = r
         if r[0] < best[0]:
             best = r
     return best
 
 
+def chain(gr, r):
+    start, ready, before, out = r[4], r[7], r[8], []
+    k = max(range(gr["n"]), key=lambda j: start[j] + gr["lat"][j])
+    while True:
+        p = before[k]
+        if p is not None and start[k] > ready[k] + 1e-6:
+            out.append((k, p, ready[k]))
+            k = p
+            continue
+        c = [(start[j] + gr["lat"][j] + g, j) for j, g in gr["pred"][k]] + [(start[j] + gr["lat"][j] + SYNC, j) for j in r[2].get(k, ())]
+        if not c:
+            return out
+        k = max(c)[1]
+
+
 def program():
     ops = build()
     deps, sess = depend(ops)
-    total, order, prev, banks, start = search(ops, graph(ops, deps, sess))
+    total, order, prev, banks, start = search(ops, graph(ops, deps, sess))[:5]
     for k, x in prev.items():
         deps[k] |= set(x)
     order = list(range(NLOAD)) + [k for k in order if k >= NLOAD and ops[k]["eng"] != "X"]
     pos = {k: i for i, k in enumerate(order)}
     pos.update({k: 0 for k, o in enumerate(ops) if o["eng"] == "X"})
-    lastg = {ops[k]["grp"]: k for k in order}
+    lastg = {x["grp"]: (k, i) for k in order for i, x in enumerate(ops[k].get("sub", [ops[k]]))}
     seen = {e: {} for e in ENG}
     marks, waits = set(), {}
     for k in order:
@@ -651,8 +777,10 @@ def program():
             val[k] = cnt[o["eng"]]
         w = [("e" + key, val[j]) if key in ENG else ("dm%d" % key[1], 16) if key[0] == "dma" else ("arr" + key[1], None)
              for key, j in waits[k]]
-        tail = [o["first"], lastg[o["grp"]] == k] if o["meth"] == "matmul" else []
-        out.append((o, w, tail, k in val))
+        sub = o.get("sub", [o])
+        for i, x in enumerate(sub):
+            tail = [x["first"], lastg[x["grp"]] == (k, i)] if o["meth"] == "matmul" else []
+            out.append((x, [] if i else w, tail, k in val and i == len(sub) - 1))
     return out, banks, total, ops
 
 
@@ -710,10 +838,10 @@ def rank_program(g, core, T, topo):
                     parts, slot = PARTS[m[0]], int(m[1])
                     to = T.cores[(r + hops[slot // 2]) % n]
                     rid, pid = topo.addr(to, core)
-                    for k, (_, land, w, by) in enumerate(parts):
+                    for k, (_, land, by) in enumerate(parts):
                         if rl[by] == core:
                             g.wait_ge(T.sem["rel" + m], share(topo, c, core, k, len(parts))[1])
-                            g.remote_dma(T[land][:, slot, 0:w], T[land][:, slot, 0:w], T.sem["arr" + m], T.sem.fwd, pid, rid,
+                            g.remote_dma(T[land][:, slot], T[land][:, slot], T.sem["arr" + m], T.sem.fwd, pid, rid,
                                          topo.mask(core, to))
                             tot += len(topo.engines(core, to))
                 g.wait_ge(T.sem.fwd, tot)
@@ -729,16 +857,16 @@ def rank_program(g, core, T, topo):
         for nm, val in waits:
             if val is None:
                 frm = relays_of(T, topo, T.cores[(rank - hops[int(nm[4]) // 2]) % n])
-                val = sum(len(topo.engines(frm[p[3]], core)) for p in PARTS[nm[3]])
+                val = sum(len(topo.engines(frm[p[2]], core)) for p in PARTS[nm[3]])
             e.wait_ge(T.sem[nm], val)
         if m == "send":
             _, msg, so = o["extra"]
             parts, tr = PARTS[msg[0]], []
-            for k, (a, b, w, by) in enumerate(parts):
+            for k, (a, b, by) in enumerate(parts):
                 rid, pid = topo.addr(rl[by], core)
                 mask, h = share(topo, core, rl[by], k, len(parts))
                 tr.append(RemoteDMATransfer(dst_ids=[DstId(rid=rid, pnc=pid)], dma_engine_mask=mask, remote_sem=T.sem["rel" + msg],
-                                            src=T[a][:, so, 0:w], dst=T[b][:, int(msg[1]), 0:w]))
+                                            src=T[a][:, so], dst=T[b][:, int(msg[1])]))
                 sent += h
             g.remote_dma_fused(tr, local_sem=T.sem.sent)
             continue

@@ -4,12 +4,12 @@ from concourse.mybir import AluOpType as ALU, AxisListType, ActivationFunctionTy
 
 W, L, H = 1600, 256, 128
 HOP = (1, 0, 3, 0)
-PA = (64, 64)
+PA = (32, 32)
 BL = (64, 64)
-SUMN = (128, 128)
+SUMN = (64, 128)
 MS = (512, 512)
 RATE = 190.0
-DV = (0, 1, 0, 0, 0, 1, 0, 1)
+DV = (0, 0, 0, 0, 0, 0, 0, 1)
 s_ = np.s_
 VDF = 1
 VABS = 1
@@ -24,6 +24,7 @@ SC_ = 4.4
 PEF = 0.5
 TOV = 4.0
 SEND = 500.0
+FIRST = 3500.0
 COMM = 7500.0
 SYNC = 230.0
 SAME = 230.0
@@ -34,10 +35,23 @@ VARS = ((0.5, 1.4, 1.6, 5.7, 170.0, 10000.0, 135.0), (0.5, 1.3, 2.0, 3.8, 230.0,
 SRUN = 8
 PH = 10000.0
 ROUNDS = 4
-MORE = 6500
+MORE = 4800
 FINE = 0
 TEMP = 400.0
-SEED = 1
+SEED = 5
+SIG = 2000.0
+NM = 3
+P2 = 0.5
+PB = 0.25
+PW_ = 0.7
+TM_ = 350.0
+COOL = 1.0
+PC = 0.05
+FST = 1
+PRE = 1
+EP = 1
+NDV = 1
+KEEP = 2
 f32, bf, f16, i32, u16 = "float32", "bfloat16", "float16", "int32", "uint16"
 SZ = {f32: 4, bf: 2, f16: 2, i32: 4, u16: 2}
 WA = f16 if VABS else f32
@@ -64,12 +78,13 @@ SCRATCH.update({k: ("psum", [128, 512], f32) for k in ("pD0", "pD1", "pM0", "pM1
 IOS = {"d0": ([128, W], bf), "p0": ([128, W], i32), "j0": ([128, 16], i32), "q0": ([128, L], i32), "v0": ([128, L], bf),
        "wa": ([128, 2], i32), "yd": ([128, W], bf), "yj": ([8, L], f32), "yq": ([128, L], f32), "yv": ([128, L], bf)}
 ENG = ("V", "S", "T", "G", "Y")
-PARTS = {"x": (("SX", "LX", 0),), "j": (("SJ", "LJ", 1),), "u": (("SQ", "LQ", 0), ("SV", "LV", 1))}
-KINDS = "xju"
+PARTS = {"x": (("SX", "LX", 0, s_[0:64]), ("SX", "LX", 1, s_[64:H])), "j": (("SJ", "LJ", 1, s_[:]),),
+         "v": (("SV", "LV", 0, s_[:]),), "u": (("SQ", "LQ", 1, s_[:]),)}
+KINDS = "xjvu"
 MSGS = [k + str(i) for i in range(4) for k in KINDS]
 SEMAPHORES = (["eV", "eS", "eT", "eG"] + ["dm%d" % i for i in range(20)] + ["rel" + m for m in MSGS]
               + ["arr" + m for m in MSGS] + ["sent", "fwd"])
-NLOAD = 7
+NLOAD = 8
 
 
 def ap(name, idx=s_[:]):
@@ -165,7 +180,7 @@ def build():
     def send(kind, slot, so):
         op("G", "send", [], [None] + [ap(p[0], s_[:, so]) for p in PARTS[kind]], cost=SEND, extra=("send", kind + str(slot), so))
     def arrive(kind, slot):
-        op("X", "arrive", [ap(p[1], s_[:, slot]) for p in PARTS[kind]], [], extra=("arr", kind + str(slot)))
+        op("X", "arrive", [ap(p[1], s_[:, slot]) for p in PARTS[kind]], [], extra=("arr", kind + str(slot), FIRST if kind + str(slot) == MSGS[0] else 0.0))
     def col(i): return ap("col", s_[:, i:i + 1])
     def coli(i): return ap("coli", s_[:, i:i + 1])
     def MT(i): return ap("MT", s_[:, i, :])
@@ -179,13 +194,14 @@ def build():
     (C_P, C_G, C_R, C_16, C_G15, C_H0, C_H1, C_P16, C_M16, C_PW, C_BIG, C_LP, C_LQ, C_A1, C_A2, C_W, C_A, C_U, C_T0, C_T1,
      C_T4, C_C, C_C3, C_4, C_ACC) = range(25)
 
-    dma("S", Dm(0), ap("d0"), 128 * 3200 + 100000)
-    dma("Y", ap("qin"), ap("q0"), 131072 + 100000)
+    dma("S", Dm(0), ap("d0"), 128 * 3200 + 50000)
+    dma("Y", ap("qin", s_[:, 0:H]), ap("q0", s_[:, 0:H]), 65536 + 100000)
     dma("Y", ap("jin"), ap("j0"), 8192 + 100000)
     dma("Y", ap("win"), ap("wa"), 1024 + 100000)
     dma("Y", ap("SV", s_[:, 0:2]), ap("v0"), 65536 + 400000)
-    dma("Y", ap("Pt", s_[:, 0:W]), ap("p0"), 128 * 6400 + 600000)
-    dma("Y", Dm(1), ap("d0"), 128 * 3200 + 1420000)
+    dma("Y", ap("Pt", s_[:, 0:W]), ap("p0"), 128 * 6400 + 550000)
+    dma("Y", ap("qin", s_[:, H:L]), ap("q0", s_[:, H:L]), 65536 + 1370000)
+    dma("Y", Dm(1), ap("d0"), 128 * 3200 + 1430000)
     iota(coli(0), [[0, 1]], 0, 1, False)
     iota(ap("IO"), [[1, 160]], 0, 0)
     iota(tmp(0), [[16, 8], [0, 16]], 0, 0)
@@ -286,12 +302,12 @@ def build():
         msum(o, (MT(M_NI), v), (MT(M_I), d))
         act(out, o, AF.Abs)
 
-    mv = 0
+    mv, late = 0, []
     src = [("S", 0), ("S", 1)]
     for s in range(4):
         last = s == 3
         Dw = Dm(s, 0, WD)
-        nsrc, late = [], []
+        nsrc = []
         for c in range(2):
             at, sl = src[c]
             vn = at + "V"
@@ -299,11 +315,13 @@ def build():
             ph[0], ph[1] = jt, 0
             Q16, Ju, v = (ap(at + x, s_[:, sl]) for x in "QJV")
             if at == "L":
-                for kind in KINDS:
+                for kind in KINDS[c:]:
                     arrive(kind, sl)
+                if not c:
+                    arrive("x", sl + 1)
                 cp(ap("JT", s_[:, jt, :]), Ju)
             if s and not c:
-                dma("Y", Dm(s + 1), Dm(s), 128 * 3200, after=[Ju] if at == "L" else [])
+                dma("Y", Dm(s + 1), Dm(s), 128 * 3200, after=[ap("LX", s_[:, sl + 1])] if at == "L" else [])
             pP, pX, p3 = (ap("pP%d" % c, s_[:, H * i:H * i + H]) for i in range(3))
             pQ, aQ = ap("pQ%d" % c, s_[:, 0:H]), ap("pQ%d" % c, s_[:, H:2 * H])
             if FIX1:
@@ -312,11 +330,12 @@ def build():
             Pu, actb = ap("Pu", s_[:, c, :]), ap("act", s_[:, c, :])
             cp(Jb, ind(ap("IOT"), Ju))
             cp(Pu, ind(ap("Pt", s_[:, 0:W]), Ju))
-            ts(NP, Pu, -1.0, ALU.mult)
             for f in late:
                 f()
-            late = []
-            act(ap("GJ", s_[:, c, 1, 0:H]), ind(Dw, Ju), AF.Identity)
+            del late[:]
+            ts(NP, ind(ap("Pt", s_[:, 0:W]), Ju) if EP and s and not c else Pu, -1.0, ALU.mult)
+            if not NDV:
+                act(ap("GJ", s_[:, c, 1, 0:H]), ind(Dw, Ju), AF.Identity)
             ph[1] = 1
             for l0 in range(0, H, PA[1]):
                 act(ap("GJ", s_[:, c, 1, 16 * (8 + l0):16 * (8 + l0 + PA[1])]), ind(Dw, ap(at + "X", s_[:, sl, l0:l0 + PA[1]])), AF.Identity)
@@ -347,7 +366,11 @@ def build():
                 mm(ap(pM, s_[:, H * t:H * t + H]), MT(m), x, gq)
             run(k)
             act(ap("sg", s_[:, c]), ap(pM, s_[:, 0:2 * H]), AF.Sign, bias=-0.5)
-            absdiff(ap("nd", s_[:, c, :]), ap("GJ", s_[:, c, 1, 0:H]), v)
+            if NDV:
+                tt(ap("GJ", s_[:, c, 1, 0:H]), ind(Dw, Ju), v, ALU.subtract)
+                act(ap("nd", s_[:, c, :]), ap("GJ", s_[:, c, 1, 0:H]), AF.Abs)
+            else:
+                absdiff(ap("nd", s_[:, c, :]), ap("GJ", s_[:, c, 1, 0:H]), v)
             o = ap(bank_(), s_[:, 0:H])
             msum(o, (MT(M_LH), v), (MT(M_LJ), Jb), (MT(M_LA), actb))
             tr(ap("XT", s_[:, c]), o)
@@ -374,30 +397,42 @@ def build():
                 scales(s + 1)
             ph[1] = 1
             for t, pb, z, msg, ml in ((1, pQ, "ZQ", M_SQ, M_LQ), (0, pP, "ZP", M_SP, M_LP)):
-                nl = BL[t]
+                nl, ph[1] = BL[t], 1
                 nh, ns = nl // 32, 512 // nl
                 for l0 in range(0, H, nl):
                     for h in range(nh):
                         bank, gq = bank_(), newg()
-                        mm(ap(bank), ap("cd", s_[:, s, 0]), ap("GJ", s_[:, c, t, 16 * (8 + l0) + h:16 * (8 + nl + l0):nh]), gq, first=True)
+                        d = ap("GJ", s_[:, c, t, 16 * (8 + l0) + h:16 * (8 + nl + l0):nh])
+                        if not PRE:
+                            mm(ap(bank), ap("cd", s_[:, s, 0]), d, gq, first=True)
                         for i in range(ns):
-                            mm(ap(bank, s_[:, i::ns]), ap("cd", s_[:, s, 1]), ap(vn, s_[:, sl, l0:l0 + nl]), gq)
-                        run(len(ops) - ns - 1)
+                            mm(ap(bank, s_[:, i::ns]), ap("cd", s_[:, s, 1]), ap(vn, s_[:, sl, l0:l0 + nl]), gq, first=bool(PRE and not i))
+                        run(len(ops) - ns - (not PRE))
+                        if PRE:
+                            ops[-1]["pre"] = True
+                            mm(ap(bank), ap("cd", s_[:, s, 0]), d, gq)
                         x = ns * (H * h + l0)
                         for y in range(0, 512, MS[t]):
                             ts(ap("mk", s_[:, c, t, x + y:x + y + MS[t]]), ap(bank, s_[:, y:y + MS[t]]), MAGIC, ALU.add, thc(s, 1), ALU.is_equal)
-                gb = newg()
-                mm(pb, MT(ml), actb, gb, first=True)
-                mm(pb, MT(msg), ap("sg", s_[:, c, H * t:H * t + H]), gb)
-                run(len(ops) - 2)
+                gb, ph[1] = newg(), 3
                 sn = SUMN[t]
+                lead = t or sn < H or not FST
+                if not FST or sn < H:
+                    mm(pb, MT(ml), actb, gb, first=True)
+                    mm(pb, MT(msg), ap("sg", s_[:, c, H * t:H * t + H]), gb)
+                    run(len(ops) - 2)
                 for l0 in range(0, H, sn):
                     for h in range(nh):
                         for i in range(ns):
                             x, y = pb[2][1].start + l0, ns * (H * h + l0)
-                            mm(ap(pb[1], s_[:, x:x + sn]), ZW(z, nh * i + h), ap("mk", s_[:, c, t, y + i:y + ns * sn:ns]), gb)
+                            mm(ap(pb[1], s_[:, x:x + sn]), ZW(z, nh * i + h), ap("mk", s_[:, c, t, y + i:y + ns * sn:ns]), gb,
+                               first=bool(FST and sn == H and not h and not i))
                             if i % SRUN == SRUN - 1:
                                 run(len(ops) - SRUN)
+                if FST and sn == H:
+                    mm(pb, MT(ml), actb, gb)
+                    mm(pb, MT(msg), ap("sg", s_[:, c, H * t:H * t + H]), gb)
+                    run(len(ops) - 2)
                 if t:
                     tt(ap("WQ", s_[:, c, :]), pQ, Q16, ALU.max)
             X, Wa, ph[1] = ap("X", s_[:, c, :]), ap("Wa", s_[:, c, :]), 2
@@ -412,6 +447,8 @@ def build():
                 act(ap("yqb", s_[:, c, 0]), pX, AF.Relu)
             elif not last:
                 ts(ap("SX", s_[:, so]), Wa, float(W), ALU.min)
+                if EP and c:
+                    cp(ind(ap("Pt"), scu), ap("SX", s_[:, so]))
                 if HOP[s]:
                     send("x", 2 * mv + c, so)
             tr(ap("WTr", s_[:, c, :]), Wa)
@@ -434,6 +471,9 @@ def build():
             else:
                 act(ap("Df", s_[:, c]), ind(Dw, fz), AF.Identity)
                 absdiff(ap("SV", s_[:, so, 0:H]), ap("Df", s_[:, c]), v)
+            if HOP[s]:
+                send("v", 2 * mv + c, so)
+            ph[1] = 4
             g1, g3 = newg(), newg()
             if DV[jt]:
                 mm(p3, MT(M_C3), ap("thr"), g3, first=True)
@@ -484,8 +524,10 @@ def build():
                 nsrc.append(("L", 2 * mv + c))
             else:
                 nsrc.append(("S", so))
-        for f in late:
-            f()
+        if not EP:
+            for f in late:
+                f()
+            del late[:]
         mv += 1 if HOP[s] else 0
         src = nsrc
     return ops
@@ -523,7 +565,9 @@ def depend(ops):
     for lst in sess.values():
         inside = set(lst)
         for k in lst[1:]:
-            deps[lst[0]] |= {j for j in deps[k] - inside if j < lst[0]}
+            for j in deps[k] - inside:
+                if j < lst[0]:
+                    deps[lst[0]] |= deps[j] if ops[lst[0]].get("pre") and ops[j]["eng"] == "S" else {j}
             deps[k].add(lst[0])
     anc = []
     for k, d in enumerate(deps):
@@ -538,7 +582,7 @@ def depend(ops):
 
 
 def latency(o):
-    return o["extra"][2] if o["meth"] == "dma_start" else COMM if o["meth"] == "arrive" else o["cost"]
+    return o["extra"][2] if o["meth"] == "dma_start" else COMM + o["extra"][2] if o["meth"] == "arrive" else o["cost"]
 
 
 def graph(ops, deps, sess):
@@ -550,8 +594,8 @@ def graph(ops, deps, sess):
             succ[j].append((k, (0.0 if eng[k] == "T" else SAME) if eng[j] == eng[k] else SYNC))
     return dict(n=n, eng=eng, succ=succ, lat=[latency(o) for o in ops], busy=[o["cost"] if o["eng"] != "X" else 0.0 for o in ops],
                 nd=[len(d) for d in deps], bank=[o["bank"] for o in ops], sess=sess,
-                opens=[bool(o["bank"]) and sess[o["bank"]][0] == k for k, o in enumerate(ops)],
-                slack=[SL2 if o["cls"] == 2 else SLACK for o in ops],
+                opens=[(KEEP if o.get("pre") else 1) if o["bank"] and sess[o["bank"]][0] == k else 0 for k, o in enumerate(ops)],
+                slack=[SL2 if o["cls"] in (2, 4) else SLACK for o in ops],
                 pred=[[(j, (0.0 if eng[k] == "T" else SAME) if eng[j] == eng[k] else SYNC) for j in deps[k]] for k in range(n)])
 
 
@@ -569,7 +613,7 @@ def schedule(gr, key, slack=None):
     while len(order) < n:
         fb = min(fbank) if fbank else None
         for e in dirty:
-            lst = [(max(ready_t[k], fb[0] + SYNC) if opens[k] else ready_t[k], k) for k in ready[e] if fb or not opens[k]]
+            lst = [(max(ready_t[k], fb[0] + SYNC) if opens[k] else ready_t[k], k) for k in ready[e] if len(fbank) >= opens[k]]
             if lst:
                 t0 = max(free[e], min(lst)[0])
                 _, k, r = max((key[k], k, r) for r, k in lst if r <= t0 + slack[k])
@@ -640,14 +684,16 @@ def backward(gr, start):
     return out
 
 
-def variant(ops, gr, f, g, sc, sync, comm, rate):
+def variant(ops, gr, f, g, sc, sync, comm, rate, ov=TOV):
     busy, lat = [], []
     for o, b in zip(ops, gr["busy"]):
         i = [k for k, a in enumerate(o["args"]) if is_ap(a) and a[0] == "ind"]
         if i:
             b = 70 + (b - 70) * (g / G_ if i[0] else sc / SC_)
+        if o["eng"] == "T":
+            b += (ov - TOV) * len(o.get("sub", [o]))
         busy.append(b * (f if o["eng"] in "VSTG" else 1.0))
-        lat.append(2200 + (o["extra"][2] - 2200) * RATE / rate if o["meth"] == "dma_start" else comm if o["meth"] == "arrive" else busy[-1])
+        lat.append(2200 + (o["extra"][2] - 2200) * RATE / rate if o["meth"] == "dma_start" else comm + o["extra"][2] if o["meth"] == "arrive" else busy[-1])
     return busy, lat, [[(j, sync if x else 0.0) for j, x in p] for p in gr["pred"]], sync
 
 
@@ -680,7 +726,7 @@ def search(ops, gr):
         pr[k] = gr["lat"][k] + max([pr[m] + g for m, g in gr["succ"][k] if ops[m]["ph"] == ops[k]["ph"]] + [0.0])
     best = None
     for w0, w2 in ((1.5, 2.5), (0.5, 2.5), (0.9, 0.9), (0.0, 0.0)):
-        r = schedule(gr, [0.3 * pr[k] + PH * ((w0, 0.0, w2)[o["cls"]] - o["ph"]) - k * 1e-3 for k, o in enumerate(ops)])
+        r = schedule(gr, [0.3 * pr[k] + PH * ((w0, 0.0, w2, 0.0, w2)[o["cls"]] - o["ph"]) - k * 1e-3 for k, o in enumerate(ops)])
         for x in range(ROUNDS + 1):
             if best is None or r[0] < best[0]:
                 best = r
@@ -691,12 +737,20 @@ def search(ops, gr):
     c2 = ["%d.%d" % (o["ph"], o["cls"]) for o in ops]
     names, name2 = sorted(set(cl)), sorted(set(c2))
     for i in range(MORE):
-        off = {names[int(x)]: float(rng.normal() * 2000) for x in rng.integers(0, len(names), 4)}
-        off[name2[int(rng.integers(0, len(name2)))]] = float(rng.normal() * 2000)
-        base = [-x for x in cur[4]] if i % 2 else backward(gr, cur[4])
+        off = {names[int(x)]: float(rng.normal() * SIG) for x in rng.integers(0, len(names), NM)}
+        if rng.random() < P2:
+            off[name2[int(rng.integers(0, len(name2)))]] = float(rng.normal() * SIG)
+        if rng.random() < PC:
+            p, x = int(rng.integers(0, 8)), float(rng.uniform(1000, 7000))
+            off.update({"%d.%d" % (p + a, b): x for a, b in ((0, 2), (0, 3), (1, 0)) if rng.random() < 0.8})
+        if rng.random() < PB:
+            t0, base = rng.random() * cur[0] * (rng.random() < PW_), backward(gr, cur[4])
+            base = [b - cur[0] if t > t0 else -t for b, t in zip(base, cur[4])]
+        else:
+            base = [-x for x in cur[4]]
         r = schedule(gr, [x + off.get(c, 0.0) + off.get(d, 0.0) for x, c, d in zip(base, cl, c2)])
         x = score(r, cur[0] + 1500)
-        if x < xc + 200:
+        if x < xc + TM_ * (1.0 - COOL * i / MORE):
             cur, xc = r, x
         if x < xb:
             best, xb = r, x
@@ -838,10 +892,10 @@ def rank_program(g, core, T, topo):
                     parts, slot = PARTS[m[0]], int(m[1])
                     to = T.cores[(r + hops[slot // 2]) % n]
                     rid, pid = topo.addr(to, core)
-                    for k, (_, land, by) in enumerate(parts):
+                    for k, (_, land, by, w) in enumerate(parts):
                         if rl[by] == core:
                             g.wait_ge(T.sem["rel" + m], share(topo, c, core, k, len(parts))[1])
-                            g.remote_dma(T[land][:, slot], T[land][:, slot], T.sem["arr" + m], T.sem.fwd, pid, rid,
+                            g.remote_dma(T[land][:, slot, w], T[land][:, slot, w], T.sem["arr" + m], T.sem.fwd, pid, rid,
                                          topo.mask(core, to))
                             tot += len(topo.engines(core, to))
                 g.wait_ge(T.sem.fwd, tot)
@@ -862,11 +916,11 @@ def rank_program(g, core, T, topo):
         if m == "send":
             _, msg, so = o["extra"]
             parts, tr = PARTS[msg[0]], []
-            for k, (a, b, by) in enumerate(parts):
+            for k, (a, b, by, w) in enumerate(parts):
                 rid, pid = topo.addr(rl[by], core)
                 mask, h = share(topo, core, rl[by], k, len(parts))
                 tr.append(RemoteDMATransfer(dst_ids=[DstId(rid=rid, pnc=pid)], dma_engine_mask=mask, remote_sem=T.sem["rel" + msg],
-                                            src=T[a][:, so], dst=T[b][:, int(msg[1])]))
+                                            src=T[a][:, so, w], dst=T[b][:, int(msg[1]), w]))
                 sent += h
             g.remote_dma_fused(tr, local_sem=T.sem.sent)
             continue

import numpy as np
from concourse.bass import DstId, RemoteDMATransfer
from concourse.mybir import AluOpType as ALU, AxisListType, ActivationFunctionType as AF

W, L, H = 1600, 256, 128
HOP = (1, 0, 3, 0)
PA = (32, 32)
BL = (64, 64)
SUMN = (64, 128)
MS = (512, 512)
RATE = 190.0
DV = (0, 0, 0, 0, 0, 0, 0, 1)
s_ = np.s_
VDF = 1
VABS = 1
FIX1 = 1
KP, KQ = 6656.0, 3328.0
MAGIC = 12582912.0
BIG = 2.0 ** 75
WT = 1872
WD = 1608
G_ = 1.7
SC_ = 4.4
PEF = 0.5
TOV = 4.0
SEND = 500.0
FIRST = 3500.0
COMM = 7500.0
SYNC = 230.0
SAME = 230.0
SLACK = 40.0
FILL = 40.0
SL2 = 240.0
VARS = ((0.5, 1.4, 1.6, 5.7, 170.0, 10000.0, 135.0), (0.5, 1.3, 2.0, 3.8, 230.0, 7000.0, 200.0))
SRUN = 8
PH = 10000.0
ROUNDS = 4
MORE = 4800
FINE = 0
TEMP = 400.0
SEED = 5
SIG = 2000.0
NM = 3
P2 = 0.5
PB = 0.25
PW_ = 0.7
TM_ = 350.0
COOL = 1.0
PC = 0.05
FST = 1
PRE = 1
EP = 1
NDV = 1
KEEP = 2
f32, bf, f16, i32, u16 = "float32", "bfloat16", "float16", "int32", "uint16"
SZ = {f32: 4, bf: 2, f16: 2, i32: 4, u16: 2}
WA = f16 if VABS else f32
SB = {
    "Dm": ([5, WT], bf), "Pt": ([WT], i32), "IOT": ([W], f32), "IO": ([160], f32),
    "jin": ([16], i32), "qin": ([L], i32), "win": ([2], i32),
    "SJ": ([10, 8], u16), "SQ": ([8, H], f16), "SV": ([10, H], bf), "SX": ([8, H], u16),
    "LJ": ([4, 8], u16), "LQ": ([4, H], f16), "LV": ([4, H], bf), "LX": ([4, H], u16), "JT": ([10, 8], f32),
    "col": ([32], f32), "coli": ([8], i32), "ct": ([4, 16], f32), "u4": ([4], f32), "thi": ([4, 4], i32), "tho": ([4, 2], u16), "cd": ([4, 2, 128], f16),
    "ZP": ([144], bf), "ZQ": ([144], bf), "Z1": ([144], bf), "RS": ([16, 8, 16], bf), "MT": ([17, 128], bf), "B0f": ([128], f32),
    "tmp": ([6, 128], f32), "CI": ([8, 32], f32), "CW": ([8, 32], bf), "thr": ([128], bf), "OH": ([16], f32), "PW": ([8], f32),
    "dump": ([16], f32), "Pu": ([2, H], u16), "NP": ([2, H], f16), "Jb": ([2, H], f16),
    "E": ([2, 8, H], bf), "E2": ([8, H], bf), "act": ([2, H], bf), "sg": ([2, 2 * H], bf),
    "rr": ([2, H], bf), "fr": ([2, H], bf), "sig": ([2, 8 * H], bf), "Df": ([2, H], bf), "nd": ([2, H], bf),
    "XT": ([2, H], f32), "hi": ([2, 2, 8], i32), "hh": ([2, 8], f32), "flag": ([H], WA), "tM": ([2, 8], f16),
    "sc1": ([2, 8], f32), "scu": ([2, 8], u16), "jm": ([2, 8], f32), "WQ": ([2, H], f16), "X": ([2, H], f16),
    "Ut": ([2, H], f32), "U": ([2, H], f16), "Wa": ([2, H], WA), "WTr": ([2, H], WA), "scn": ([2, H], WA),
    "fi": ([2, 2, 8], i32), "fM": ([2, 16], f16), "fz": ([2, 8], u16), "yqb": ([2, 2, H], f32), "yjb": ([2, H], f32),
    "GJ": ([2, 2, 136 * 16], bf), "mk": ([2, 2, H * 16], bf),
}
POOL = ("pD0", "pD1", "pM0", "pM1") + (("pQ0", "pQ1") if FIX1 else ())
SCRATCH = {k: ("sbuf", [128] + v[0], v[1]) for k, v in SB.items()}
SCRATCH.update({k: ("psum", [128, 512], f32) for k in ("pD0", "pD1", "pM0", "pM1", "pQ0", "pQ1", "pP0", "pP1")})
IOS = {"d0": ([128, W], bf), "p0": ([128, W], i32), "j0": ([128, 16], i32), "q0": ([128, L], i32), "v0": ([128, L], bf),
       "wa": ([128, 2], i32), "yd": ([128, W], bf), "yj": ([8, L], f32), "yq": ([128, L], f32), "yv": ([128, L], bf)}
ENG = ("V", "S", "T", "G", "Y")
PARTS = {"x": (("SX", "LX", 0, s_[0:64]), ("SX", "LX", 1, s_[64:H])), "j": (("SJ", "LJ", 1, s_[:]),),
         "v": (("SV", "LV", 0, s_[:]),), "u": (("SQ", "LQ", 1, s_[:]),)}
KINDS = "xjvu"
MSGS = [k + str(i) for i in range(4) for k in KINDS]
SEMAPHORES = (["eV", "eS", "eT", "eG"] + ["dm%d" % i for i in range(20)] + ["rel" + m for m in MSGS]
              + ["arr" + m for m in MSGS] + ["sent", "fwd"])
NLOAD = 8


def ap(name, idx=s_[:]):
    return ("ap", name, idx if isinstance(idx, tuple) else (idx,))


def ind(win, off):
    return ("ind", win, off)


def is_ap(a):
    return isinstance(a, tuple) and len(a) == 3 and a[0] in ("ap", "ind")


_span = {}


def span(a):
    key = (a[1], repr(a[2]))
    if key not in _span:
        shape, dt = ([128, 512], f32) if a[1][0] == "#" else SCRATCH[a[1]][1:] if a[1] in SCRATCH else IOS[a[1]]
        x = np.arange(int(np.prod(shape[1:]))).reshape([1] + list(shape[1:]))[(slice(None),) + a[2][1:]]
        _span[key] = (a[1], int(x.min()) * SZ[dt], (int(x.max()) + 1) * SZ[dt], int(x.size), SZ[dt])
    return _span[key]


def nel(a):
    return 16 * span(a[2])[3] if a[0] == "ind" else span(a)[3]


def is_ps(name):
    return name[0] == "#" or name in SCRATCH and SCRATCH[name][0] == "psum"


def build():
    ops, ph, cnt = [], [0, 0], [0, 0, 0, 0]

    def op(eng, meth, outs, args, kw=None, cost=64.0, grp=None, first=False, extra=None, after=()):
        kw = kw or {}
        wr, rd = [], [span(a) for a in after]
        for o in outs:
            if o[0] == "ind":
                wr.append(span(o[1])); rd.append(span(o[2]))
            else:
                wr.append(span(o))
        for k, a in enumerate(list(args) + list(kw.values())):
            if is_ap(a) and not ((k == 0 or k >= len(args)) and a in outs):
                rd += [span(a[1]), span(a[2])] if a[0] == "ind" else [span(a)]
        bank = [x[0] for x in wr + rd if x[0][0] == "#"]
        ops.append(dict(eng=eng, meth=meth, args=args, kw=kw, wr=wr, rd=rd, cost=cost, grp=grp, first=first, extra=extra,
                        ph=ph[0], cls=ph[1], bank=bank[0] if bank else None))

    def vcost(out, ins, base):
        if out[0] == "ind":
            return 60 + SC_ * nel(out)
        if ins[0][0] == "ind":
            return 60 + G_ * nel(ins[0])
        if base == 2:
            r = 1.0 if any(is_ps(a[1]) for a in ins) else 2.0
        else:
            r = 0.5 if all(span(a)[4] == 2 for a in ins + [out]) else 1.0
        return max(64.0, 30 + r * nel(out))

    def cp(out, a): op("V", "tensor_copy", [out], [out, a], cost=vcost(out, [a], 1))
    def tt(out, a, b, o): op("V", "tensor_tensor", [out], [out, a, b, o], cost=vcost(out, [a, b], 2))
    def ts(out, a, s1, o1, s2=None, o2=None):
        op("V", "tensor_scalar", [out], [out, a, s1, s2, o1] + ([o2] if o2 is not None else []), cost=vcost(out, [a], 1))
    def ms(out, c): op("V", "memset", [out], [out, c], cost=max(64.0, 30 + nel(out) * span(out)[4] / 4))
    def tr(out, a): op("V", "transpose", [out], [out, a], cost=vcost(out, [a], 1))
    def scan(out, a, b, o0, o1): op("V", "tensor_tensor_scan", [out], [out, a, b, 0.0, o0, o1], cost=vcost(out, [a, b], 1))
    def act(out, a, f, bias=None, scale=None, acc=None, more=0):
        kw = {k: x for k, x in (("bias", bias), ("scale", scale), ("accum_out", acc)) if x is not None}
        op("S", "activation", [out] + ([acc] if acc else []), [out, a, f], kw,
           cost=80 + more + nel(out) * (G_ if a[0] == "ind" else 1.0))
    def sc(out, a, c): act(out, a, AF.Identity, scale=c)
    def new(i):
        cnt[i] += 1
        return cnt[i]
    def newg(): return new(0)
    def bank_(): return "#%d" % new(1)
    def mm(out, lt, rhs, grp, first=False, f=1.0):
        op("T", "matmul", [out], [out, lt, rhs], cost=max(64, nel(rhs)) * f * PEF + TOV, grp=grp, first=first)
    def run(k):
        sub = ops[k:]
        del ops[k:]
        whole = sub[0]["first"] and len({o["grp"] for o in sub}) > 1
        ops.append(dict(sub[0], wr=sorted({x for o in sub for x in o["wr"]}), rd=sorted({x for o in sub for x in o["rd"]}),
                        cost=sum(o["cost"] for o in sub), grp=newg() if whole else sub[0]["grp"], sub=sub))
    def dma(q, out, a, nbytes, after=()):
        op(q, "dma_start", [out], [out, a], cost=60.0, extra=("dma", new(2) - 1, 2200 + nbytes / RATE), after=after)
    def iota(out, pat, base, cm, fl=True):
        op("G", "iota", [out], [out, pat, base, cm], {"allow_small_or_imprecise_dtypes": True} if fl else {}, cost=160 + 2 * nel(out))
    def send(kind, slot, so):
        op("G", "send", [], [None] + [ap(p[0], s_[:, so]) for p in PARTS[kind]], cost=SEND, extra=("send", kind + str(slot), so))
    def arrive(kind, slot):
        op("X", "arrive", [ap(p[1], s_[:, slot]) for p in PARTS[kind]], [], extra=("arr", kind + str(slot), FIRST if kind + str(slot) == MSGS[0] else 0.0))
    def col(i): return ap("col", s_[:, i:i + 1])
    def coli(i): return ap("coli", s_[:, i:i + 1])
    def MT(i): return ap("MT", s_[:, i, :])
    def RS(i): return ap("RS", s_[:, i])
    def tmp(i): return ap("tmp", s_[:, i, :])
    def OH(i): return ap("OH", s_[:, i:i + 1])
    def ZW(z, i): return ap(z, s_[:, 15 - i:143 - i])
    def thc(s, i): return ap("ct", s_[:, s, (i if s else 4 * i):(i if s else 4 * i) + 1])
    def Dm(s, a=0, b=W): return ap("Dm", s_[:, s, a:b])
    (M_I, M_NI, M_SP, M_SQ, M_R, M_LP, M_LQ, M_LA, M_LJ, M_LH, M_T00, M_T01, M_T10, M_T11, M_BO, M_C, M_C3) = range(17)
    (C_P, C_G, C_R, C_16, C_G15, C_H0, C_H1, C_P16, C_M16, C_PW, C_BIG, C_LP, C_LQ, C_A1, C_A2, C_W, C_A, C_U, C_T0, C_T1,
     C_T4, C_C, C_C3, C_4, C_ACC) = range(25)

    dma("S", Dm(0), ap("d0"), 128 * 3200 + 50000)
    dma("Y", ap("qin", s_[:, 0:H]), ap("q0", s_[:, 0:H]), 65536 + 100000)
    dma("Y", ap("jin"), ap("j0"), 8192 + 100000)
    dma("Y", ap("win"), ap("wa"), 1024 + 100000)
    dma("Y", ap("SV", s_[:, 0:2]), ap("v0"), 65536 + 400000)
    dma("Y", ap("Pt", s_[:, 0:W]), ap("p0"), 128 * 6400 + 550000)
    dma("Y", ap("qin", s_[:, H:L]), ap("q0", s_[:, H:L]), 65536 + 1370000)
    dma("Y", Dm(1), ap("d0"), 128 * 3200 + 1430000)
    iota(coli(0), [[0, 1]], 0, 1, False)
    iota(ap("IO"), [[1, 160]], 0, 0)
    iota(tmp(0), [[16, 8], [0, 16]], 0, 0)
    iota(tmp(1), [[0, 8], [1, 16]], 0, 0)
    iota(ap("dump"), [[16, 16]], W + 1 - 2048, 0)
    iota(ap("IOT"), [[1, W]], 0, 0)
    iota(ap("CI"), [[16, 8], [0, 2], [1, 16]], 0, 0)
    for i in range(4):
        ms(Dm(i, W, WD), 0.0)
    ms(tmp(2), 0.5)
    for i, m in ((1, 112), (2, 15), (3, 16)):
        ts(coli(i), coli(0), m, ALU.bitwise_and)
    cp(ap("col", s_[:, 0:4]), ap("coli", s_[:, 0:4]))
    ts(col(C_G15), col(C_G), 15.0, ALU.add)
    act(col(C_H1), col(C_16), AF.Sigmoid, bias=-800.0, scale=100.0, more=1560)
    act(col(C_H0), col(C_16), AF.Sigmoid, bias=800.0, scale=-100.0)
    ts(col(C_P16), col(C_P), 16.0, ALU.add)
    ts(col(C_M16), col(C_P), -16.0, ALU.add)
    cp(ap("col", s_[:, C_W:C_W + 2]), ap("win"))
    IO128 = ap("IO", s_[:, 0:128])
    ts(ap("OH"), ap("IO", s_[:, 0:16]), col(C_R), ALU.is_equal)
    ts(MT(M_BO), tmp(0), col(C_G), ALU.is_equal)
    ts(MT(M_I), IO128, col(C_P), ALU.is_equal)
    ts(ap("Z1"), ap("IO", s_[:, 0:144]), col(C_G15), ALU.is_equal)
    sc(ap("ZP"), ap("Z1"), KP)
    sc(ap("ZQ"), ap("Z1"), KQ)
    for m, c in ((M_NI, -1.0), (M_SP, -4.5 * KP), (M_SQ, -4.5 * KQ), (M_R, 3200.0)):
        sc(MT(m), MT(M_I), c)
    ts(ap("B0f"), MT(M_BO), OH(0), ALU.mult, -0.5, ALU.mult)
    ts(tmp(3), IO128, 0.0, ALU.is_equal, 2.0 ** 63, ALU.mult)
    ts(ap("flag"), tmp(1), 0.0, ALU.is_equal, 8192.0, ALU.mult)
    scan(tmp(4), tmp(2), tmp(3), ALU.mult, ALU.max)
    tt(ap("tmp", s_[:, 5, 0:16]), ap("tmp", s_[:, 4, 0:16]), ap("OH"), ALU.mult)
    op("V", "tensor_reduce", [col(C_PW)], [col(C_PW), ap("tmp", s_[:, 5, 0:16]), AxisListType.X, ALU.add])
    ts(col(C_BIG), col(C_R), 13.0, ALU.is_ge, BIG, ALU.mult)
    ts(ap("thr"), tmp(4), 2.5, ALU.mult, col(C_BIG), ALU.max)
    ts(ap("PW"), ap("tmp", s_[:, 4, 0::16]), col(C_PW), ALU.mult, 2.0 ** -63, ALU.mult)
    ts(col(C_T0), OH(0), -4.5 * KP, ALU.mult)
    ts(col(C_LP), OH(15), 0.5 * KP, ALU.mult, col(C_T0), ALU.add)
    ts(col(C_T1), OH(0), 8.5 * KQ, ALU.mult)
    ts(col(C_LQ), OH(15), -12.0 * KQ, ALU.mult, col(C_T1), ALU.add)
    ts(col(C_C3), OH(14), -1.0 / 256 / BIG, ALU.mult)
    ts(col(C_C), OH(15), 192.0 / BIG, ALU.mult, col(C_C3), ALU.add)
    for m, c in ((M_LP, C_LP), (M_LQ, C_LQ), (M_C, C_C)):
        sc(MT(m), MT(M_BO), col(c))
    ts(MT(M_C3), MT(M_BO), col(C_C3), ALU.mult, -3200.0 * 256, ALU.mult)
    ts(col(C_T4), OH(0), -1024.0, ALU.mult)
    ts(col(C_A1), OH(15), 1024.0, ALU.mult, col(C_T4), ALU.add)
    ts(col(C_A2), OH(15), -1024.0, ALU.mult, col(C_T4), ALU.add)
    sc(tmp(2), ZW("Z1", 1), col(C_A1))
    sc(tmp(5), ZW("Z1", 2), col(C_A2))
    tt(MT(M_LA), tmp(2), tmp(5), ALU.add)
    sc(MT(M_LJ), ZW("Z1", 2), OH(0))
    sc(MT(M_LH), ZW("Z1", 0), col(C_W))
    sc(MT(M_T00), MT(M_I), col(C_H0))
    sc(MT(M_T11), MT(M_I), col(C_H1))
    ts(MT(M_T10), IO128, col(C_P16), ALU.is_equal, col(C_H0), ALU.mult)
    ts(MT(M_T01), IO128, col(C_M16), ALU.is_equal, col(C_H1), ALU.mult)
    TM = {(0, 0): M_T00, (0, 1): M_T01, (1, 0): M_T10, (1, 1): M_T11}
    ts(ap("dump"), ap("dump"), col(C_R), ALU.add)
    ts(col(C_U), col(C_A), 2.0, ALU.mult, -1.0, ALU.add)
    ts(ap("CW"), ap("CI"), col(C_P), ALU.is_equal)
    for i in range(1, 16):
        op("G", "affine_select", [RS(i)], [RS(i), ap("CW", s_[:, :, i:i + 16]), [[-16, 8], [-1, 16]], ALU.not_equal, 1.0, 0, 1],
           cost=205 + 2 * 128)
    ts(ap("u4"), ap("IO", s_[:, 0:8:2]), col(C_U), ALU.add)
    op("V", "reciprocal", [ap("ct", s_[:, 0, 0:4])], [ap("ct", s_[:, 0, 0:4]), ap("u4")], cost=260)
    ts(ap("ct", s_[:, 0, 4:8]), ap("u4"), 1.0, ALU.min, MAGIC, ALU.mult)
    ts(col(C_4), OH(1), 4.0, ALU.mult)

    def scales(s):
        ts(ap("cd", s_[:, s, 0]), MT(M_I), thc(s, 0), ALU.mult)
        ts(ap("cd", s_[:, s, 1]), MT(M_I), thc(s, 0), ALU.mult, -1.0, ALU.mult)

    scales(0)
    for c in range(2):
        cp(ap("SJ", s_[:, c]), ap("jin", s_[:, 8 * c:8 * c + 8]))
        cp(ap("JT", s_[:, c]), ap("jin", s_[:, 8 * c:8 * c + 8]))
        cp(ap("SX", s_[:, c]), ap("qin", s_[:, H * c:H * c + H]))
        cp(ap("SQ", s_[:, c]), ap("qin", s_[:, H * c:H * c + H]))

    def tolist(bank, rhs_of, nq):
        k = len(ops)
        for u in range(2):
            gq = newg()
            for h in range(2):
                mm(ap(bank, s_[:, u:8 * nq:2]), MT(TM[(h, u)]), rhs_of(h), gq, first=(h == 0))
        run(k)

    def msum(o, *terms):
        gq, k = newg(), len(ops)
        for i, (m, x) in enumerate(terms):
            mm(o, m, x, gq, first=not i)
        run(k)

    def absdiff(out, d, v):
        o = ap(bank_(), s_[:, 0:H])
        msum(o, (MT(M_NI), v), (MT(M_I), d))
        act(out, o, AF.Abs)

    mv, late = 0, []
    src = [("S", 0), ("S", 1)]
    for s in range(4):
        last = s == 3
        Dw = Dm(s, 0, WD)
        nsrc = []
        for c in range(2):
            at, sl = src[c]
            vn = at + "V"
            jt, so = 2 * s + c, 2 * (s + 1) + c
            ph[0], ph[1] = jt, 0
            Q16, Ju, v = (ap(at + x, s_[:, sl]) for x in "QJV")
            if at == "L":
                for kind in KINDS[c:]:
                    arrive(kind, sl)
                if not c:
                    arrive("x", sl + 1)
                cp(ap("JT", s_[:, jt, :]), Ju)
            if s and not c:
                dma("Y", Dm(s + 1), Dm(s), 128 * 3200, after=[ap("LX", s_[:, sl + 1])] if at == "L" else [])
            pP, pX, p3 = (ap("pP%d" % c, s_[:, H * i:H * i + H]) for i in range(3))
            pQ, aQ = ap("pQ%d" % c, s_[:, 0:H]), ap("pQ%d" % c, s_[:, H:2 * H])
            if FIX1:
                pQ = aQ = ap("pP%d" % c, s_[:, 3 * H:4 * H])
            NP, Jb = ap("NP", s_[:, c, :]), ap("Jb", s_[:, c, :])
            Pu, actb = ap("Pu", s_[:, c, :]), ap("act", s_[:, c, :])
            cp(Jb, ind(ap("IOT"), Ju))
            cp(Pu, ind(ap("Pt", s_[:, 0:W]), Ju))
            for f in late:
                f()
            del late[:]
            ts(NP, ind(ap("Pt", s_[:, 0:W]), Ju) if EP and s and not c else Pu, -1.0, ALU.mult)
            if not NDV:
                act(ap("GJ", s_[:, c, 1, 0:H]), ind(Dw, Ju), AF.Identity)
            ph[1] = 1
            for l0 in range(0, H, PA[1]):
                act(ap("GJ", s_[:, c, 1, 16 * (8 + l0):16 * (8 + l0 + PA[1])]), ind(Dw, ap(at + "X", s_[:, sl, l0:l0 + PA[1]])), AF.Identity)
            for l0 in range(0, H, PA[0]):
                act(ap("GJ", s_[:, c, 0, 16 * (8 + l0):16 * (8 + l0 + PA[0])]), ind(Dw, ap("Pu", s_[:, c, l0:l0 + PA[0]])), AF.Identity)
            ph[1] = 0
            pM = bank_()
            gq = newg()
            for b in range(8):
                ts(ap("E", s_[:, c, b, 0:H - 16 * b]), ap("Jb", s_[:, c, 16 * b:H]), ap("JT", s_[:, jt, b:b + 1]), ALU.is_equal,
                   ap("PW", s_[:, b:b + 1]), ALU.mult)
            for b in range(8 * c):
                ts(ap("E2", s_[:, b, :]), Jb, ap("JT", s_[:, jt - 1, b:b + 1]), ALU.is_equal, 2.0 ** 64, ALU.mult)
            k = len(ops)
            mm(ap(pM, s_[:, 0:H]), MT(M_NI), ap("thr"), gq, first=True)
            for b in range(8):
                mm(ap(pM, s_[:, 16 * b:H]), MT(M_BO), ap("E", s_[:, c, b, 0:H - 16 * b]), gq)
            run(k)
            if c:
                for b in range(8):
                    mm(ap(pM, s_[:, 0:H]), MT(M_BO), ap("E2", s_[:, b, :]), gq)
                run(k + 1)
            act(actb, ap(pM, s_[:, 0:H]), AF.Sign, scale=-1.0, acc=None if last else col(C_ACC + c))
            pM, k = bank_(), len(ops)
            for t, m, x in ((1, M_I, Q16), (0, M_NI, NP)):
                gq = newg()
                mm(ap(pM, s_[:, H * t:H * t + H]), MT(M_NI), Jb, gq, first=True)
                mm(ap(pM, s_[:, H * t:H * t + H]), MT(m), x, gq)
            run(k)
            act(ap("sg", s_[:, c]), ap(pM, s_[:, 0:2 * H]), AF.Sign, bias=-0.5)
            if NDV:
                tt(ap("GJ", s_[:, c, 1, 0:H]), ind(Dw, Ju), v, ALU.subtract)
                act(ap("nd", s_[:, c, :]), ap("GJ", s_[:, c, 1, 0:H]), AF.Abs)
            else:
                absdiff(ap("nd", s_[:, c, :]), ap("GJ", s_[:, c, 1, 0:H]), v)
            o = ap(bank_(), s_[:, 0:H])
            msum(o, (MT(M_LH), v), (MT(M_LJ), Jb), (MT(M_LA), actb))
            tr(ap("XT", s_[:, c]), o)
            cp(ap("tM", s_[:, c]), ap("XT", s_[:, c, 2::16]))
            cp(ap("hi", s_[:, c, 0]), ap("XT", s_[:, c, 0::16]))
            ts(ap("hi", s_[:, c, 1]), ap("hi", s_[:, c, 0]), 1023, ALU.bitwise_and)
            ts(ap("hh", s_[:, c]), ap("hi", s_[:, c, 1]), 2048.0, ALU.add)
            pM = bank_()
            tolist(pM, lambda h: ap("tM", s_[:, c, h::2]), 1)
            tt(ap("sc1", s_[:, c, :]), ap(pM, s_[:, 0:8]), ap("dump", s_[:, 8 * c:8 * c + 8]), ALU.min)
            act(ap("jm", s_[:, c, :]), ap(pM, s_[:, 0:8]), AF.Identity)
            scu = ap("scu", s_[:, c, :])
            ts(scu, ap("sc1", s_[:, c, :]), 2048.0, ALU.add)
            cp(ind(Dm(s + 1, 0, WT), scu), ap("nd", s_[:, c, :]))
            if c == 1 and last:
                dma("Y", ap("yd"), Dm(4), 128 * 3200)
            elif c == 1:
                pM = bank_()
                mm(ap(pM, s_[:, 0:2]), ap("B0f"), ap("col", s_[:, C_ACC:C_ACC + 2]), newg(), first=True, f=4.0)
                ts(ap("thi", s_[:, s, 0:1]), ap(pM, s_[:, 0:1]), ap(pM, s_[:, 1:2]), ALU.add, 128.0, ALU.add)
                ts(ap("thi", s_[:, s, 1:2]), ap("thi", s_[:, s, 0:1]), 3, ALU.bitwise_and)
                ts(ap("tho", s_[:, s, 0:1]), ap("thi", s_[:, s, 1:2]), col(C_4), ALU.add)
                cp(ap("ct", s_[:, s + 1]), ind(ap("ct", s_[:, 0, 0:8]), ap("tho", s_[:, s, 0:1])))
                scales(s + 1)
            ph[1] = 1
            for t, pb, z, msg, ml in ((1, pQ, "ZQ", M_SQ, M_LQ), (0, pP, "ZP", M_SP, M_LP)):
                nl, ph[1] = BL[t], 1
                nh, ns = nl // 32, 512 // nl
                for l0 in range(0, H, nl):
                    for h in range(nh):
                        bank, gq = bank_(), newg()
                        d = ap("GJ", s_[:, c, t, 16 * (8 + l0) + h:16 * (8 + nl + l0):nh])
                        if not PRE:
                            mm(ap(bank), ap("cd", s_[:, s, 0]), d, gq, first=True)
                        for i in range(ns):
                            mm(ap(bank, s_[:, i::ns]), ap("cd", s_[:, s, 1]), ap(vn, s_[:, sl, l0:l0 + nl]), gq, first=bool(PRE and not i))
                        run(len(ops) - ns - (not PRE))
                        if PRE:
                            ops[-1]["pre"] = True
                            mm(ap(bank), ap("cd", s_[:, s, 0]), d, gq)
                        x = ns * (H * h + l0)
                        for y in range(0, 512, MS[t]):
                            ts(ap("mk", s_[:, c, t, x + y:x + y + MS[t]]), ap(bank, s_[:, y:y + MS[t]]), MAGIC, ALU.add, thc(s, 1), ALU.is_equal)
                gb, ph[1] = newg(), 3
                sn = SUMN[t]
                lead = t or sn < H or not FST
                if not FST or sn < H:
                    mm(pb, MT(ml), actb, gb, first=True)
                    mm(pb, MT(msg), ap("sg", s_[:, c, H * t:H * t + H]), gb)
                    run(len(ops) - 2)
                for l0 in range(0, H, sn):
                    for h in range(nh):
                        for i in range(ns):
                            x, y = pb[2][1].start + l0, ns * (H * h + l0)
                            mm(ap(pb[1], s_[:, x:x + sn]), ZW(z, nh * i + h), ap("mk", s_[:, c, t, y + i:y + ns * sn:ns]), gb,
                               first=bool(FST and sn == H and not h and not i))
                            if i % SRUN == SRUN - 1:
                                run(len(ops) - SRUN)
                if FST and sn == H:
                    mm(pb, MT(ml), actb, gb)
                    mm(pb, MT(msg), ap("sg", s_[:, c, H * t:H * t + H]), gb)
                    run(len(ops) - 2)
                if t:
                    tt(ap("WQ", s_[:, c, :]), pQ, Q16, ALU.max)
            X, Wa, ph[1] = ap("X", s_[:, c, :]), ap("Wa", s_[:, c, :]), 2
            tt(pP, pP, NP, ALU.max)
            tt(X, pP, ap("WQ", s_[:, c, :]), ALU.min)
            mm(pX, MT(M_NI), X, newg(), first=True)
            if VABS:
                tt(Wa, pX, X, ALU.max)
            else:
                act(Wa, pX, AF.Abs)
            if last and DV[jt]:
                act(ap("yqb", s_[:, c, 0]), pX, AF.Relu)
            elif not last:
                ts(ap("SX", s_[:, so]), Wa, float(W), ALU.min)
                if EP and c:
                    cp(ind(ap("Pt"), scu), ap("SX", s_[:, so]))
                if HOP[s]:
                    send("x", 2 * mv + c, so)
            tr(ap("WTr", s_[:, c, :]), Wa)
            scan(ap("scn", s_[:, c]), ap("flag"), ap("WTr", s_[:, c, :]), ALU.add, ALU.min)
            tt(ap("fi", s_[:, c, 0]), ap("scn", s_[:, c, 15::16]), ap("hh", s_[:, c]), ALU.min)
            ts(ap("fi", s_[:, c, 1]), ap("fi", s_[:, c, 0]), 2047, ALU.bitwise_and)
            tt(ap("fM", s_[:, c, 0:8]), ap("fi", s_[:, c, 1]), ap("XT", s_[:, c, 1::16]), ALU.add)
            tt(ap("fM", s_[:, c, 8:16]), ap("fi", s_[:, c, 1]), ap("XT", s_[:, c, 1::16]), ALU.subtract)
            pM = bank_()
            tolist(pM, lambda h: ap("fM", s_[:, c, h::2]), 2)
            fz = ap("fz", s_[:, c, :])
            ts(fz, ap(pM, s_[:, 0:8]), float(W), ALU.min)
            tt(ap("JT", s_[:, so, :]), ap(pM, s_[:, 8:16]), ap("jm", s_[:, c, :]), ALU.max)
            cp(ap("SJ", s_[:, so]), ap("JT", s_[:, so, :]))
            if HOP[s]:
                send("j", 2 * mv + c, so)
            if VDF:
                tt(ap("Df", s_[:, c]), ind(Dw, fz), v, ALU.subtract)
                act(ap("SV", s_[:, so, 0:H]), ap("Df", s_[:, c]), AF.Abs)
            else:
                act(ap("Df", s_[:, c]), ind(Dw, fz), AF.Identity)
                absdiff(ap("SV", s_[:, so, 0:H]), ap("Df", s_[:, c]), v)
            if HOP[s]:
                send("v", 2 * mv + c, so)
            ph[1] = 4
            g1, g3 = newg(), newg()
            if DV[jt]:
                mm(p3, MT(M_C3), ap("thr"), g3, first=True)
                mm(p3, MT(M_NI), X, g3)
                run(len(ops) - 2)
            else:
                mm(aQ, MT(M_C), ap("thr"), g1, first=True)
            for k in range(2):
                bank = bank_()
                for i in range(4):
                    mm(ap(bank, s_[:, H * i:H * i + H]), RS(4 * k + i + 1), X, newg(), first=True)
                run(len(ops) - 4)
                o = ap("sig", s_[:, c, 512 * k:512 * k + 512])
                if DV[jt]:
                    ts(o, ap(bank), 0.0, ALU.is_equal, -8192.0, ALU.mult)
                else:
                    act(o, ap(bank), AF.Sigmoid, bias=-4.125, scale=128.0)
                for i in range(4):
                    x = 512 * k + H * i
                    mm(p3 if DV[jt] else aQ, RS(15 - 4 * k - i), ap("sig", s_[:, c, x:x + H]), g3 if DV[jt] else g1)
                run(len(ops) - 4)
            if not DV[jt]:
                act(ap("rr", s_[:, c, :]), aQ, AF.Identity)
                tt(ap("fr", s_[:, c, :]), aQ, ap("rr", s_[:, c, :]), ALU.is_le)
                msum(p3, (MT(M_NI), X), (MT(M_R), ap("fr", s_[:, c, :])))
            if last:
                if DV[jt]:
                    tt(p3, p3, X, ALU.min)
                    tt(ap("yqb", s_[:, c, 1]), p3, ap("yqb", s_[:, c, 0]), ALU.max)
                else:
                    tt(ap("yqb", s_[:, c, 0]), p3, Wa, ALU.min)
                    ts(ap("yqb", s_[:, c, 1]), ap("yqb", s_[:, c, 0]), 0.0, ALU.max)
                dma("Y", ap("yq", s_[:, H * c:H * c + H]), ap("yqb", s_[:, c, 1]), 65536)
                act(ap("yjb", s_[:, c, :]), ind(ap("IOT"), ap("SJ", s_[:, so])), AF.Identity)
                dma("Y", ap("yv", s_[:, H * c:H * c + H]), ap("SV", s_[:, so, 0:H]), 32768)
                dma("Y", ap("yj", s_[:, H * c:H * c + H]), ap("yjb", s_[0:128:16, c, :]), 4096)
            else:
                U = ap("U", s_[:, c, :])
                if DV[jt]:
                    tt(ap("Ut", s_[:, c, :]), p3, X, ALU.min)
                    tt(U, pX, ap("Ut", s_[:, c, :]), ALU.max)
                else:
                    tt(U, p3, Wa, ALU.min)
                ts(ap("SQ", s_[:, so]), U, 0.0, ALU.max)
                late.append(lambda U=U, scu=scu: cp(ind(ap("Pt"), scu), U))
            if HOP[s]:
                send("u", 2 * mv + c, so)
                nsrc.append(("L", 2 * mv + c))
            else:
                nsrc.append(("S", so))
        if not EP:
            for f in late:
                f()
            del late[:]
        mv += 1 if HOP[s] else 0
        src = nsrc
    return ops


def depend(ops):
    deps = [set() for _ in ops]
    hist, firsts, sends, sess = {}, {}, {}, {}
    for k, o in enumerate(ops):
        acc = [(x, True) for x in o["wr"]] + [(x, False) for x in o["rd"]]
        for (nm, lo, hi, _, _), w in acc:
            ps = is_ps(nm)
            for (j, lo2, hi2, w2) in hist.get(nm, ()):
                p = ops[j]
                if ps:
                    if p["eng"] != o["eng"] or o["grp"] != p["grp"] or o["grp"] is None and (w or w2):
                        deps[k].add(j)
                elif (w or w2) and (lo < hi2 and lo2 < hi or (p["extra"] or o["extra"])
                                    and lo // 16 <= (hi2 - 1) // 16 and lo2 // 16 <= (hi - 1) // 16):
                    deps[k].add(j)
        if o["grp"] is not None:
            if o["first"]:
                firsts[o["grp"]] = k
            else:
                deps[k].add(firsts[o["grp"]])
        if o["meth"] == "send":
            sends[o["extra"][1]] = k
        if o["meth"] == "arrive":
            deps[k].add(sends[o["extra"][1]])
        for (nm, lo, hi, _, _), w in acc:
            hist.setdefault(nm, []).append((k, lo, hi, w))
        deps[k].discard(k)
        if o["bank"]:
            sess.setdefault(o["bank"], []).append(k)
    for lst in sess.values():
        inside = set(lst)
        for k in lst[1:]:
            for j in deps[k] - inside:
                if j < lst[0]:
                    deps[lst[0]] |= deps[j] if ops[lst[0]].get("pre") and ops[j]["eng"] == "S" else {j}
            deps[k].add(lst[0])
    anc = []
    for k, d in enumerate(deps):
        m = 0
        for j in d:
            m |= anc[j]
        deps[k] = {j for j in d if not m >> j & 1 or ops[j]["extra"]}
        for j in d:
            m |= 1 << j
        anc.append(0 if ops[k]["meth"] in ("arrive", "send") else m)
    return deps, sess


def latency(o):
    return o["extra"][2] if o["meth"] == "dma_start" else COMM + o["extra"][2] if o["meth"] == "arrive" else o["cost"]


def graph(ops, deps, sess):
    n = len(ops)
    eng = [o["eng"] for o in ops]
    succ = [[] for _ in range(n)]
    for k in range(n):
        for j in deps[k]:
            succ[j].append((k, (0.0 if eng[k] == "T" else SAME) if eng[j] == eng[k] else SYNC))
    return dict(n=n, eng=eng, succ=succ, lat=[latency(o) for o in ops], busy=[o["cost"] if o["eng"] != "X" else 0.0 for o in ops],
                nd=[len(d) for d in deps], bank=[o["bank"] for o in ops], sess=sess,
                opens=[(KEEP if o.get("pre") else 1) if o["bank"] and sess[o["bank"]][0] == k else 0 for k, o in enumerate(ops)],
                slack=[SL2 if o["cls"] in (2, 4) else SLACK for o in ops],
                pred=[[(j, (0.0 if eng[k] == "T" else SAME) if eng[j] == eng[k] else SYNC) for j in deps[k]] for k in range(n)])


def schedule(gr, key, slack=None):
    n, eng, succ, lat, busy, bank, sess, opens = (gr[x] for x in "n eng succ lat busy bank sess opens".split())
    slack = slack or gr["slack"]
    left, rdy, before, lastk = list(gr["nd"]), [0.0] * n, [None] * n, {}
    ready_t, done_t = [0.0] * n, [0.0] * n
    free = {e: 0.0 for e in ENG + ("X",)}
    ready = {e: [k for k in range(n) if not left[k] and eng[k] == e] for e in free}
    fbank = [(0.0, b) for b in POOL]
    held, heldt, banks, prev, lastof = {}, {}, {}, {}, {}
    order, start, cand = [], [0.0] * n, {}
    dirty = set(free)
    while len(order) < n:
        fb = min(fbank) if fbank else None
        for e in dirty:
            lst = [(max(ready_t[k], fb[0] + SYNC) if opens[k] else ready_t[k], k) for k in ready[e] if len(fbank) >= opens[k]]
            if lst:
                t0 = max(free[e], min(lst)[0])
                _, k, r = max((key[k], k, r) for r, k in lst if r <= t0 + slack[k])
                if r > t0 + 30.0:
                    fill = [(key[m], m, x) for x, m in lst if max(x, t0) + busy[m] <= r + FILL]
                    if fill:
                        _, k, r = max(fill)
                cand[e] = (max(free[e], r), e, k, r)
            else:
                cand.pop(e, None)
        t, e, k, rdy[k] = min(cand.values())
        before[k], lastk[e] = lastk.get(e), k
        dirty = {e}
        ready[e].remove(k)
        order.append(k)
        free[e] = t + busy[k]
        d = done_t[k] = t + lat[k]
        start[k] = t
        b = bank[k]
        if b:
            if opens[k]:
                fbank.remove(fb)
                banks[b], held[b], heldt[b] = fb[1], len(sess[b]), 0.0
                prev[k] = lastof.get(fb[1], ())
                lastof[fb[1]] = sess[b]
            held[b] -= 1
            heldt[b] = max(heldt[b], d)
            if not held[b]:
                fbank.append((heldt[b], banks[b]))
                dirty.add("T")
        for m, gp in succ[k]:
            if d + gp > ready_t[m]:
                ready_t[m] = d + gp
            left[m] -= 1
            if not left[m]:
                ready[eng[m]].append(m)
                dirty.add(eng[m])
    return max(done_t), order, prev, banks, start, key, slack, rdy, before


def backward(gr, start):
    n, eng, pred, lat, busy = (gr[x] for x in "n eng pred lat busy".split())
    left = [len(x) for x in gr["succ"]]
    end = [start[k] + lat[k] for k in range(n)]
    free = {e: 0.0 for e in ENG + ("X",)}
    ready = {e: [k for k in range(n) if not left[k] and eng[k] == e] for e in free}
    rt, out, cand = [0.0] * n, [0.0] * n, {}
    dirty = set(free)
    for _ in range(n):
        for e in dirty:
            lst = ready[e]
            if lst:
                t0 = max(free[e], min(rt[k] for k in lst))
                _, k = max((end[k], k) for k in lst if rt[k] <= t0 + SLACK)
                cand[e] = (max(free[e], rt[k]), e, k)
            else:
                cand.pop(e, None)
        t, e, k = min(cand.values())
        dirty = {e}
        ready[e].remove(k)
        free[e] = out[k] = t + busy[k]
        for j, gp in pred[k]:
            rt[j] = max(rt[j], out[k] + lat[j] - busy[j] + gp)
            left[j] -= 1
            if not left[j]:
                ready[eng[j]].append(j)
                dirty.add(eng[j])
    return out


def variant(ops, gr, f, g, sc, sync, comm, rate, ov=TOV):
    busy, lat = [], []
    for o, b in zip(ops, gr["busy"]):
        i = [k for k, a in enumerate(o["args"]) if is_ap(a) and a[0] == "ind"]
        if i:
            b = 70 + (b - 70) * (g / G_ if i[0] else sc / SC_)
        if o["eng"] == "T":
            b += (ov - TOV) * len(o.get("sub", [o]))
        busy.append(b * (f if o["eng"] in "VSTG" else 1.0))
        lat.append(2200 + (o["extra"][2] - 2200) * RATE / rate if o["meth"] == "dma_start" else comm + o["extra"][2] if o["meth"] == "arrive" else busy[-1])
    return busy, lat, [[(j, sync if x else 0.0) for j, x in p] for p in gr["pred"]], sync


def replay(gr, r, var):
    busy, lat, pred, sync = var
    done, free, eng, prev = [0.0] * gr["n"], dict.fromkeys(ENG + ("X",), 0.0), gr["eng"], r[2]
    for k in r[1]:
        t = free[eng[k]]
        for j, g in pred[k]:
            if done[j] + g > t:
                t = done[j] + g
        if k in prev:
            for j in prev[k]:
                if done[j] + sync > t:
                    t = done[j] + sync
        free[eng[k]] = t + busy[k]
        done[k] = t + lat[k]
    return max(done)


def search(ops, gr):
    n = gr["n"]
    var = [(variant(ops, gr, *v[1:]), v[0] / v[1]) for v in VARS]
    tot = 1.0 + sum(v[0] for v in VARS)

    def score(r, lim):
        return (r[0] + sum(w * replay(gr, r, v) for v, w in var)) / tot if r[0] < lim else 1e9
    pr = [0.0] * n
    for k in range(n - 1, -1, -1):
        pr[k] = gr["lat"][k] + max([pr[m] + g for m, g in gr["succ"][k] if ops[m]["ph"] == ops[k]["ph"]] + [0.0])
    best = None
    for w0, w2 in ((1.5, 2.5), (0.5, 2.5), (0.9, 0.9), (0.0, 0.0)):
        r = schedule(gr, [0.3 * pr[k] + PH * ((w0, 0.0, w2, 0.0, w2)[o["cls"]] - o["ph"]) - k * 1e-3 for k, o in enumerate(ops)])
        for x in range(ROUNDS + 1):
            if best is None or r[0] < best[0]:
                best = r
            r = schedule(gr, backward(gr, r[4]))
    rng, cur = np.random.default_rng(SEED), best
    xc = xb = score(best, 1e9)
    cl = [o["eng"] + (o["wr"][0][0] if o["wr"] and not o["bank"] else "") + str(o["ph"]) for o in ops]
    c2 = ["%d.%d" % (o["ph"], o["cls"]) for o in ops]
    names, name2 = sorted(set(cl)), sorted(set(c2))
    for i in range(MORE):
        off = {names[int(x)]: float(rng.normal() * SIG) for x in rng.integers(0, len(names), NM)}
        if rng.random() < P2:
            off[name2[int(rng.integers(0, len(name2)))]] = float(rng.normal() * SIG)
        if rng.random() < PC:
            p, x = int(rng.integers(0, 8)), float(rng.uniform(1000, 7000))
            off.update({"%d.%d" % (p + a, b): x for a, b in ((0, 2), (0, 3), (1, 0)) if rng.random() < 0.8})
        if rng.random() < PB:
            t0, base = rng.random() * cur[0] * (rng.random() < PW_), backward(gr, cur[4])
            base = [b - cur[0] if t > t0 else -t for b, t in zip(base, cur[4])]
        else:
            base = [-x for x in cur[4]]
        r = schedule(gr, [x + off.get(c, 0.0) + off.get(d, 0.0) for x, c, d in zip(base, cl, c2)])
        x = score(r, cur[0] + 1500)
        if x < xc + TM_ * (1.0 - COOL * i / MORE):
            cur, xc = r, x
        if x < xb:
            best, xb = r, x
    cur, slack = best, best[6]
    for i in range(FINE):
        key, sl = list(cur[5]), list(cur[6])
        late = chain(gr, cur)
        for _ in range(int(rng.integers(1, 3)) if late else 0):
            k, p, rdy = late[int(rng.integers(0, len(late)))]
            up, x = [k], rng.random()
            if x < 0.4:
                sl[k] = max(sl[k], rdy - cur[4][p] + 1.0)
            elif x < 0.7:
                for j in up:
                    up += [m for m, _ in gr["pred"][j] if m not in up and cur[4][m] > cur[4][k] - 2500.0]
            d = max(key[p] - key[k], 0.0) + 1.0 + (600.0 * rng.random() if x > 0.4 else 0.0)
            if x < 0.85:
                for j in up:
                    key[j] += d
            else:
                key[p] -= d
                sl[p] = SLACK
        r = schedule(gr, key, sl)
        if r[0] < cur[0] + TEMP * (1.0 - i / FINE) * rng.random():
            cur = r
        if r[0] < best[0]:
            best = r
    return best


def chain(gr, r):
    start, ready, before, out = r[4], r[7], r[8], []
    k = max(range(gr["n"]), key=lambda j: start[j] + gr["lat"][j])
    while True:
        p = before[k]
        if p is not None and start[k] > ready[k] + 1e-6:
            out.append((k, p, ready[k]))
            k = p
            continue
        c = [(start[j] + gr["lat"][j] + g, j) for j, g in gr["pred"][k]] + [(start[j] + gr["lat"][j] + SYNC, j) for j in r[2].get(k, ())]
        if not c:
            return out
        k = max(c)[1]


def program():
    ops = build()
    deps, sess = depend(ops)
    total, order, prev, banks, start = search(ops, graph(ops, deps, sess))[:5]
    for k, x in prev.items():
        deps[k] |= set(x)
    order = list(range(NLOAD)) + [k for k in order if k >= NLOAD and ops[k]["eng"] != "X"]
    pos = {k: i for i, k in enumerate(order)}
    pos.update({k: 0 for k, o in enumerate(ops) if o["eng"] == "X"})
    lastg = {x["grp"]: (k, i) for k in order for i, x in enumerate(ops[k].get("sub", [ops[k]]))}
    seen = {e: {} for e in ENG}
    marks, waits = set(), {}
    for k in order:
        e, m = ops[k]["eng"], {}
        for j in deps[k]:
            b = ops[j]
            if b["meth"] == "send" or e == "T" and b["eng"] == "T":
                continue
            key = b["extra"][:2] if b["extra"] else b["eng"]
            if key not in m or pos[j] > pos[m[key]]:
                m[key] = j
        waits[k] = []
        for key, j in m.items():
            if seen[e].get(key, -1) < pos[j]:
                seen[e][key] = pos[j]
                waits[k].append((key, j)); marks.add(j)
    cnt, val, out = {e: 0 for e in ENG}, {}, []
    for k in order:
        o = ops[k]
        o["t"] = start[k]
        if k in marks and not o["extra"]:
            cnt[o["eng"]] += 1
            val[k] = cnt[o["eng"]]
        w = [("e" + key, val[j]) if key in ENG else ("dm%d" % key[1], 16) if key[0] == "dma" else ("arr" + key[1], None)
             for key, j in waits[k]]
        sub = o.get("sub", [o])
        for i, x in enumerate(sub):
            tail = [x["first"], lastg[x["grp"]] == (k, i)] if o["meth"] == "matmul" else []
            out.append((x, [] if i else w, tail, k in val and i == len(sub) - 1))
    return out, banks, total, ops


_prog = []


def res(T, banks, a):
    if not is_ap(a):
        return a
    if a[0] == "ind":
        return res(T, banks, a[1]).indirect(res(T, banks, a[2]))
    return T[banks.get(a[1], a[1])][a[2] if len(a[2]) > 1 else a[2][0]]


def share(topo, a, b, k, n):
    e = topo.engines(a, b)
    h = len(e) // n
    return sum(1 << x for x in e[h * k:h * k + h]), h


def relays_of(T, topo, core):
    r = T.rank_of(core)
    dsts = [T.cores[(r + h) % len(T.cores)] for h in HOP if h]
    c = [x for x in topo.cores_of(core) if T.rank_of(x) is None and all(topo.may_write(x, d) for d in dsts)]
    c.sort(key=lambda x: topo.die(x) != topo.die(core))
    return c[:2]


def call(e, m, args, kw):
    if m == "matmul": return e.matmul(*args)
    if m == "activation": return e.activation(*args, **kw)
    if m == "tensor_copy": return e.tensor_copy(*args)
    if m == "tensor_tensor": return e.tensor_tensor(*args)
    if m == "tensor_scalar": return e.tensor_scalar(*args)
    if m == "tensor_reduce": return e.tensor_reduce(*args)
    if m == "tensor_tensor_scan": return e.tensor_tensor_scan(*args)
    if m == "transpose": return e.transpose(*args)
    if m == "reciprocal": return e.reciprocal(*args)
    if m == "memset": return e.memset(*args)
    if m == "affine_select": return e.affine_select(*args)
    if m == "iota": return e.iota(*args, **kw)
    return e.dma_start(*args)


def rank_program(g, core, T, topo):
    rank = T.rank_of(core)
    n = len(T.cores)
    hops = [h for h in HOP if h]
    if rank is None:
        for r, c in enumerate(T.cores):
            rl = relays_of(T, topo, c)
            if core in rl:
                tot = 0
                for m in MSGS:
                    parts, slot = PARTS[m[0]], int(m[1])
                    to = T.cores[(r + hops[slot // 2]) % n]
                    rid, pid = topo.addr(to, core)
                    for k, (_, land, by, w) in enumerate(parts):
                        if rl[by] == core:
                            g.wait_ge(T.sem["rel" + m], share(topo, c, core, k, len(parts))[1])
                            g.remote_dma(T[land][:, slot, w], T[land][:, slot, w], T.sem["arr" + m], T.sem.fwd, pid, rid,
                                         topo.mask(core, to))
                            tot += len(topo.engines(core, to))
                g.wait_ge(T.sem.fwd, tot)
        return
    if not _prog:
        _prog.append(program())
    calls, banks = _prog[0][:2]
    q = {"V": g.vector, "S": g.scalar, "T": g.tensor, "G": g, "Y": g.sync}
    rl = relays_of(T, topo, core)
    sent, dmas = 0, []
    for o, waits, tail, inc in calls:
        e, m = q[o["eng"]], o["meth"]
        for nm, val in waits:
            if val is None:
                frm = relays_of(T, topo, T.cores[(rank - hops[int(nm[4]) // 2]) % n])
                val = sum(len(topo.engines(frm[p[2]], core)) for p in PARTS[nm[3]])
            e.wait_ge(T.sem[nm], val)
        if m == "send":
            _, msg, so = o["extra"]
            parts, tr = PARTS[msg[0]], []
            for k, (a, b, by, w) in enumerate(parts):
                rid, pid = topo.addr(rl[by], core)
                mask, h = share(topo, core, rl[by], k, len(parts))
                tr.append(RemoteDMATransfer(dst_ids=[DstId(rid=rid, pnc=pid)], dma_engine_mask=mask, remote_sem=T.sem["rel" + msg],
                                            src=T[a][:, so, w], dst=T[b][:, int(msg[1]), w]))
                sent += h
            g.remote_dma_fused(tr, local_sem=T.sem.sent)
            continue
        ins = call(e, m, [res(T, banks, a) for a in o["args"]] + tail, {k: res(T, banks, a) for k, a in o["kw"].items()})
        if m == "dma_start":
            ins.then_inc(T.sem["dm%d" % o["extra"][1]], 16); dmas.append(o["extra"][1])
        elif inc:
            ins.then_inc(T.sem["e" + o["eng"]], 1)
    for d in dmas:
        g.sync.wait_ge(T.sem["dm%d" % d], 16)
    g.wait_ge(T.sem.sent, sent)
